import numpy as np
import ml_dtypes


def mxq(x, axis, fmt="e4m3"):
    dtype, down = {"e4m3": (ml_dtypes.float8_e4m3fn, 7), "e5m2": (ml_dtypes.float8_e5m2, 14)}[fmt]
    v = np.moveaxis(np.asarray(x, np.float32).astype(ml_dtypes.bfloat16).astype(np.float64), axis, -1)
    blocks = v.reshape(v.shape[:-1] + (-1, 32))
    amax = np.abs(blocks).max(-1, keepdims=True)
    byte = np.maximum(np.where(amax > 0, np.frexp(amax)[1] - 1 + 127, 0) - down, 1)
    scale = np.exp2(byte - 127.0)
    codes = (blocks / scale).astype(np.float32).astype(dtype).astype(np.float64)
    return np.moveaxis((codes * scale).reshape(v.shape), -1, axis)


WIDE = False


def mx_kscale(k):
    if not WIDE:
        return np.ones(k)
    levels = np.array([18, -18])
    if k % 512:
        return np.exp2(np.random.permutation(np.resize(levels, k // 32))).repeat(32)
    a = np.empty((k // 512, 16))
    for p in range(k // 512):
        a[p, :8] = np.random.permutation(np.resize(levels, 8))
        for g in range(8):
            far = levels[np.abs(levels - a[p, g]) >= 10]
            a[p, g + 8] = far[np.random.randint(len(far))]
    return np.exp2(a.ravel()).repeat(32)


def f64(x):
    return np.asarray(x).astype(np.float64)


def striped(idx):
    return np.tile(np.asarray(idx).reshape(-1, 16).T, (8, 1)).astype(np.uint16)


def unstriped(offs):
    return offs[:16].T.reshape(-1).astype(np.int64)


B, N, T, D, R = 2, 512, 2048, 512, 512
LR = 0.1
BETA = 0.9


def setup_inputs():
    n = np.random.standard_normal
    idx = np.random.permutation(T)[:B * N]
    s = mx_kscale(D)[:, None]
    z = mx_kscale(R)[:, None]
    x = n((B, D, R))
    return {
        "xT": (x * s).astype(np.float32),
        "wT": (n((D, T)) * (1.00 / np.sqrt(D)) / s).astype(np.float32),
        "y": (2 * np.random.randint(0, 2, (B, R, N)) - 1).astype(np.float32),
        "wt": (np.random.uniform(0.5, 1.5, (B, R, 1)) * 1.0 / np.sqrt(R) * z).astype(np.float32),
        "xm": (x.transpose(0, 2, 1) / z / s[:, 0]).astype(np.float32),
        "mT": (0.3 * n((D, T)) / s).astype(np.float32),
        "offs": striped(idx),
    }


def reference(xT, wT, y, wt, xm, mT, offs):
    idx = unstriped(offs)
    pick = lambda x: x[:, idx].reshape(x.shape[0], B, N).transpose(1, 0, 2)
    w = pick(f64(wT))
    a = mxq(f64(xT), 1, "e4m3").transpose(0, 2, 1) @ mxq(w, 1, "e4m3")
    g = -f64(wt) * f64(y) / (1.0 + np.exp(f64(y) * a))
    dw = mxq(f64(xm), 1, "e4m3").transpose(0, 2, 1) @ mxq(g, 1, "e5m2")
    nm = BETA * pick(f64(mT)) + dw
    nw = w - LR * nm
    tables = []
    for old, new in ((wT, nw), (mT, nm),):
        table = f64(old)
        table[:, idx] = new.transpose(1, 0, 2).reshape(D, B * N)
        tables.append(table)
    return tuple(tables)

@@ -1,0 +1,166 @@
+from contextlib import ExitStack
+
+import concourse.mybir as mybir
+
+B, N, T, D, R = 2, 512, 2048, 512, 512
+LR = 0.1
+BETA = 0.9
+FLOPS = 2 * 2 * B * N * D * R
+
+F32 = mybir.dt.float32
+BF16 = mybir.dt.bfloat16
+U32 = mybir.dt.uint32
+U16 = mybir.dt.uint16
+U8 = mybir.dt.uint8
+E4M3 = mybir.dt.float8_e4m3fn_x4
+E5M2 = mybir.dt.float8_e5m2_x4
+MULT = mybir.AluOpType.mult
+ADD = mybir.AluOpType.add
+COPY = mybir.ActivationFunctionType.Copy
+SIGMOID = mybir.ActivationFunctionType.Sigmoid
+
+P = 128
+PACK = 4
+LIST_COLS = N // 16
+
+
+def tile_attend_gsig_mom_kernel(tc, xT, wT, y, wt, xm, mT, offs, out_0, out_1):
+    nc = tc.nc
+
+    def planes(table):
+        return table.rearrange("(p t) c -> t p c", t=PACK)
+
+    def rows4(matrix):
+        return matrix.rearrange("(p j) c -> p j c", j=PACK)
+
+    with ExitStack() as ctx:
+        keep = ctx.enter_context(tc.tile_pool(name="keep", bufs=1))
+        ring = ctx.enter_context(tc.tile_pool(name="ring", bufs=4))
+        psum = ctx.enter_context(tc.psum_pool(name="psum", bufs=1))
+
+        offsets = keep.tile([P, B * LIST_COLS], U16, name="offsets")
+        nc.sync.dma_start(offsets[:], offs)
+
+        def listed(window, b):
+            return window[:].indirect(offsets[:, b * LIST_COLS : (b + 1) * LIST_COLS])
+
+        def load(pool, tag, source, shape):
+            dest = pool.tile(shape, F32, name=tag, tag=tag)
+            nc.sync.dma_start(dest[:], source)
+            return dest
+
+        w_src = [load(ring, "early", planes(wT)[t], [P, T]) for t in range(PACK)]
+        x_raw = [load(keep, "x0", rows4(xT[0]), [P, PACK, R])]
+        m_src = [load(keep, "m_src0", planes(mT)[0], [P, T])]
+        y_raw = [load(keep, "y0", rows4(y[0]), [P, PACK, N])]
+        wt_raw = load(keep, "wt", wt.rearrange("b (p j) o -> p b (j o)", j=PACK), [P, B, PACK])
+        xm_raw = [load(keep, "xm0", rows4(xm[0]), [P, PACK, D])]
+        for t in range(1, PACK):
+            m_src.append(load(keep, "m_src%d" % t, planes(mT)[t], [P, T]))
+
+        w_got = [keep.tile([P, PACK, N], F32, name="w_got%d" % b) for b in range(B)]
+        m_got = [keep.tile([P, PACK, N], F32, name="m_got%d" % b) for b in range(B)]
+        w_out = [keep.tile([P, T], F32, name="w_out%d" % t) for t in range(PACK)]
+        neg_wt = keep.tile([P, B, PACK], F32, name="neg_wt")
+
+        warm = keep.tile([P, 8], F32, name="warm")
+        nc.vector.memset(warm[:], 0.0)
+        nc.scalar.activation(warm[:], warm[:], SIGMOID)
+
+        def gather(got, src, b, t):
+            nc.vector.tensor_copy(got[b][:, t, :], listed(src[t], b))
+
+        def rounded():
+            return ring.tile([P, PACK * 512], BF16, name="rounded", tag="rounded", align_bytes=64)
+
+        def moving_views(dest, *sources):
+            return [dest[:].rearrange("p (c i j) -> p c j i", i=4, j=PACK)] + [
+                s[:].rearrange("p j (c i) -> p c j i", i=4) for s in sources
+            ]
+
+        def round_stationary(raw):
+            dest = rounded()
+            nc.scalar.activation(
+                dest[:].rearrange("p (t m j) -> p m j t", t=PACK, j=PACK),
+                raw[:].rearrange("p j (m t) -> p m j t", t=PACK),
+                COPY,
+            )
+            return dest
+
+        def quantize(source, tag, fmt):
+            codes = keep.tile([P, 512], U32, name=tag + "_codes", tag=tag + "_codes", align_bytes=64)
+            scales = keep.tile([P, 512], U8, name=tag + "_scales", tag=tag + "_scales", align_bytes=64)
+            nc.vector.quantize_mx(out=codes[:].bitcast(fmt), scales=scales[:], in_=source[:])
+            return codes, scales, fmt
+
+        def product(tag, stationary, moving):
+            banks = []
+            for t in range(PACK):
+                bank = psum.tile([P, 512], F32, name=tag + str(t), tag=tag + str(t))
+                cols = slice(t * P, (t + 1) * P)
+                nc.tensor.matmul_mx(
+                    out=bank[:],
+                    lhsT=stationary[0][:, cols].bitcast(stationary[2]),
+                    lhsT_scale=stationary[1][:, cols],
+                    rhs=moving[0][:].bitcast(moving[2]),
+                    rhs_scale=moving[1][:],
+                    start=True,
+                    stop=True,
+                )
+                banks.append(bank)
+            return banks
+
+        def step(b, w_rounded, x_rounded):
+            w_q = quantize(w_rounded, "w", E4M3)
+            x_q = quantize(x_rounded, "x", E4M3)
+            scores = product("a", x_q, w_q)
+            margin = keep.tile([P, PACK, N], F32, name="margin", tag="margin")
+            weight = keep.tile([P, PACK, N], F32, name="weight", tag="x0")
+            for t in range(PACK):
+                nc.vector.tensor_tensor(margin[:, t, :], scores[t][:], y_raw[b][:, t, :], MULT)
+                nc.scalar.activation(weight[:, t, :], y_raw[b][:, t, :], COPY, scale=neg_wt[:, b, t : t + 1])
+                nc.scalar.activation(margin[:, t, :], margin[:, t, :], SIGMOID, scale=-1.0)
+            xm_rounded = round_stationary(xm_raw[b])
+            g_rounded = rounded()
+            g_view, s_view, weight_view = moving_views(g_rounded, margin, weight)
+            nc.vector.tensor_tensor(g_view, s_view, weight_view, MULT)
+            xm_q = quantize(xm_rounded, "xm", E4M3)
+            g_q = quantize(g_rounded, "g", E5M2)
+            grads = product("dw", xm_q, g_q)
+            for t in range(PACK):
+                gather(m_got, m_src, b, t)
+            for t in range(PACK):
+                nc.vector.scalar_tensor_tensor(m_got[b][:, t, :], m_got[b][:, t, :], BETA, grads[t][:], MULT, ADD)
+            for t in range(PACK):
+                nc.vector.scalar_tensor_tensor(w_got[b][:, t, :], m_got[b][:, t, :], -LR, w_got[b][:, t, :], MULT, ADD)
+
+        for t in range(PACK):
+            gather(w_got, w_src, 0, t)
+            nc.scalar.activation(w_out[t][:], w_src[t][:], COPY)
+            if t < PACK - 1:
+                gather(w_got, w_src, 1, t)
+        nc.scalar.activation(neg_wt[:], wt_raw[:], COPY, scale=-1.0)
+        w_rounded = rounded()
+        nc.vector.tensor_copy(*moving_views(w_rounded, w_got[0]))
+        gather(w_got, w_src, 1, PACK - 1)
+        step(0, w_rounded, round_stationary(x_raw[0]))
+
+        x_raw.append(load(ring, "early", rows4(xT[1]), [P, PACK, R]))
+        y_raw.append(load(ring, "early", rows4(y[1]), [P, PACK, N]))
+        xm_raw.append(load(ring, "early", rows4(xm[1]), [P, PACK, D]))
+        m_out = [load(keep, "m_out%d" % t, planes(mT)[t], [P, T]) for t in range(PACK)]
+
+        w_rounded = rounded()
+        w_view, got_view = moving_views(w_rounded, w_got[1])
+        nc.scalar.activation(w_view, got_view, COPY)
+        step(1, w_rounded, round_stationary(x_raw[1]))
+
+        for t in range(PACK):
+            nc.vector.tensor_copy(listed(w_out[t], 0), w_got[0][:, t, :])
+        for t in range(PACK):
+            nc.vector.tensor_copy(listed(m_out[t], 0), m_got[0][:, t, :])
+        for t in range(PACK):
+            nc.vector.tensor_copy(listed(m_out[t], 1), m_got[1][:, t, :])
+            nc.sync.dma_start(planes(out_1)[t], m_out[t][:])
+            nc.vector.tensor_copy(listed(w_out[t], 1), w_got[1][:, t, :])
+            nc.sync.dma_start(planes(out_0)[t], w_out[t][:])

@@ -22,6 +22,19 @@ SIGMOID = mybir.ActivationFunctionType.Sigmoid
 P = 128
 PACK = 4
 LIST_COLS = N // 16
+LOADS = 'w0 w1 w2 w3 wt0 m0 x0 m2 y0 m1 m3 mo1 xm0 x1 wo3 wo1 mo2 wo2 wt1 y1 xm1 mo0 mo3 wo0'
+STEPS = 'gm0 rw0 gm1 a0 wgt0 rw1 xm0 u0 g0 dw0 a1 nm0 xm1 nw0 sm0 wgt1 u1 g1 dw1 sw0 nm1 sm1 nw1 sw1'
+RW_ON_VECTOR = (0,)
+WEIGHT_ON_GPSIMD = (0,)
+U_ON_VECTOR = ((0, 0), (0, 3))
+G_ON_VECTOR = (0,)
+M_ON_VECTOR = ((0, 0), (0, 1), (0, 2))
+W_ON_VECTOR = ()
+WO_ON_SCALAR = (1, 3)
+GQ_AFTER_XM = (0,)
+BETA_LATE = (1,)
+BETA_ON_GPSIMD = (0,)
+RTAG = {'w0': 5, 'g0': 5, 'x0': 1, 'xm0': 3, 'w1': 2, 'g1': 4, 'x1': 2, 'xm1': 0}
 
 
 def tile_attend_gsig_mom_kernel(tc, xT, wT, y, wt, xm, mT, offs, out_0, out_1):
@@ -34,52 +47,65 @@ def tile_attend_gsig_mom_kernel(tc, xT, wT, y, wt, xm, mT, offs, out_0, out_1):
         return matrix.rearrange("(p j) c -> p j c", j=PACK)
 
     with ExitStack() as ctx:
-        keep = ctx.enter_context(tc.tile_pool(name="keep", bufs=1))
-        ring = ctx.enter_context(tc.tile_pool(name="ring", bufs=4))
+        sbuf = ctx.enter_context(tc.tile_pool(name="sbuf", bufs=1))
         psum = ctx.enter_context(tc.psum_pool(name="psum", bufs=1))
 
-        offsets = keep.tile([P, B * LIST_COLS], U16, name="offsets")
+        offsets = sbuf.tile([P, B * LIST_COLS], U16, name="offsets")
         nc.sync.dma_start(offsets[:], offs)
 
         def listed(window, b):
             return window[:].indirect(offsets[:, b * LIST_COLS : (b + 1) * LIST_COLS])
 
-        def load(pool, tag, source, shape):
-            dest = pool.tile(shape, F32, name=tag, tag=tag)
+        def load(tag, source, shape):
+            dest = sbuf.tile(shape, F32, name=tag, tag=tag)
             nc.sync.dma_start(dest[:], source)
             return dest
 
-        w_src = [load(ring, "early", planes(wT)[t], [P, T]) for t in range(PACK)]
-        x_raw = [load(keep, "x0", rows4(xT[0]), [P, PACK, R])]
-        m_src = [load(keep, "m_src0", planes(mT)[0], [P, T])]
-        y_raw = [load(keep, "y0", rows4(y[0]), [P, PACK, N])]
-        wt_raw = load(keep, "wt", wt.rearrange("b (p j) o -> p b (j o)", j=PACK), [P, B, PACK])
-        xm_raw = [load(keep, "xm0", rows4(xm[0]), [P, PACK, D])]
-        for t in range(1, PACK):
-            m_src.append(load(keep, "m_src%d" % t, planes(mT)[t], [P, T]))
+        w_got = [sbuf.tile([P, PACK, N], F32, name="w_got%d" % b) for b in range(B)]
+        m_got = [sbuf.tile([P, PACK, N], F32, name="m_got%d" % b) for b in range(B)]
 
-        w_got = [keep.tile([P, PACK, N], F32, name="w_got%d" % b) for b in range(B)]
-        m_got = [keep.tile([P, PACK, N], F32, name="m_got%d" % b) for b in range(B)]
-        w_out = [keep.tile([P, T], F32, name="w_out%d" % t) for t in range(PACK)]
-        neg_wt = keep.tile([P, B, PACK], F32, name="neg_wt")
-
-        warm = keep.tile([P, 8], F32, name="warm")
+        warm = sbuf.tile([P, 8], F32, name="warm")
         nc.vector.memset(warm[:], 0.0)
         nc.scalar.activation(warm[:], warm[:], SIGMOID)
 
-        def gather(got, src, b, t):
-            nc.vector.tensor_copy(got[b][:, t, :], listed(src[t], b))
+        have = {}
+        late = dict(zip(("xm1", "y1", "x1"), ["w%d" % t for t in WO_ON_SCALAR]))
 
-        def rounded():
-            return ring.tile([P, PACK * 512], BF16, name="rounded", tag="rounded", align_bytes=64)
+        sources = {}
+        for b in range(B):
+            sources["wt%d" % b] = ("wt%d" % b, rows4(wt[b]), [P, PACK, 1])
+            sources["x%d" % b] = (late.get("x%d" % b, "x%d" % b), rows4(xT[b]), [P, PACK, R])
+            sources["y%d" % b] = (late.get("y%d" % b, "y%d" % b), rows4(y[b]), [P, PACK, N])
+            sources["xm%d" % b] = (late.get("xm%d" % b, "xm%d" % b), rows4(xm[b]), [P, PACK, D])
+        for t in range(PACK):
+            sources["w%d" % t] = ("w%d" % t, planes(wT)[t], [P, T])
+            sources["m%d" % t] = ("m%d" % t, planes(mT)[t], [P, T])
+            sources["mo%d" % t] = ("mo%d" % t, planes(mT)[t], [P, T])
+            sources["wo%d" % t] = ("w%d" % t, planes(wT)[t], [P, T])
+        for name in LOADS.split():
+            if name not in have:
+                have[name] = load(*sources[name])
+            if name == "w3":
+                for t in range(PACK):
+                    for b in range(B):
+                        nc.vector.tensor_copy(w_got[b][:, t, :], listed(have["w%d" % t], b))
+                for t in WO_ON_SCALAR:
+                    have["wo%d" % t] = sbuf.tile([P, T], F32, name="wo%d" % t)
+                    nc.scalar.activation(have["wo%d" % t][:], have["w%d" % t][:], COPY)
 
-        def moving_views(dest, *sources):
+        def rounded(tag):
+            return sbuf.tile([P, PACK * 512], BF16, name=tag, tag=tag, align_bytes=64)
+
+        def block(tag):
+            return sbuf.tile([P, PACK, N], F32, name=tag, tag=tag)
+
+        def moving_views(dest, *planar):
             return [dest[:].rearrange("p (c i j) -> p c j i", i=4, j=PACK)] + [
-                s[:].rearrange("p j (c i) -> p c j i", i=4) for s in sources
+                s[:].rearrange("p j (c i) -> p c j i", i=4) for s in planar
             ]
 
-        def round_stationary(raw):
-            dest = rounded()
+        def round_stationary(raw, name):
+            dest = rounded("r%d" % RTAG[name])
             nc.scalar.activation(
                 dest[:].rearrange("p (t m j) -> p m j t", t=PACK, j=PACK),
                 raw[:].rearrange("p j (m t) -> p m j t", t=PACK),
@@ -87,16 +113,17 @@ def tile_attend_gsig_mom_kernel(tc, xT, wT, y, wt, xm, mT, offs, out_0, out_1):
             )
             return dest
 
-        def quantize(source, tag, fmt):
-            codes = keep.tile([P, 512], U32, name=tag + "_codes", tag=tag + "_codes", align_bytes=64)
-            scales = keep.tile([P, 512], U8, name=tag + "_scales", tag=tag + "_scales", align_bytes=64)
+        def quantize(source, tag, fmt, codes_tag=None):
+            codes = sbuf.tile([P, 512], U32, name=tag + "_codes", tag=codes_tag or tag + "_codes", align_bytes=64)
+            scales = sbuf.tile([P, 512], U8, name=tag + "_scales", tag=tag + "_scales", align_bytes=64)
             nc.vector.quantize_mx(out=codes[:].bitcast(fmt), scales=scales[:], in_=source[:])
             return codes, scales, fmt
 
-        def product(tag, stationary, moving):
+        def product(b, stationary, moving):
             banks = []
             for t in range(PACK):
-                bank = psum.tile([P, 512], F32, name=tag + str(t), tag=tag + str(t))
+                tag = "bank%d%d" % (b, t)
+                bank = psum.tile([P, 512], F32, name=tag, tag=tag)
                 cols = slice(t * P, (t + 1) * P)
                 nc.tensor.matmul_mx(
                     out=bank[:],
@@ -110,57 +137,91 @@ def tile_attend_gsig_mom_kernel(tc, xT, wT, y, wt, xm, mT, offs, out_0, out_1):
                 banks.append(bank)
             return banks
 
-        def step(b, w_rounded, x_rounded):
-            w_q = quantize(w_rounded, "w", E4M3)
-            x_q = quantize(x_rounded, "x", E4M3)
-            scores = product("a", x_q, w_q)
-            margin = keep.tile([P, PACK, N], F32, name="margin", tag="margin")
-            weight = keep.tile([P, PACK, N], F32, name="weight", tag="x0")
-            for t in range(PACK):
-                nc.vector.tensor_tensor(margin[:, t, :], scores[t][:], y_raw[b][:, t, :], MULT)
-                nc.scalar.activation(weight[:, t, :], y_raw[b][:, t, :], COPY, scale=neg_wt[:, b, t : t + 1])
-                nc.scalar.activation(margin[:, t, :], margin[:, t, :], SIGMOID, scale=-1.0)
-            xm_rounded = round_stationary(xm_raw[b])
-            g_rounded = rounded()
-            g_view, s_view, weight_view = moving_views(g_rounded, margin, weight)
-            nc.vector.tensor_tensor(g_view, s_view, weight_view, MULT)
-            xm_q = quantize(xm_rounded, "xm", E4M3)
-            g_q = quantize(g_rounded, "g", E5M2)
-            grads = product("dw", xm_q, g_q)
-            for t in range(PACK):
-                gather(m_got, m_src, b, t)
-            for t in range(PACK):
-                nc.vector.scalar_tensor_tensor(m_got[b][:, t, :], m_got[b][:, t, :], BETA, grads[t][:], MULT, ADD)
-            for t in range(PACK):
-                nc.vector.scalar_tensor_tensor(w_got[b][:, t, :], m_got[b][:, t, :], -LR, w_got[b][:, t, :], MULT, ADD)
+        def step(kind, b, t):
+            if kind == "rw":
+                dest = rounded("r%d" % RTAG["w%d" % b])
+                views = moving_views(dest, w_got[b])
+                if b in RW_ON_VECTOR:
+                    nc.vector.tensor_copy(*views)
+                else:
+                    nc.scalar.activation(views[0], views[1], COPY)
+                have["w_q", b] = quantize(dest, "moving%d" % b, E4M3)
+            if kind == "a":
+                x_q = quantize(round_stationary(have["x%d" % b], "x%d" % b), "still%d" % b, E4M3)
+                have["a", b] = product(b, x_q, have["w_q", b])
+            if kind == "wgt":
+                neg_wt = sbuf.tile([P, PACK, 1], F32, name="neg_wt%d" % b)
+                nc.scalar.activation(neg_wt[:], have["wt%d" % b][:], COPY, scale=-1.0)
+                weight = block(sources["x%d" % b][0])
+                for j in range(PACK):
+                    if b in WEIGHT_ON_GPSIMD:
+                        nc.gpsimd.tensor_scalar(weight[:, j, :], have["y%d" % b][:, j, :], neg_wt[:, j, :], 0.0, MULT, ADD)
+                    else:
+                        nc.scalar.activation(weight[:, j, :], have["y%d" % b][:, j, :], COPY, scale=neg_wt[:, j, :])
+                have["weight", b] = weight
+            if kind == "u":
+                margin = block("margin%d" % b)
+                for j in range(PACK):
+                    if (b, j) in U_ON_VECTOR:
+                        nc.vector.tensor_tensor(margin[:, j, :], have["a", b][j][:], have["y%d" % b][:, j, :], MULT)
+                    else:
+                        nc.scalar.activation(margin[:, j, :], have["a", b][j][:], COPY)
+                        nc.gpsimd.tensor_tensor(margin[:, j, :], margin[:, j, :], have["y%d" % b][:, j, :], MULT)
+                    nc.scalar.activation(margin[:, j, :], margin[:, j, :], SIGMOID, scale=-1.0)
+                have["margin", b] = margin
+            if kind == "g":
+                margin, weight = have["margin", b], have["weight", b]
+                dest = rounded("r%d" % RTAG["g%d" % b])
+                g_view, s_view, weight_view = moving_views(dest, margin, weight)
+                if b in G_ON_VECTOR:
+                    nc.vector.tensor_tensor(g_view, s_view, weight_view, MULT)
+                else:
+                    for j in range(PACK):
+                        nc.gpsimd.tensor_tensor(margin[:, j, :], margin[:, j, :], weight[:, j, :], MULT)
+                    nc.scalar.activation(g_view, s_view, COPY)
+                have["g_rounded", b] = dest
+            if kind == "xm":
+                have["xm_q", b] = quantize(round_stationary(have["xm%d" % b], "xm%d" % b), "still%d" % b, E4M3)
+            if kind == "dw":
+                g_q = quantize(have["g_rounded", b], "moving%d" % b, E5M2, "r%d" % RTAG["xm%d" % b] if b in GQ_AFTER_XM else None)
+                have["dw", b] = product(b, have["xm_q", b], g_q)
+                have["grad", b] = block("margin%d" % b)
+                if b in BETA_LATE:
+                    have["kept", b] = block(sources["x%d" % b][0])
+                have["change", b] = block(sources["y%d" % b][0])
+            if kind == "gm":
+                nc.vector.tensor_copy(m_got[b][:, t, :], listed(have["m%d" % t], b))
+            if kind == "nm":
+                new_m = m_got[b][:, t, :]
+                if (b, t) in M_ON_VECTOR:
+                    nc.vector.scalar_tensor_tensor(new_m, new_m, BETA, have["dw", b][t][:], MULT, ADD)
+                else:
+                    grad = have["grad", b][:, t, :]
+                    kept = have["kept", b][:, t, :] if b in BETA_LATE else new_m
+                    if b in BETA_ON_GPSIMD:
+                        nc.gpsimd.tensor_scalar(kept, new_m, BETA, 0.0, MULT, ADD)
+                    else:
+                        nc.scalar.activation(kept, new_m, COPY, scale=BETA)
+                    nc.scalar.activation(grad, have["dw", b][t][:], COPY)
+                    nc.gpsimd.tensor_tensor(new_m, kept, grad, ADD)
+            if kind == "nw":
+                new_w = w_got[b][:, t, :]
+                if (b, t) in W_ON_VECTOR:
+                    nc.vector.scalar_tensor_tensor(new_w, m_got[b][:, t, :], -LR, new_w, MULT, ADD)
+                else:
+                    change = have["change", b][:, t, :]
+                    nc.scalar.activation(change, m_got[b][:, t, :], COPY, scale=-LR)
+                    nc.gpsimd.tensor_tensor(new_w, new_w, change, ADD)
+            if kind == "sm":
+                nc.vector.tensor_copy(listed(have["mo%d" % t], b), m_got[b][:, t, :])
+                if b == B - 1:
+                    nc.sync.dma_start(planes(out_1)[t], have["mo%d" % t][:])
+            if kind == "sw":
+                nc.vector.tensor_copy(listed(have["wo%d" % t], b), w_got[b][:, t, :])
+                if b == B - 1:
+                    nc.sync.dma_start(planes(out_0)[t], have["wo%d" % t][:])
 
-        for t in range(PACK):
-            gather(w_got, w_src, 0, t)
-            nc.scalar.activation(w_out[t][:], w_src[t][:], COPY)
-            if t < PACK - 1:
-                gather(w_got, w_src, 1, t)
-        nc.scalar.activation(neg_wt[:], wt_raw[:], COPY, scale=-1.0)
-        w_rounded = rounded()
-        nc.vector.tensor_copy(*moving_views(w_rounded, w_got[0]))
-        gather(w_got, w_src, 1, PACK - 1)
-        step(0, w_rounded, round_stationary(x_raw[0]))
-
-        x_raw.append(load(ring, "early", rows4(xT[1]), [P, PACK, R]))
-        y_raw.append(load(ring, "early", rows4(y[1]), [P, PACK, N]))
-        xm_raw.append(load(ring, "early", rows4(xm[1]), [P, PACK, D]))
-        m_out = [load(keep, "m_out%d" % t, planes(mT)[t], [P, T]) for t in range(PACK)]
-
-        w_rounded = rounded()
-        w_view, got_view = moving_views(w_rounded, w_got[1])
-        nc.scalar.activation(w_view, got_view, COPY)
-        step(1, w_rounded, round_stationary(x_raw[1]))
-
-        for t in range(PACK):
-            nc.vector.tensor_copy(listed(w_out[t], 0), w_got[0][:, t, :])
-        for t in range(PACK):
-            nc.vector.tensor_copy(listed(m_out[t], 0), m_got[0][:, t, :])
-        for t in range(PACK):
-            nc.vector.tensor_copy(listed(m_out[t], 1), m_got[1][:, t, :])
-            nc.sync.dma_start(planes(out_1)[t], m_out[t][:])
-            nc.vector.tensor_copy(listed(w_out[t], 1), w_got[1][:, t, :])
-            nc.sync.dma_start(planes(out_0)[t], w_out[t][:])
+        for name in STEPS.split():
+            kind, b = name[:-1], int(name[-1])
+            for t in range(PACK if kind in ("gm", "nm", "nw", "sm", "sw") else 1):
+                step(kind, b, t)

@@ -22,19 +22,9 @@ SIGMOID = mybir.ActivationFunctionType.Sigmoid
 P = 128
 PACK = 4
 LIST_COLS = N // 16
-LOADS = 'w0 w1 w2 w3 wt0 m0 x0 m2 y0 m1 m3 mo1 xm0 x1 wo3 wo1 mo2 wo2 wt1 y1 xm1 mo0 mo3 wo0'
-STEPS = 'gm0 rw0 gm1 a0 wgt0 rw1 xm0 u0 g0 dw0 a1 nm0 xm1 nw0 sm0 wgt1 u1 g1 dw1 sw0 nm1 sm1 nw1 sw1'
-RW_ON_VECTOR = (0,)
-WEIGHT_ON_GPSIMD = (0,)
-U_ON_VECTOR = ((0, 0), (0, 3))
-G_ON_VECTOR = (0,)
-M_ON_VECTOR = ((0, 0), (0, 1), (0, 2))
-W_ON_VECTOR = ()
-WO_ON_SCALAR = (1, 3)
-GQ_AFTER_XM = (0,)
-BETA_LATE = (1,)
-BETA_ON_GPSIMD = (0,)
-RTAG = {'w0': 5, 'g0': 5, 'x0': 1, 'xm0': 3, 'w1': 2, 'g1': 4, 'x1': 2, 'xm1': 0}
+CHUNK = 128
+CHUNKS = N // CHUNK
+MARGINS_ON_VECTOR = 4
 
 
 def tile_attend_gsig_mom_kernel(tc, xT, wT, y, wt, xm, mT, offs, out_0, out_1):
@@ -53,175 +43,230 @@ def tile_attend_gsig_mom_kernel(tc, xT, wT, y, wt, xm, mT, offs, out_0, out_1):
         offsets = sbuf.tile([P, B * LIST_COLS], U16, name="offsets")
         nc.sync.dma_start(offsets[:], offs)
 
+        def new(name, shape, dtype, slot=None):
+            return sbuf.tile(shape, dtype, name=name, tag=slot or name, align_bytes=64)
+
         def listed(window, b):
             return window[:].indirect(offsets[:, b * LIST_COLS : (b + 1) * LIST_COLS])
 
-        def load(tag, source, shape):
-            dest = sbuf.tile(shape, F32, name=tag, tag=tag)
+        def load(name, source, shape, slot=None):
+            dest = new(name, shape, F32, slot)
             nc.sync.dma_start(dest[:], source)
             return dest
 
-        w_got = [sbuf.tile([P, PACK, N], F32, name="w_got%d" % b) for b in range(B)]
-        m_got = [sbuf.tile([P, PACK, N], F32, name="m_got%d" % b) for b in range(B)]
+        def load_plane(name, table, t, slot=None):
+            return load(name, planes(table)[t], [P, T], slot)
 
-        warm = sbuf.tile([P, 8], F32, name="warm")
+        def load_rows(name, matrix, slot=None):
+            return load(name, rows4(matrix), [P, PACK, 512], slot)
+
+        warm = new("warm", [P, 8], F32)
         nc.vector.memset(warm[:], 0.0)
         nc.scalar.activation(warm[:], warm[:], SIGMOID)
 
-        have = {}
-        late = dict(zip(("xm1", "y1", "x1"), ["w%d" % t for t in WO_ON_SCALAR]))
+        def moving_views(dest, planar):
+            return dest.rearrange("p (c i j) -> p c j i", i=4, j=PACK), planar.rearrange("p j (c i) -> p c j i", i=4)
 
-        sources = {}
-        for b in range(B):
-            sources["wt%d" % b] = ("wt%d" % b, rows4(wt[b]), [P, PACK, 1])
-            sources["x%d" % b] = (late.get("x%d" % b, "x%d" % b), rows4(xT[b]), [P, PACK, R])
-            sources["y%d" % b] = (late.get("y%d" % b, "y%d" % b), rows4(y[b]), [P, PACK, N])
-            sources["xm%d" % b] = (late.get("xm%d" % b, "xm%d" % b), rows4(xm[b]), [P, PACK, D])
-        for t in range(PACK):
-            sources["w%d" % t] = ("w%d" % t, planes(wT)[t], [P, T])
-            sources["m%d" % t] = ("m%d" % t, planes(mT)[t], [P, T])
-            sources["mo%d" % t] = ("mo%d" % t, planes(mT)[t], [P, T])
-            sources["wo%d" % t] = ("w%d" % t, planes(wT)[t], [P, T])
-        for name in LOADS.split():
-            if name not in have:
-                have[name] = load(*sources[name])
-            if name == "w3":
-                for t in range(PACK):
-                    for b in range(B):
-                        nc.vector.tensor_copy(w_got[b][:, t, :], listed(have["w%d" % t], b))
-                for t in WO_ON_SCALAR:
-                    have["wo%d" % t] = sbuf.tile([P, T], F32, name="wo%d" % t)
-                    nc.scalar.activation(have["wo%d" % t][:], have["w%d" % t][:], COPY)
-
-        def rounded(tag):
-            return sbuf.tile([P, PACK * 512], BF16, name=tag, tag=tag, align_bytes=64)
-
-        def block(tag):
-            return sbuf.tile([P, PACK, N], F32, name=tag, tag=tag)
-
-        def moving_views(dest, *planar):
-            return [dest[:].rearrange("p (c i j) -> p c j i", i=4, j=PACK)] + [
-                s[:].rearrange("p j (c i) -> p c j i", i=4) for s in planar
-            ]
-
-        def round_stationary(raw, name):
-            dest = rounded("r%d" % RTAG[name])
-            nc.scalar.activation(
-                dest[:].rearrange("p (t m j) -> p m j t", t=PACK, j=PACK),
-                raw[:].rearrange("p j (m t) -> p m j t", t=PACK),
-                COPY,
+        def stationary_views(dest, raw, part=slice(0, P)):
+            return (
+                dest.rearrange("p (t m j) -> p m j t", t=PACK, j=PACK)[:, part, :, :],
+                raw.rearrange("p j (m t) -> p m j t", t=PACK)[:, part, :, :],
             )
-            return dest
 
-        def quantize(source, tag, fmt, codes_tag=None):
-            codes = sbuf.tile([P, 512], U32, name=tag + "_codes", tag=codes_tag or tag + "_codes", align_bytes=64)
-            scales = sbuf.tile([P, 512], U8, name=tag + "_scales", tag=tag + "_scales", align_bytes=64)
+        def round_on_scalar(views):
+            nc.scalar.activation(views[0], views[1], COPY)
+
+        def round_on_vector(views):
+            nc.vector.tensor_copy(views[0], views[1])
+
+        def quantize(name, source, fmt, slot=None):
+            codes = new(name + "_codes", [P, 512], U32, slot)
+            scales = new(name + "_scales", [P, 512], U8)
             nc.vector.quantize_mx(out=codes[:].bitcast(fmt), scales=scales[:], in_=source[:])
             return codes, scales, fmt
 
-        def product(b, stationary, moving):
+        def product(out, stationary, t, moving, cols):
+            rows = slice(t * P, (t + 1) * P)
+            nc.tensor.matmul_mx(
+                out=out,
+                lhsT=stationary[0][:, rows].bitcast(stationary[2]),
+                lhsT_scale=stationary[1][:, rows],
+                rhs=moving[0][:, cols].bitcast(moving[2]),
+                rhs_scale=moving[1][:, cols],
+                start=True,
+                stop=True,
+            )
+
+        def scores(b, x_q, w_q):
             banks = []
-            for t in range(PACK):
-                tag = "bank%d%d" % (b, t)
-                bank = psum.tile([P, 512], F32, name=tag, tag=tag)
-                cols = slice(t * P, (t + 1) * P)
-                nc.tensor.matmul_mx(
-                    out=bank[:],
-                    lhsT=stationary[0][:, cols].bitcast(stationary[2]),
-                    lhsT_scale=stationary[1][:, cols],
-                    rhs=moving[0][:].bitcast(moving[2]),
-                    rhs_scale=moving[1][:],
-                    start=True,
-                    stop=True,
-                )
+            for c in range(CHUNKS):
+                bank = psum.tile([P, PACK, CHUNK], F32, name="score%d%d" % (b, c), tag="score%d" % c)
+                for j in range(PACK):
+                    product(bank[:, j, :], x_q, j, w_q, slice(c * CHUNK, (c + 1) * CHUNK))
                 banks.append(bank)
             return banks
 
-        def step(kind, b, t):
-            if kind == "rw":
-                dest = rounded("r%d" % RTAG["w%d" % b])
-                views = moving_views(dest, w_got[b])
-                if b in RW_ON_VECTOR:
-                    nc.vector.tensor_copy(*views)
+        def row_weights(b, y_b, slot):
+            weight = new("weight%d" % b, [P, PACK, N], F32, slot)
+            for j in range(PACK):
+                if b == 0:
+                    nc.gpsimd.tensor_scalar(weight[:, j, :], y_b[:, j, :], neg_wt[:, b, j : j + 1], 0.0, MULT, ADD)
                 else:
-                    nc.scalar.activation(views[0], views[1], COPY)
-                have["w_q", b] = quantize(dest, "moving%d" % b, E4M3)
-            if kind == "a":
-                x_q = quantize(round_stationary(have["x%d" % b], "x%d" % b), "still%d" % b, E4M3)
-                have["a", b] = product(b, x_q, have["w_q", b])
-            if kind == "wgt":
-                neg_wt = sbuf.tile([P, PACK, 1], F32, name="neg_wt%d" % b)
-                nc.scalar.activation(neg_wt[:], have["wt%d" % b][:], COPY, scale=-1.0)
-                weight = block(sources["x%d" % b][0])
-                for j in range(PACK):
-                    if b in WEIGHT_ON_GPSIMD:
-                        nc.gpsimd.tensor_scalar(weight[:, j, :], have["y%d" % b][:, j, :], neg_wt[:, j, :], 0.0, MULT, ADD)
-                    else:
-                        nc.scalar.activation(weight[:, j, :], have["y%d" % b][:, j, :], COPY, scale=neg_wt[:, j, :])
-                have["weight", b] = weight
-            if kind == "u":
-                margin = block("margin%d" % b)
-                for j in range(PACK):
-                    if (b, j) in U_ON_VECTOR:
-                        nc.vector.tensor_tensor(margin[:, j, :], have["a", b][j][:], have["y%d" % b][:, j, :], MULT)
-                    else:
-                        nc.scalar.activation(margin[:, j, :], have["a", b][j][:], COPY)
-                        nc.gpsimd.tensor_tensor(margin[:, j, :], margin[:, j, :], have["y%d" % b][:, j, :], MULT)
-                    nc.scalar.activation(margin[:, j, :], margin[:, j, :], SIGMOID, scale=-1.0)
-                have["margin", b] = margin
-            if kind == "g":
-                margin, weight = have["margin", b], have["weight", b]
-                dest = rounded("r%d" % RTAG["g%d" % b])
-                g_view, s_view, weight_view = moving_views(dest, margin, weight)
-                if b in G_ON_VECTOR:
-                    nc.vector.tensor_tensor(g_view, s_view, weight_view, MULT)
-                else:
-                    for j in range(PACK):
-                        nc.gpsimd.tensor_tensor(margin[:, j, :], margin[:, j, :], weight[:, j, :], MULT)
-                    nc.scalar.activation(g_view, s_view, COPY)
-                have["g_rounded", b] = dest
-            if kind == "xm":
-                have["xm_q", b] = quantize(round_stationary(have["xm%d" % b], "xm%d" % b), "still%d" % b, E4M3)
-            if kind == "dw":
-                g_q = quantize(have["g_rounded", b], "moving%d" % b, E5M2, "r%d" % RTAG["xm%d" % b] if b in GQ_AFTER_XM else None)
-                have["dw", b] = product(b, have["xm_q", b], g_q)
-                have["grad", b] = block("margin%d" % b)
-                if b in BETA_LATE:
-                    have["kept", b] = block(sources["x%d" % b][0])
-                have["change", b] = block(sources["y%d" % b][0])
-            if kind == "gm":
-                nc.vector.tensor_copy(m_got[b][:, t, :], listed(have["m%d" % t], b))
-            if kind == "nm":
-                new_m = m_got[b][:, t, :]
-                if (b, t) in M_ON_VECTOR:
-                    nc.vector.scalar_tensor_tensor(new_m, new_m, BETA, have["dw", b][t][:], MULT, ADD)
-                else:
-                    grad = have["grad", b][:, t, :]
-                    kept = have["kept", b][:, t, :] if b in BETA_LATE else new_m
-                    if b in BETA_ON_GPSIMD:
-                        nc.gpsimd.tensor_scalar(kept, new_m, BETA, 0.0, MULT, ADD)
-                    else:
-                        nc.scalar.activation(kept, new_m, COPY, scale=BETA)
-                    nc.scalar.activation(grad, have["dw", b][t][:], COPY)
-                    nc.gpsimd.tensor_tensor(new_m, kept, grad, ADD)
-            if kind == "nw":
-                new_w = w_got[b][:, t, :]
-                if (b, t) in W_ON_VECTOR:
-                    nc.vector.scalar_tensor_tensor(new_w, m_got[b][:, t, :], -LR, new_w, MULT, ADD)
-                else:
-                    change = have["change", b][:, t, :]
-                    nc.scalar.activation(change, m_got[b][:, t, :], COPY, scale=-LR)
-                    nc.gpsimd.tensor_tensor(new_w, new_w, change, ADD)
-            if kind == "sm":
-                nc.vector.tensor_copy(listed(have["mo%d" % t], b), m_got[b][:, t, :])
-                if b == B - 1:
-                    nc.sync.dma_start(planes(out_1)[t], have["mo%d" % t][:])
-            if kind == "sw":
-                nc.vector.tensor_copy(listed(have["wo%d" % t], b), w_got[b][:, t, :])
-                if b == B - 1:
-                    nc.sync.dma_start(planes(out_0)[t], have["wo%d" % t][:])
+                    nc.scalar.activation(weight[:, j, :], y_b[:, j, :], COPY, scale=neg_wt[:, b, j : j + 1])
+            return weight
 
-        for name in STEPS.split():
-            kind, b = name[:-1], int(name[-1])
-            for t in range(PACK if kind in ("gm", "nm", "nw", "sm", "sw") else 1):
-                step(kind, b, t)
+        def gradient(b, banks, y_b, weight, on_vector):
+            rounded = new("g_rounded%d" % b, [P, PACK * N], BF16)
+            margins = [new("margin%d%d" % (b, c), [P, PACK, CHUNK], F32, "margin%d" % c)[:] for c in range(CHUNKS)]
+
+            def cols(c):
+                return slice(c * CHUNK, (c + 1) * CHUNK)
+
+            def leave_bank(c):
+                if c < on_vector:
+                    nc.vector.tensor_tensor(margins[c], banks[c][:], y_b[:, :, cols(c)], MULT)
+                else:
+                    nc.scalar.activation(margins[c], banks[c][:], COPY)
+
+            def times_y(c):
+                if c >= on_vector:
+                    nc.gpsimd.tensor_tensor(margins[c], margins[c], y_b[:, :, cols(c)], MULT)
+
+            def sigmoid(c):
+                nc.scalar.activation(margins[c], margins[c], SIGMOID, scale=-1.0)
+
+            def times_weight(c):
+                nc.gpsimd.tensor_tensor(margins[c], margins[c], weight[:, :, cols(c)], MULT)
+
+            def round_chunk(c):
+                round_on_scalar(moving_views(rounded[:, c * PACK * CHUNK : (c + 1) * PACK * CHUNK], margins[c]))
+
+            stages = [leave_bank, times_y, sigmoid, times_weight, round_chunk]
+            for tick in range(CHUNKS + len(stages) - 1):
+                for s in reversed(range(len(stages))):
+                    if 0 <= tick - s < CHUNKS:
+                        stages[s](tick - s)
+            return rounded
+
+        def table_gradient(b, xm_q, g_q):
+            banks = []
+            for t in range(PACK):
+                bank = psum.tile([P, N], F32, name="dw%d%d" % (b, t), tag="dw%d" % t)
+                product(bank[:], xm_q, t, g_q, slice(0, N))
+                banks.append(bank)
+            return banks
+
+        def gather_kept(t, slot=None):
+            pair = new("kept%d" % t, [P, B, N], F32, slot) if slot else None
+            for b in range(B):
+                momentum[b, t] = pair[:, b, :] if slot else new("kept%d%d" % (b, t), [P, N], F32)[:]
+                nc.vector.tensor_scalar(momentum[b, t], listed(m_in[t], b), BETA, 0.0, MULT, ADD)
+
+        def update_m(b, t, bank, slot=None):
+            new_m = momentum[b, t]
+            grad = new("grad%d%d" % (b, t), [P, N], F32, slot or "grad%d" % t)
+            nc.scalar.activation(grad[:], bank[:], COPY)
+            nc.gpsimd.tensor_tensor(new_m, new_m, grad[:], ADD)
+
+        def update_w(b, t, change):
+            nc.scalar.activation(change, momentum[b, t], COPY, scale=-LR)
+            new_w = w_got[:, t, b * N : (b + 1) * N]
+            nc.gpsimd.tensor_tensor(new_w, new_w, change, ADD)
+
+        def scatter_w(b, t):
+            nc.vector.tensor_copy(listed(w_out[t], b), w_got[:, t, b * N : (b + 1) * N])
+
+        def scatter_m(b, t):
+            nc.vector.tensor_copy(listed(m_out[t], b), momentum[b, t])
+
+        momentum, w_out, m_out, m_in = {}, {}, {}, {}
+        w_got = new("w_got", [P, PACK, B * N], F32)
+        w_in = [load_plane("w%d" % t, wT, t) for t in range(PACK)]
+        x0 = load_rows("x0", xT[0])
+        wt_in = new("wt_in", [P, B, PACK], F32)
+        nc.sync.dma_start(wt_in[:], wt.rearrange("b (p j) c -> p b (j c)", j=PACK))
+        m_in[0] = load_plane("m0", mT, 0)
+        y0 = load_rows("y0", y[0])
+        xm0 = load_rows("xm0", xm[0])
+        for t in range(1, PACK):
+            m_in[t] = load_plane("m%d" % t, mT, t)
+
+        for t in range(PACK):
+            nc.vector.tensor_copy(w_got[:, t, :], w_in[t][:].indirect(offsets[:]))
+        for t in range(PACK - 1):
+            w_out[t] = new("w_out%d" % t, [P, T], F32)
+            nc.scalar.activation(w_out[t][:], w_in[t][:], COPY)
+
+        w_rounded = new("w_rounded0", [P, PACK * N], BF16)
+        round_on_vector(moving_views(w_rounded[:], w_got[:, :, 0:N]))
+        w_q = quantize("w0", w_rounded, E4M3)
+        x_rounded = new("x_rounded0", [P, PACK * R], BF16, "x_rounded")
+        round_on_scalar(stationary_views(x_rounded[:], x0[:]))
+        x_q = quantize("x0", x_rounded, E4M3)
+        banks = scores(0, x_q, w_q)
+        gather_kept(0, "x_rounded")
+        w1_rounded = new("w_rounded1", [P, PACK * N], BF16, "x0")
+        round_on_scalar(moving_views(w1_rounded[:], w_got[:, :, N : 2 * N]))
+        neg_wt = new("neg_wt", [P, B, PACK], F32)
+        nc.scalar.activation(neg_wt[:], wt_in[:], COPY, scale=-1.0)
+        weight = row_weights(0, y0, "weight")
+        xm_rounded = new("xm_rounded0", [P, PACK * D], BF16)
+        round_on_scalar(stationary_views(xm_rounded[:], xm0[:]))
+        g_rounded = gradient(0, banks, y0, weight, MARGINS_ON_VECTOR)
+        gather_kept(1)
+        xm_q = quantize("xm0", xm_rounded, E4M3, "m1")
+        gather_kept(2)
+        g_q = quantize("g0", g_rounded, E5M2, "m2")
+        gather_kept(3, "g_rounded0")
+        banks = table_gradient(0, xm_q, g_q)
+        w_q = quantize("w1", w1_rounded, E4M3, "m3")
+
+        x1 = load_rows("x1", xT[1], "m0")
+        xm1 = load_rows("xm1", xm[1], "xm0")
+        y1 = load_rows("y1", y[1], "y0")
+        for t in range(PACK):
+            m_out[t] = load_plane("m_out%d" % t, mT, t, "w%d" % t)
+        w_out[3] = load_plane("w_out3", wT, 3, "m1")
+
+        change = new("change_kept", [P, N], F32, "margin2")
+        update_w(0, 0, change[:])
+        change = new("change_grad", [P, N], F32)
+        nc.scalar.activation(change[:], banks[0][:], COPY, scale=-LR)
+        nc.gpsimd.tensor_tensor(w_got[:, 0, 0:N], w_got[:, 0, 0:N], change[:], ADD)
+        scatter_w(0, 0)
+        for t in (1, 2, 0):
+            update_m(0, t, banks[t])
+        last_bank = banks[3]
+        x_rounded = new("x_rounded1", [P, PACK * R], BF16, "w_rounded0")
+        round_on_scalar(stationary_views(x_rounded[:], x1[:]))
+        x_q = quantize("x1", x_rounded, E4M3)
+        banks = scores(1, x_q, w_q)
+        changes = new("changes0", [P, 2, N], F32, "m0")
+        for t in (1, 2):
+            update_w(0, t, changes[:, t - 1, :])
+        xm_rounded = new("xm_rounded1", [P, PACK * D], BF16, "xm_rounded0")
+        round_on_scalar(stationary_views(xm_rounded[:], xm1[:]))
+        weight = row_weights(1, y1, "weight")
+        scatter_w(0, 1)
+        xm_q = quantize("xm1", xm_rounded, E4M3)
+        scatter_w(0, 2)
+        g_rounded = gradient(1, banks, y1, weight, 0)
+        scatter_m(0, 0)
+        scatter_m(0, 1)
+        scatter_m(0, 2)
+        update_m(0, 3, last_bank, "margin2")
+        g_q = quantize("g1", g_rounded, E5M2, "kept02")
+        banks = table_gradient(1, xm_q, g_q)
+        scatter_m(0, 3)
+        change = new("change03", [P, N], F32, "change_grad")
+        update_w(0, 3, change[:])
+        scatter_w(0, 3)
+        changes = new("changes1", [P, PACK, N], F32, "m0")
+        for t in range(PACK):
+            update_m(1, t, banks[t])
+            update_w(1, t, changes[:, t, :])
+        for t in range(PACK):
+            scatter_m(1, t)
+            nc.sync.dma_start(planes(out_1)[t], m_out[t][:])
+            scatter_w(1, t)
+            nc.sync.dma_start(planes(out_0)[t], w_out[t][:])

@@ -22,8 +22,6 @@ SIGMOID = mybir.ActivationFunctionType.Sigmoid
 P = 128
 PACK = 4
 LIST_COLS = N // 16
-CHUNK = 128
-CHUNKS = N // CHUNK
 MARGINS_ON_VECTOR = 4
 
 
@@ -99,10 +97,9 @@ def tile_attend_gsig_mom_kernel(tc, xT, wT, y, wt, xm, mT, offs, out_0, out_1):
 
         def scores(b, x_q, w_q):
             banks = []
-            for c in range(CHUNKS):
-                bank = psum.tile([P, PACK, CHUNK], F32, name="score%d%d" % (b, c), tag="score%d" % c)
-                for j in range(PACK):
-                    product(bank[:, j, :], x_q, j, w_q, slice(c * CHUNK, (c + 1) * CHUNK))
+            for j in range(PACK):
+                bank = psum.tile([P, N], F32, name="score%d%d" % (b, j), tag="score%d" % j)
+                product(bank[:], x_q, j, w_q, slice(0, N))
                 banks.append(bank)
             return banks
 
@@ -117,35 +114,32 @@ def tile_attend_gsig_mom_kernel(tc, xT, wT, y, wt, xm, mT, offs, out_0, out_1):
 
         def gradient(b, banks, y_b, weight, on_vector):
             rounded = new("g_rounded%d" % b, [P, PACK * N], BF16)
-            margins = [new("margin%d%d" % (b, c), [P, PACK, CHUNK], F32, "margin%d" % c)[:] for c in range(CHUNKS)]
+            margin = new("margin%d" % b, [P, PACK, N], F32, "margin")
 
-            def cols(c):
-                return slice(c * CHUNK, (c + 1) * CHUNK)
-
-            def leave_bank(c):
-                if c < on_vector:
-                    nc.vector.tensor_tensor(margins[c], banks[c][:], y_b[:, :, cols(c)], MULT)
+            def leave_bank(j):
+                if j < on_vector:
+                    nc.vector.tensor_tensor(margin[:, j, :], banks[j][:], y_b[:, j, :], MULT)
                 else:
-                    nc.scalar.activation(margins[c], banks[c][:], COPY)
+                    nc.scalar.activation(margin[:, j, :], banks[j][:], COPY)
 
-            def times_y(c):
-                if c >= on_vector:
-                    nc.gpsimd.tensor_tensor(margins[c], margins[c], y_b[:, :, cols(c)], MULT)
+            def times_y(j):
+                if j >= on_vector:
+                    nc.gpsimd.tensor_tensor(margin[:, j, :], margin[:, j, :], y_b[:, j, :], MULT)
 
-            def sigmoid(c):
-                nc.scalar.activation(margins[c], margins[c], SIGMOID, scale=-1.0)
+            def sigmoid(j):
+                nc.scalar.activation(margin[:, j, :], margin[:, j, :], SIGMOID, scale=-1.0)
 
-            def times_weight(c):
-                nc.gpsimd.tensor_tensor(margins[c], margins[c], weight[:, :, cols(c)], MULT)
+            def times_weight(j):
+                for cols in halves if j == PACK - 1 else [slice(0, N)]:
+                    nc.gpsimd.tensor_tensor(margin[:, j, cols], margin[:, j, cols], weight[:, j, cols], MULT)
 
-            def round_chunk(c):
-                round_on_scalar(moving_views(rounded[:, c * PACK * CHUNK : (c + 1) * PACK * CHUNK], margins[c]))
-
-            stages = [leave_bank, times_y, sigmoid, times_weight, round_chunk]
-            for tick in range(CHUNKS + len(stages) - 1):
+            stages = [leave_bank, times_y, sigmoid, times_weight]
+            for tick in range(PACK + len(stages) - 1):
                 for s in reversed(range(len(stages))):
-                    if 0 <= tick - s < CHUNKS:
+                    if 0 <= tick - s < PACK:
                         stages[s](tick - s)
+            for cols in halves:
+                round_on_scalar(moving_views(rounded[:, cols.start * PACK : cols.stop * PACK], margin[:, :, cols]))
             return rounded
 
         def table_gradient(b, xm_q, g_q):
@@ -156,17 +150,16 @@ def tile_attend_gsig_mom_kernel(tc, xT, wT, y, wt, xm, mT, offs, out_0, out_1):
                 banks.append(bank)
             return banks
 
-        def gather_kept(t, slot=None):
-            pair = new("kept%d" % t, [P, B, N], F32, slot) if slot else None
-            for b in range(B):
-                momentum[b, t] = pair[:, b, :] if slot else new("kept%d%d" % (b, t), [P, N], F32)[:]
-                nc.vector.tensor_scalar(momentum[b, t], listed(m_in[t], b), BETA, 0.0, MULT, ADD)
+        def gather_kept(b, t, slot=None):
+            momentum[b, t] = new("kept%d%d" % (b, t), [P, N], F32, slot)[:]
+            nc.vector.tensor_scalar(momentum[b, t], listed(m_in[t], b), BETA, 0.0, MULT, ADD)
 
-        def update_m(b, t, bank, slot=None):
+        def update_m(b, t, bank, grad=None):
             new_m = momentum[b, t]
-            grad = new("grad%d%d" % (b, t), [P, N], F32, slot or "grad%d" % t)
-            nc.scalar.activation(grad[:], bank[:], COPY)
-            nc.gpsimd.tensor_tensor(new_m, new_m, grad[:], ADD)
+            if grad is None:
+                grad = new("grad%d%d" % (b, t), [P, N], F32, "grad%d" % t)[:]
+            nc.scalar.activation(grad, bank[:], COPY)
+            nc.gpsimd.tensor_tensor(new_m, new_m, grad, ADD)
 
         def update_w(b, t, change):
             nc.scalar.activation(change, momentum[b, t], COPY, scale=-LR)
@@ -179,6 +172,7 @@ def tile_attend_gsig_mom_kernel(tc, xT, wT, y, wt, xm, mT, offs, out_0, out_1):
         def scatter_m(b, t):
             nc.vector.tensor_copy(listed(m_out[t], b), momentum[b, t])
 
+        halves = [slice(0, N // 2), slice(N // 2, N)]
         momentum, w_out, m_out, m_in = {}, {}, {}, {}
         w_got = new("w_got", [P, PACK, B * N], F32)
         w_in = [load_plane("w%d" % t, wT, t) for t in range(PACK)]
@@ -204,7 +198,8 @@ def tile_attend_gsig_mom_kernel(tc, xT, wT, y, wt, xm, mT, offs, out_0, out_1):
         round_on_scalar(stationary_views(x_rounded[:], x0[:]))
         x_q = quantize("x0", x_rounded, E4M3)
         banks = scores(0, x_q, w_q)
-        gather_kept(0, "x_rounded")
+        gather_kept(0, 0, "x_rounded")
+        gather_kept(1, 0, "w_rounded0")
         w1_rounded = new("w_rounded1", [P, PACK * N], BF16, "x0")
         round_on_scalar(moving_views(w1_rounded[:], w_got[:, :, N : 2 * N]))
         neg_wt = new("neg_wt", [P, B, PACK], F32)
@@ -213,11 +208,14 @@ def tile_attend_gsig_mom_kernel(tc, xT, wT, y, wt, xm, mT, offs, out_0, out_1):
         xm_rounded = new("xm_rounded0", [P, PACK * D], BF16)
         round_on_scalar(stationary_views(xm_rounded[:], xm0[:]))
         g_rounded = gradient(0, banks, y0, weight, MARGINS_ON_VECTOR)
-        gather_kept(1)
+        gather_kept(0, 1)
+        gather_kept(1, 1)
         xm_q = quantize("xm0", xm_rounded, E4M3, "m1")
-        gather_kept(2)
+        gather_kept(0, 2)
+        gather_kept(1, 2)
         g_q = quantize("g0", g_rounded, E5M2, "m2")
-        gather_kept(3, "g_rounded0")
+        gather_kept(0, 3, "g_rounded0")
+        gather_kept(1, 3)
         banks = table_gradient(0, xm_q, g_q)
         w_q = quantize("w1", w1_rounded, E4M3, "m3")
 
@@ -228,22 +226,24 @@ def tile_attend_gsig_mom_kernel(tc, xT, wT, y, wt, xm, mT, offs, out_0, out_1):
             m_out[t] = load_plane("m_out%d" % t, mT, t, "w%d" % t)
         w_out[3] = load_plane("w_out3", wT, 3, "m1")
 
-        change = new("change_kept", [P, N], F32, "margin2")
+        change = new("change_kept", [P, N], F32, "weight")
         update_w(0, 0, change[:])
         change = new("change_grad", [P, N], F32)
         nc.scalar.activation(change[:], banks[0][:], COPY, scale=-LR)
         nc.gpsimd.tensor_tensor(w_got[:, 0, 0:N], w_got[:, 0, 0:N], change[:], ADD)
         scatter_w(0, 0)
-        for t in (1, 2, 0):
+        for t in (1, 2):
             update_m(0, t, banks[t])
-        last_bank = banks[3]
-        x_rounded = new("x_rounded1", [P, PACK * R], BF16, "w_rounded0")
+        dw_banks = banks
+        x_rounded = new("x_rounded1", [P, PACK * R], BF16)
         round_on_scalar(stationary_views(x_rounded[:], x1[:]))
         x_q = quantize("x1", x_rounded, E4M3)
         banks = scores(1, x_q, w_q)
-        changes = new("changes0", [P, 2, N], F32, "m0")
+        staged = new("staged0", [P, PACK, N], F32, "m0")
         for t in (1, 2):
-            update_w(0, t, changes[:, t - 1, :])
+            update_w(0, t, staged[:, t, :])
+        for t in (0, 3):
+            update_m(0, t, dw_banks[t], staged[:, t, :])
         xm_rounded = new("xm_rounded1", [P, PACK * D], BF16, "xm_rounded0")
         round_on_scalar(stationary_views(xm_rounded[:], xm1[:]))
         weight = row_weights(1, y1, "weight")
@@ -254,19 +254,21 @@ def tile_attend_gsig_mom_kernel(tc, xT, wT, y, wt, xm, mT, offs, out_0, out_1):
         scatter_m(0, 0)
         scatter_m(0, 1)
         scatter_m(0, 2)
-        update_m(0, 3, last_bank, "margin2")
-        g_q = quantize("g1", g_rounded, E5M2, "kept02")
-        banks = table_gradient(1, xm_q, g_q)
         scatter_m(0, 3)
         change = new("change03", [P, N], F32, "change_grad")
-        update_w(0, 3, change[:])
-        scatter_w(0, 3)
+        nc.scalar.activation(change[:], momentum[0, 3], COPY, scale=-LR)
+        g_q = quantize("g1", g_rounded, E5M2, "g_rounded0")
+        banks = table_gradient(1, xm_q, g_q)
+        last_w = new("last_w", [P, N], F32, "margin")
+        nc.gpsimd.tensor_tensor(last_w[:], w_got[:, 3, 0:N], change[:], ADD)
+        nc.vector.tensor_copy(listed(w_out[3], 0), last_w[:])
         changes = new("changes1", [P, PACK, N], F32, "m0")
-        for t in range(PACK):
-            update_m(1, t, banks[t])
-            update_w(1, t, changes[:, t, :])
-        for t in range(PACK):
-            scatter_m(1, t)
-            nc.sync.dma_start(planes(out_1)[t], m_out[t][:])
-            scatter_w(1, t)
-            nc.sync.dma_start(planes(out_0)[t], w_out[t][:])
+        for t in range(PACK + 1):
+            if t < PACK:
+                update_m(1, t, banks[t])
+                scatter_m(1, t)
+                nc.sync.dma_start(planes(out_1)[t], m_out[t][:])
+            if t > 0:
+                update_w(1, t - 1, changes[:, t - 1, :])
+                scatter_w(1, t - 1)
+                nc.sync.dma_start(planes(out_0)[t - 1], w_out[t - 1][:])

@@ -150,16 +150,20 @@ def tile_attend_gsig_mom_kernel(tc, xT, wT, y, wt, xm, mT, offs, out_0, out_1):
                 banks.append(bank)
             return banks
 
-        def gather_kept(b, t, slot=None):
-            momentum[b, t] = new("kept%d%d" % (b, t), [P, N], F32, slot)[:]
-            nc.vector.tensor_scalar(momentum[b, t], listed(m_in[t], b), BETA, 0.0, MULT, ADD)
+        def gather_m(b, t, slot=None):
+            momentum[b, t] = new("m_got%d%d" % (b, t), [P, N], F32, slot)[:]
+            nc.vector.tensor_copy(momentum[b, t], listed(m_in[t], b))
 
-        def update_m(b, t, bank, grad=None):
-            new_m = momentum[b, t]
+        def decay(b, t, kept):
+            nc.scalar.activation(kept, momentum[b, t], COPY, scale=BETA)
+
+        def update_m(b, t, bank, kept, grad=None, dest=None):
+            new_m = momentum[b, t] if dest is None else dest
+            momentum[b, t] = new_m
             if grad is None:
                 grad = new("grad%d%d" % (b, t), [P, N], F32, "grad%d" % t)[:]
             nc.scalar.activation(grad, bank[:], COPY)
-            nc.gpsimd.tensor_tensor(new_m, new_m, grad, ADD)
+            nc.gpsimd.tensor_tensor(new_m, kept, grad, ADD)
 
         def update_w(b, t, change):
             nc.scalar.activation(change, momentum[b, t], COPY, scale=-LR)
@@ -186,7 +190,8 @@ def tile_attend_gsig_mom_kernel(tc, xT, wT, y, wt, xm, mT, offs, out_0, out_1):
             m_in[t] = load_plane("m%d" % t, mT, t)
 
         for t in range(PACK):
-            nc.vector.tensor_copy(w_got[:, t, :], w_in[t][:].indirect(offsets[:]))
+            for b in range(B):
+                nc.vector.tensor_copy(w_got[:, t, b * N : (b + 1) * N], listed(w_in[t], b))
         for t in range(PACK - 1):
             w_out[t] = new("w_out%d" % t, [P, T], F32)
             nc.scalar.activation(w_out[t][:], w_in[t][:], COPY)
@@ -198,74 +203,81 @@ def tile_attend_gsig_mom_kernel(tc, xT, wT, y, wt, xm, mT, offs, out_0, out_1):
         round_on_scalar(stationary_views(x_rounded[:], x0[:]))
         x_q = quantize("x0", x_rounded, E4M3)
         banks = scores(0, x_q, w_q)
-        gather_kept(0, 0, "x_rounded")
-        gather_kept(1, 0, "w_rounded0")
+        gather_m(0, 0, "x_rounded")
+        gather_m(1, 0, "w_rounded0")
         w1_rounded = new("w_rounded1", [P, PACK * N], BF16, "x0")
         round_on_scalar(moving_views(w1_rounded[:], w_got[:, :, N : 2 * N]))
         neg_wt = new("neg_wt", [P, B, PACK], F32)
         nc.scalar.activation(neg_wt[:], wt_in[:], COPY, scale=-1.0)
+        drift = new("drift", [P, N], F32)
+        nc.scalar.activation(drift[:], momentum[0, 0], COPY, scale=-LR * BETA)
+        kept = new("kept00", [P, N], F32)
+        decay(0, 0, kept[:])
         weight = row_weights(0, y0, "weight")
         xm_rounded = new("xm_rounded0", [P, PACK * D], BF16)
         round_on_scalar(stationary_views(xm_rounded[:], xm0[:]))
         g_rounded = gradient(0, banks, y0, weight, MARGINS_ON_VECTOR)
-        gather_kept(0, 1)
-        gather_kept(1, 1)
-        xm_q = quantize("xm0", xm_rounded, E4M3, "m1")
-        gather_kept(0, 2)
-        gather_kept(1, 2)
-        g_q = quantize("g0", g_rounded, E5M2, "m2")
-        gather_kept(0, 3, "g_rounded0")
-        gather_kept(1, 3)
+        early = new("early", [P, 3, N], F32, "weight")
+        nc.gpsimd.tensor_tensor(early[:, 0, :], w_got[:, 0, 0:N], drift[:], ADD)
+        for t in (1, 2):
+            for b in range(B):
+                gather_m(b, t)
+        xm_q = quantize("xm0", xm_rounded, E4M3, "m2")
+        g_q = quantize("g0", g_rounded, E5M2, "xm_rounded0")
         banks = table_gradient(0, xm_q, g_q)
-        w_q = quantize("w1", w1_rounded, E4M3, "m3")
+        w_q = quantize("w1", w1_rounded, E4M3, "g_rounded0")
+        gather_m(0, 3, "x0")
+        gather_m(1, 3)
 
-        x1 = load_rows("x1", xT[1], "m0")
-        xm1 = load_rows("xm1", xm[1], "xm0")
-        y1 = load_rows("y1", y[1], "y0")
-        for t in range(PACK):
-            m_out[t] = load_plane("m_out%d" % t, mT, t, "w%d" % t)
+        x1 = load_rows("x1", xT[1], "w0")
+        y1 = load_rows("y1", y[1], "w2")
+        xm1 = load_rows("xm1", xm[1], "w3")
+        for t, slot in ((1, "w1"), (2, "m0"), (0, "y0"), (3, "xm0")):
+            m_out[t] = load_plane("m_out%d" % t, mT, t, slot)
         w_out[3] = load_plane("w_out3", wT, 3, "m1")
 
-        change = new("change_kept", [P, N], F32, "weight")
-        update_w(0, 0, change[:])
+        for t in (1, 2):
+            decay(0, t, early[:, t, :])
         change = new("change_grad", [P, N], F32)
         nc.scalar.activation(change[:], banks[0][:], COPY, scale=-LR)
-        nc.gpsimd.tensor_tensor(w_got[:, 0, 0:N], w_got[:, 0, 0:N], change[:], ADD)
+        nc.gpsimd.tensor_tensor(w_got[:, 0, 0:N], early[:, 0, :], change[:], ADD)
         scatter_w(0, 0)
-        for t in (1, 2):
-            update_m(0, t, banks[t])
+        update_m(0, 1, banks[1], early[:, 1, :])
+        update_w(0, 1, new("change01", [P, N], F32, "drift")[:])
+        update_m(0, 2, banks[2], early[:, 2, :])
+        update_m(0, 0, banks[0], kept[:], dest=new("new_m00", [P, N], F32, "drift")[:])
+        scatter_w(0, 1)
         dw_banks = banks
         x_rounded = new("x_rounded1", [P, PACK * R], BF16)
         round_on_scalar(stationary_views(x_rounded[:], x1[:]))
         x_q = quantize("x1", x_rounded, E4M3)
         banks = scores(1, x_q, w_q)
-        staged = new("staged0", [P, PACK, N], F32, "m0")
-        for t in (1, 2):
-            update_w(0, t, staged[:, t, :])
-        for t in (0, 3):
-            update_m(0, t, dw_banks[t], staged[:, t, :])
-        xm_rounded = new("xm_rounded1", [P, PACK * D], BF16, "xm_rounded0")
-        round_on_scalar(stationary_views(xm_rounded[:], xm1[:]))
+        staged = new("staged0", [P, 3, N], F32, "w0")
+        update_w(0, 2, staged[:, 2, :])
+        decay(0, 3, staged[:, 0, :])
+        decay(1, 0, staged[:, 1, :])
         weight = row_weights(1, y1, "weight")
-        scatter_w(0, 1)
-        xm_q = quantize("xm1", xm_rounded, E4M3)
         scatter_w(0, 2)
+        update_m(0, 3, dw_banks[3], staged[:, 0, :], new("grad03", [P, N], F32, "neg_wt")[:])
         g_rounded = gradient(1, banks, y1, weight, 0)
-        scatter_m(0, 0)
-        scatter_m(0, 1)
-        scatter_m(0, 2)
-        scatter_m(0, 3)
+        xm_rounded = new("xm_rounded1", [P, PACK * D], BF16)
+        round_on_scalar(stationary_views(xm_rounded[:], xm1[:]))
+        for t in (1, 2, 0, 3):
+            scatter_m(0, t)
         change = new("change03", [P, N], F32, "change_grad")
         nc.scalar.activation(change[:], momentum[0, 3], COPY, scale=-LR)
-        g_q = quantize("g1", g_rounded, E5M2, "g_rounded0")
+        xm_q = quantize("xm1", xm_rounded, E4M3, "x0")
+        g_q = quantize("g1", g_rounded, E5M2, "xm_rounded1")
         banks = table_gradient(1, xm_q, g_q)
-        last_w = new("last_w", [P, N], F32, "margin")
-        nc.gpsimd.tensor_tensor(last_w[:], w_got[:, 3, 0:N], change[:], ADD)
-        nc.vector.tensor_copy(listed(w_out[3], 0), last_w[:])
-        changes = new("changes1", [P, PACK, N], F32, "m0")
+        late = new("late", [P, PACK + 1, N], F32, "margin")
+        nc.gpsimd.tensor_tensor(late[:, PACK, :], w_got[:, 3, 0:N], change[:], ADD)
+        nc.vector.tensor_copy(listed(w_out[3], 0), late[:, PACK, :])
+        for t in range(1, PACK):
+            decay(1, t, late[:, t, :])
+        changes = new("changes1", [P, PACK, N], F32, "w2")
         for t in range(PACK + 1):
             if t < PACK:
-                update_m(1, t, banks[t])
+                update_m(1, t, banks[t], late[:, t, :] if t else staged[:, 1, :])
                 scatter_m(1, t)
                 nc.sync.dma_start(planes(out_1)[t], m_out[t][:])
             if t > 0:

@@ -21,8 +21,8 @@ SIGMOID = mybir.ActivationFunctionType.Sigmoid
 
 P = 128
 PACK = 4
+HALF = N // 2
 LIST_COLS = N // 16
-MARGINS_ON_VECTOR = 4
 
 
 def tile_attend_gsig_mom_kernel(tc, xT, wT, y, wt, xm, mT, offs, out_0, out_1):
@@ -65,10 +65,10 @@ def tile_attend_gsig_mom_kernel(tc, xT, wT, y, wt, xm, mT, offs, out_0, out_1):
         def moving_views(dest, planar):
             return dest.rearrange("p (c i j) -> p c j i", i=4, j=PACK), planar.rearrange("p j (c i) -> p c j i", i=4)
 
-        def stationary_views(dest, raw, part=slice(0, P)):
+        def stationary_views(dest, raw):
             return (
-                dest.rearrange("p (t m j) -> p m j t", t=PACK, j=PACK)[:, part, :, :],
-                raw.rearrange("p j (m t) -> p m j t", t=PACK)[:, part, :, :],
+                dest.rearrange("p (t m j) -> p m j t", t=PACK, j=PACK),
+                raw.rearrange("p j (m t) -> p m j t", t=PACK),
             )
 
         def round_on_scalar(views):
@@ -83,101 +83,88 @@ def tile_attend_gsig_mom_kernel(tc, xT, wT, y, wt, xm, mT, offs, out_0, out_1):
             nc.vector.quantize_mx(out=codes[:].bitcast(fmt), scales=scales[:], in_=source[:])
             return codes, scales, fmt
 
-        def product(out, stationary, t, moving, cols):
-            rows = slice(t * P, (t + 1) * P)
-            nc.tensor.matmul_mx(
-                out=out,
-                lhsT=stationary[0][:, rows].bitcast(stationary[2]),
-                lhsT_scale=stationary[1][:, rows],
-                rhs=moving[0][:, cols].bitcast(moving[2]),
-                rhs_scale=moving[1][:, cols],
-                start=True,
-                stop=True,
-            )
-
-        def scores(b, x_q, w_q):
-            banks = []
-            for j in range(PACK):
-                bank = psum.tile([P, N], F32, name="score%d%d" % (b, j), tag="score%d" % j)
-                product(bank[:], x_q, j, w_q, slice(0, N))
-                banks.append(bank)
-            return banks
-
-        def row_weights(b, y_b, slot):
-            weight = new("weight%d" % b, [P, PACK, N], F32, slot)
-            for j in range(PACK):
-                if b == 0:
-                    nc.gpsimd.tensor_scalar(weight[:, j, :], y_b[:, j, :], neg_wt[:, b, j : j + 1], 0.0, MULT, ADD)
-                else:
-                    nc.scalar.activation(weight[:, j, :], y_b[:, j, :], COPY, scale=neg_wt[:, b, j : j + 1])
-            return weight
-
-        def gradient(b, banks, y_b, weight, on_vector):
-            rounded = new("g_rounded%d" % b, [P, PACK * N], BF16)
-            margin = new("margin%d" % b, [P, PACK, N], F32, "margin")
-
-            def leave_bank(j):
-                if j < on_vector:
-                    nc.vector.tensor_tensor(margin[:, j, :], banks[j][:], y_b[:, j, :], MULT)
-                else:
-                    nc.scalar.activation(margin[:, j, :], banks[j][:], COPY)
-
-            def times_y(j):
-                if j >= on_vector:
-                    nc.gpsimd.tensor_tensor(margin[:, j, :], margin[:, j, :], y_b[:, j, :], MULT)
-
-            def sigmoid(j):
-                nc.scalar.activation(margin[:, j, :], margin[:, j, :], SIGMOID, scale=-1.0)
-
-            def times_weight(j):
-                for cols in halves if j == PACK - 1 else [slice(0, N)]:
-                    nc.gpsimd.tensor_tensor(margin[:, j, cols], margin[:, j, cols], weight[:, j, cols], MULT)
-
-            stages = [leave_bank, times_y, sigmoid, times_weight]
-            for tick in range(PACK + len(stages) - 1):
-                for s in reversed(range(len(stages))):
-                    if 0 <= tick - s < PACK:
-                        stages[s](tick - s)
-            for cols in halves:
-                round_on_scalar(moving_views(rounded[:, cols.start * PACK : cols.stop * PACK], margin[:, :, cols]))
-            return rounded
-
-        def table_gradient(b, xm_q, g_q):
+        def products(name, stationary, moving):
             banks = []
             for t in range(PACK):
-                bank = psum.tile([P, N], F32, name="dw%d%d" % (b, t), tag="dw%d" % t)
-                product(bank[:], xm_q, t, g_q, slice(0, N))
+                rows = slice(t * P, (t + 1) * P)
+                bank = psum.tile([P, N], F32, name="%s%d" % (name, t), tag="%s%d" % (name[:-1], t))
+                nc.tensor.matmul_mx(
+                    out=bank[:],
+                    lhsT=stationary[0][:, rows].bitcast(stationary[2]),
+                    lhsT_scale=stationary[1][:, rows],
+                    rhs=moving[0][:].bitcast(moving[2]),
+                    rhs_scale=moving[1][:],
+                    start=True,
+                    stop=True,
+                )
                 banks.append(bank)
             return banks
 
-        def gather_m(b, t, slot=None):
-            momentum[b, t] = new("m_got%d%d" % (b, t), [P, N], F32, slot)[:]
-            nc.vector.tensor_copy(momentum[b, t], listed(m_in[t], b))
+        def gather_w(b, t):
+            nc.vector.tensor_copy(w_got[:, t, b * N : (b + 1) * N], listed(w_in[t], b))
 
-        def decay(b, t, kept):
-            nc.scalar.activation(kept, momentum[b, t], COPY, scale=BETA)
+        def gather_m(b, t, dest=None, factor=BETA):
+            momentum[b, t] = new("m_got%d%d" % (b, t), [P, N], F32)[:] if dest is None else dest
+            nc.vector.tensor_scalar(momentum[b, t], listed(m_in[t], b), factor, 0.0, MULT, ADD)
 
-        def update_m(b, t, bank, kept, grad=None, dest=None):
-            new_m = momentum[b, t] if dest is None else dest
-            momentum[b, t] = new_m
+        def round_gradient(rounded, margin):
+            for cols in halves:
+                round_on_scalar(moving_views(rounded[:, cols.start * PACK : cols.stop * PACK], margin[:, :, cols]))
+
+        def gradient_on_vector(banks, y_b):
+            rounded = new("g_rounded0", [P, PACK * N], BF16)
+            margin = new("margin0", [P, PACK, N], F32)
+            for j in range(PACK):
+                nc.vector.tensor_tensor(margin[:, j, :], banks[j][:], y_b[:, j, :], MULT)
+                nc.scalar.activation(margin[:, j, :], margin[:, j, :], SIGMOID, scale=-1.0)
+            for j in range(PACK):
+                nc.vector.scalar_tensor_tensor(margin[:, j, :], margin[:, j, :], neg_wt[:, 0, j : j + 1], y_b[:, j, :], MULT, MULT)
+            xm_rounded = new("xm_rounded0", [P, PACK * D], BF16)
+            round_on_scalar(stationary_views(xm_rounded[:], xm0[:]))
+            round_gradient(rounded, margin)
+            return rounded, xm_rounded
+
+        def gradient_on_gpsimd(banks, y_b, slot, weight_slot):
+            rounded = new("g_rounded1", [P, PACK * N], BF16)
+            margin = new("margin1", [P, PACK, N], F32, slot)
+            weight = new("weight1", [P, PACK, N], F32, weight_slot)
+
+            for j in range(PACK):
+                nc.scalar.activation(margin[:, j, :], banks[j][:], COPY)
+                nc.gpsimd.tensor_tensor(margin[:, j, :], margin[:, j, :], y_b[:, j, :], MULT)
+            for j in range(PACK):
+                nc.scalar.activation(weight[:, j, :], y_b[:, j, :], COPY, scale=neg_wt[:, 1, j : j + 1])
+                nc.scalar.activation(margin[:, j, :], margin[:, j, :], SIGMOID, scale=-1.0)
+            xm_rounded = new("xm_rounded1", [P, PACK * D], BF16, "w1")
+            round_on_scalar(stationary_views(xm_rounded[:], xm1[:]))
+            for j in range(PACK):
+                for cols in halves if j == PACK - 1 else [slice(0, N)]:
+                    nc.gpsimd.tensor_tensor(margin[:, j, cols], margin[:, j, cols], weight[:, j, cols], MULT)
+            round_gradient(rounded, margin)
+            return rounded, xm_rounded
+
+        def update_m(b, t, bank, grad=None):
             if grad is None:
                 grad = new("grad%d%d" % (b, t), [P, N], F32, "grad%d" % t)[:]
             nc.scalar.activation(grad, bank[:], COPY)
-            nc.gpsimd.tensor_tensor(new_m, kept, grad, ADD)
+            nc.gpsimd.tensor_tensor(momentum[b, t], momentum[b, t], grad, ADD)
 
-        def update_w(b, t, change):
+        def update_w(b, t, dest=None, change=None):
+            if change is None:
+                change = new("change%d%d" % (b, t), [P, N], F32, "grad%d" % t)[:]
             nc.scalar.activation(change, momentum[b, t], COPY, scale=-LR)
-            new_w = w_got[:, t, b * N : (b + 1) * N]
-            nc.gpsimd.tensor_tensor(new_w, new_w, change, ADD)
+            old = w_got[:, t, b * N : (b + 1) * N]
+            new_w[b, t] = old if dest is None else dest
+            nc.gpsimd.tensor_tensor(new_w[b, t], old, change, ADD)
 
         def scatter_w(b, t):
-            nc.vector.tensor_copy(listed(w_out[t], b), w_got[:, t, b * N : (b + 1) * N])
+            nc.vector.tensor_copy(listed(w_out[t], b), new_w[b, t])
 
         def scatter_m(b, t):
             nc.vector.tensor_copy(listed(m_out[t], b), momentum[b, t])
 
-        halves = [slice(0, N // 2), slice(N // 2, N)]
-        momentum, w_out, m_out, m_in = {}, {}, {}, {}
+        halves = [slice(0, HALF), slice(HALF, N)]
+        momentum, new_w, w_out, m_out, m_in = {}, {}, {}, {}, {}
         w_got = new("w_got", [P, PACK, B * N], F32)
         w_in = [load_plane("w%d" % t, wT, t) for t in range(PACK)]
         x0 = load_rows("x0", xT[0])
@@ -191,7 +178,7 @@ def tile_attend_gsig_mom_kernel(tc, xT, wT, y, wt, xm, mT, offs, out_0, out_1):
 
         for t in range(PACK):
             for b in range(B):
-                nc.vector.tensor_copy(w_got[:, t, b * N : (b + 1) * N], listed(w_in[t], b))
+                gather_w(b, t)
         for t in range(PACK - 1):
             w_out[t] = new("w_out%d" % t, [P, T], F32)
             nc.scalar.activation(w_out[t][:], w_in[t][:], COPY)
@@ -199,88 +186,71 @@ def tile_attend_gsig_mom_kernel(tc, xT, wT, y, wt, xm, mT, offs, out_0, out_1):
         w_rounded = new("w_rounded0", [P, PACK * N], BF16)
         round_on_vector(moving_views(w_rounded[:], w_got[:, :, 0:N]))
         w_q = quantize("w0", w_rounded, E4M3)
-        x_rounded = new("x_rounded0", [P, PACK * R], BF16, "x_rounded")
+        x_rounded = new("x_rounded0", [P, PACK * R], BF16)
         round_on_scalar(stationary_views(x_rounded[:], x0[:]))
         x_q = quantize("x0", x_rounded, E4M3)
-        banks = scores(0, x_q, w_q)
-        gather_m(0, 0, "x_rounded")
-        gather_m(1, 0, "w_rounded0")
-        w1_rounded = new("w_rounded1", [P, PACK * N], BF16, "x0")
-        round_on_scalar(moving_views(w1_rounded[:], w_got[:, :, N : 2 * N]))
+        banks = products("score0", x_q, w_q)
+        gather_m(0, 0, new("drift", [P, N], F32)[:], -LR * BETA)
+        early = new("early", [P, N], F32)
+        nc.gpsimd.tensor_tensor(early[:], w_got[:, 0, 0:N], momentum[0, 0], ADD)
+        w_rounded = new("w_rounded1", [P, PACK * N], BF16, "x0")
+        round_on_scalar(moving_views(w_rounded[:], w_got[:, :, N : 2 * N]))
         neg_wt = new("neg_wt", [P, B, PACK], F32)
         nc.scalar.activation(neg_wt[:], wt_in[:], COPY, scale=-1.0)
-        drift = new("drift", [P, N], F32)
-        nc.scalar.activation(drift[:], momentum[0, 0], COPY, scale=-LR * BETA)
-        kept = new("kept00", [P, N], F32)
-        decay(0, 0, kept[:])
-        weight = row_weights(0, y0, "weight")
-        xm_rounded = new("xm_rounded0", [P, PACK * D], BF16)
-        round_on_scalar(stationary_views(xm_rounded[:], xm0[:]))
-        g_rounded = gradient(0, banks, y0, weight, MARGINS_ON_VECTOR)
-        early = new("early", [P, 3, N], F32, "weight")
-        nc.gpsimd.tensor_tensor(early[:, 0, :], w_got[:, 0, 0:N], drift[:], ADD)
-        for t in (1, 2):
-            for b in range(B):
-                gather_m(b, t)
-        xm_q = quantize("xm0", xm_rounded, E4M3, "m2")
-        g_q = quantize("g0", g_rounded, E5M2, "xm_rounded0")
-        banks = table_gradient(0, xm_q, g_q)
-        w_q = quantize("w1", w1_rounded, E4M3, "g_rounded0")
-        gather_m(0, 3, "x0")
-        gather_m(1, 3)
+        g_rounded, xm_rounded = gradient_on_vector(banks, y0)
+        xm_q = quantize("xm0", xm_rounded, E4M3)
+        for b in range(B):
+            gather_m(b, 1)
+        gather_m(1, 0, new("m_got10", [P, N], F32, "xm0")[:])
+        w_q = quantize("w1", w_rounded, E4M3, "xm_rounded0")
+        g_q = quantize("g0", g_rounded, E5M2)
+        banks = products("dw0", xm_q, g_q)
 
         x1 = load_rows("x1", xT[1], "w0")
-        y1 = load_rows("y1", y[1], "w2")
-        xm1 = load_rows("xm1", xm[1], "w3")
-        for t, slot in ((1, "w1"), (2, "m0"), (0, "y0"), (3, "xm0")):
+        y1 = load_rows("y1", y[1], "w1")
+        xm1 = load_rows("xm1", xm[1], "w2")
+        for t, slot in ((1, "w3"), (2, "y0"), (0, "m0"), (3, "x0")):
             m_out[t] = load_plane("m_out%d" % t, mT, t, slot)
-        w_out[3] = load_plane("w_out3", wT, 3, "m1")
+        w_out[3] = load_plane("w_out3", wT, 3, "m3")
 
-        for t in (1, 2):
-            decay(0, t, early[:, t, :])
-        change = new("change_grad", [P, N], F32)
+        late = new("m_got_late", [P, 2, B, N], F32, "margin0")
+        for t in (2, 3):
+            for b in range(B):
+                gather_m(b, t, late[:, t - 2, b, :])
+
+        change = new("change00", [P, N], F32, "grad0")
         nc.scalar.activation(change[:], banks[0][:], COPY, scale=-LR)
-        nc.gpsimd.tensor_tensor(w_got[:, 0, 0:N], early[:, 0, :], change[:], ADD)
+        new_w[0, 0] = w_got[:, 0, 0:N]
+        nc.gpsimd.tensor_tensor(new_w[0, 0], early[:], change[:], ADD)
         scatter_w(0, 0)
-        update_m(0, 1, banks[1], early[:, 1, :])
-        update_w(0, 1, new("change01", [P, N], F32, "drift")[:])
-        update_m(0, 2, banks[2], early[:, 2, :])
-        update_m(0, 0, banks[0], kept[:], dest=new("new_m00", [P, N], F32, "drift")[:])
-        scatter_w(0, 1)
-        dw_banks = banks
+        update_m(0, 1, banks[1])
+        update_m(0, 2, banks[2])
         x_rounded = new("x_rounded1", [P, PACK * R], BF16)
         round_on_scalar(stationary_views(x_rounded[:], x1[:]))
+        update_w(0, 1, change=new("change01", [P, N], F32, "w0")[:])
         x_q = quantize("x1", x_rounded, E4M3)
-        banks = scores(1, x_q, w_q)
-        staged = new("staged0", [P, 3, N], F32, "w0")
-        update_w(0, 2, staged[:, 2, :])
-        decay(0, 3, staged[:, 0, :])
-        decay(1, 0, staged[:, 1, :])
-        weight = row_weights(1, y1, "weight")
+        scatter_w(0, 1)
+        staged = new("staged", [P, 3, N], F32, "x_rounded1")
+        update_w(0, 2, change=staged[:, 0, :])
         scatter_w(0, 2)
-        update_m(0, 3, dw_banks[3], staged[:, 0, :], new("grad03", [P, N], F32, "neg_wt")[:])
-        g_rounded = gradient(1, banks, y1, weight, 0)
-        xm_rounded = new("xm_rounded1", [P, PACK * D], BF16)
-        round_on_scalar(stationary_views(xm_rounded[:], xm1[:]))
+        nc.gpsimd.tensor_tensor(staged[:, 1, :], momentum[0, 0], change[:], ADD)
+        nc.scalar.activation(momentum[0, 0], staged[:, 1, :], COPY, scale=-1.0 / LR)
+        update_m(0, 3, banks[3], staged[:, 2, :])
+        banks = products("score1", x_q, w_q)
+        g_rounded, xm_rounded = gradient_on_gpsimd(banks, y1, "m1", "m2")
         for t in (1, 2, 0, 3):
             scatter_m(0, t)
-        change = new("change03", [P, N], F32, "change_grad")
-        nc.scalar.activation(change[:], momentum[0, 3], COPY, scale=-LR)
-        xm_q = quantize("xm1", xm_rounded, E4M3, "x0")
-        g_q = quantize("g1", g_rounded, E5M2, "xm_rounded1")
-        banks = table_gradient(1, xm_q, g_q)
-        late = new("late", [P, PACK + 1, N], F32, "margin")
-        nc.gpsimd.tensor_tensor(late[:, PACK, :], w_got[:, 3, 0:N], change[:], ADD)
-        nc.vector.tensor_copy(listed(w_out[3], 0), late[:, PACK, :])
-        for t in range(1, PACK):
-            decay(1, t, late[:, t, :])
-        changes = new("changes1", [P, PACK, N], F32, "w2")
+        xm_q = quantize("xm1", xm_rounded, E4M3, "m2")
+        g_q = quantize("g1", g_rounded, E5M2)
+        banks = products("dw1", xm_q, g_q)
+        update_w(0, 3, new("new_w03", [P, N], F32, "m1")[:])
+        scatter_w(0, 3)
         for t in range(PACK + 1):
             if t < PACK:
-                update_m(1, t, banks[t], late[:, t, :] if t else staged[:, 1, :])
+                update_m(1, t, banks[t])
                 scatter_m(1, t)
                 nc.sync.dma_start(planes(out_1)[t], m_out[t][:])
             if t > 0:
-                update_w(1, t - 1, changes[:, t - 1, :])
+                update_w(1, t - 1)
                 scatter_w(1, t - 1)
                 nc.sync.dma_start(planes(out_0)[t - 1], w_out[t - 1][:])

@@ -230,12 +230,12 @@ def tile_attend_gsig_mom_kernel(tc, xT, wT, y, wt, xm, mT, offs, out_0, out_1):
         update_w(0, 1, change=new("change01", [P, N], F32, "w0")[:])
         x_q = quantize("x1", x_rounded, E4M3)
         scatter_w(0, 1)
-        staged = new("staged", [P, 3, N], F32, "x_rounded1")
+        staged = new("staged", [P, 2, N], F32, "x_rounded1")
         update_w(0, 2, change=staged[:, 0, :])
         scatter_w(0, 2)
-        nc.gpsimd.tensor_tensor(staged[:, 1, :], momentum[0, 0], change[:], ADD)
-        nc.scalar.activation(momentum[0, 0], staged[:, 1, :], COPY, scale=-1.0 / LR)
-        update_m(0, 3, banks[3], staged[:, 2, :])
+        nc.gpsimd.tensor_tensor(staged[:, 0, :], momentum[0, 0], change[:], ADD)
+        nc.scalar.activation(momentum[0, 0], staged[:, 0, :], COPY, scale=-1.0 / LR)
+        update_m(0, 3, banks[3], staged[:, 1, :])
         banks = products("score1", x_q, w_q)
         g_rounded, xm_rounded = gradient_on_gpsimd(banks, y1, "m1", "m2")
         for t in (1, 2, 0, 3):

@@ -1,6 +1,7 @@
 from contextlib import ExitStack
 
 import concourse.mybir as mybir
+from concourse.masks import make_identity
 
 B, N, T, D, R = 2, 512, 2048, 512, 512
 LR = 0.1
@@ -58,6 +59,8 @@ def tile_attend_gsig_mom_kernel(tc, xT, wT, y, wt, xm, mT, offs, out_0, out_1):
         def load_rows(name, matrix, slot=None):
             return load(name, rows4(matrix), [P, PACK, 512], slot)
 
+        ident = new("ident", [P, P], F32)
+        make_identity(nc, ident[:])
         warm = new("warm", [P, 8], F32)
         nc.vector.memset(warm[:], 0.0)
         nc.scalar.activation(warm[:], warm[:], SIGMOID)
@@ -124,47 +127,30 @@ def tile_attend_gsig_mom_kernel(tc, xT, wT, y, wt, xm, mT, offs, out_0, out_1):
             round_gradient(rounded, margin)
             return rounded, xm_rounded
 
-        def gradient_on_gpsimd(banks, y_b, slot, weight_slot):
-            rounded = new("g_rounded1", [P, PACK * N], BF16)
-            margin = new("margin1", [P, PACK, N], F32, slot)
-            weight = new("weight1", [P, PACK, N], F32, weight_slot)
+        def turned(tag, *terms):
+            bank = psum.tile([P, N], F32, name="turned", tag=tag)
+            for s in range(N // P):
+                cols = slice(s * P, (s + 1) * P)
+                for k, term in enumerate(terms):
+                    nc.tensor.matmul(bank[:, cols], term[:, cols], ident[:], start=k == 0, stop=k == len(terms) - 1, is_transpose=True)
+            return bank
 
-            for j in range(PACK):
-                nc.scalar.activation(margin[:, j, :], banks[j][:], COPY)
-                nc.gpsimd.tensor_tensor(margin[:, j, :], margin[:, j, :], y_b[:, j, :], MULT)
-            for j in range(PACK):
-                nc.scalar.activation(weight[:, j, :], y_b[:, j, :], COPY, scale=neg_wt[:, 1, j : j + 1])
-                nc.scalar.activation(margin[:, j, :], margin[:, j, :], SIGMOID, scale=-1.0)
-            xm_rounded = new("xm_rounded1", [P, PACK * D], BF16, "w1")
-            round_on_scalar(stationary_views(xm_rounded[:], xm1[:]))
-            for j in range(PACK):
-                for cols in halves if j == PACK - 1 else [slice(0, N)]:
-                    nc.gpsimd.tensor_tensor(margin[:, j, cols], margin[:, j, cols], weight[:, j, cols], MULT)
-            round_gradient(rounded, margin)
-            return rounded, xm_rounded
+        def leave(name, bank, scale, slot=None):
+            dest = new(name, [P, N], F32, slot)
+            nc.scalar.activation(dest[:], bank[:], COPY, scale=scale)
+            return dest[:]
 
-        def update_m(b, t, bank, grad=None):
-            if grad is None:
-                grad = new("grad%d%d" % (b, t), [P, N], F32, "grad%d" % t)[:]
-            nc.scalar.activation(grad, bank[:], COPY)
-            nc.gpsimd.tensor_tensor(momentum[b, t], momentum[b, t], grad, ADD)
+        def old_w(b, t):
+            return w_got[:, t, b * N : (b + 1) * N]
 
-        def update_w(b, t, dest=None, change=None):
-            if change is None:
-                change = new("change%d%d" % (b, t), [P, N], F32, "grad%d" % t)[:]
-            nc.scalar.activation(change, momentum[b, t], COPY, scale=-LR)
-            old = w_got[:, t, b * N : (b + 1) * N]
-            new_w[b, t] = old if dest is None else dest
-            nc.gpsimd.tensor_tensor(new_w[b, t], old, change, ADD)
-
-        def scatter_w(b, t):
-            nc.vector.tensor_copy(listed(w_out[t], b), new_w[b, t])
-
-        def scatter_m(b, t):
-            nc.vector.tensor_copy(listed(m_out[t], b), momentum[b, t])
+        def scatter(window, b, values, more=None):
+            if more is None:
+                nc.vector.tensor_copy(listed(window, b), values)
+            else:
+                nc.vector.tensor_tensor(listed(window, b), values, more, ADD)
 
         halves = [slice(0, HALF), slice(HALF, N)]
-        momentum, new_w, w_out, m_out, m_in = {}, {}, {}, {}, {}
+        momentum, w_turned, w_out, m_out, m_in = {}, {}, {}, {}, {}
         w_got = new("w_got", [P, PACK, B * N], F32)
         w_in = [load_plane("w%d" % t, wT, t) for t in range(PACK)]
         x0 = load_rows("x0", xT[0])
@@ -173,8 +159,7 @@ def tile_attend_gsig_mom_kernel(tc, xT, wT, y, wt, xm, mT, offs, out_0, out_1):
         m_in[0] = load_plane("m0", mT, 0)
         y0 = load_rows("y0", y[0])
         xm0 = load_rows("xm0", xm[0])
-        for t in range(1, PACK):
-            m_in[t] = load_plane("m%d" % t, mT, t)
+        m_in[1] = load_plane("m1", mT, 1)
 
         for t in range(PACK):
             for b in range(B):
@@ -182,6 +167,7 @@ def tile_attend_gsig_mom_kernel(tc, xT, wT, y, wt, xm, mT, offs, out_0, out_1):
         for t in range(PACK - 1):
             w_out[t] = new("w_out%d" % t, [P, T], F32)
             nc.scalar.activation(w_out[t][:], w_in[t][:], COPY)
+        w_turned[1] = leave("w_turned1", turned("dw1", old_w(0, 1)), 1.0)
 
         w_rounded = new("w_rounded0", [P, PACK * N], BF16)
         round_on_vector(moving_views(w_rounded[:], w_got[:, :, 0:N]))
@@ -198,6 +184,7 @@ def tile_attend_gsig_mom_kernel(tc, xT, wT, y, wt, xm, mT, offs, out_0, out_1):
         neg_wt = new("neg_wt", [P, B, PACK], F32)
         nc.scalar.activation(neg_wt[:], wt_in[:], COPY, scale=-1.0)
         g_rounded, xm_rounded = gradient_on_vector(banks, y0)
+        w_turned[2] = leave("w_turned2", turned("score3", old_w(0, 2)), 1.0)
         xm_q = quantize("xm0", xm_rounded, E4M3)
         for b in range(B):
             gather_m(b, 1)
@@ -207,50 +194,77 @@ def tile_attend_gsig_mom_kernel(tc, xT, wT, y, wt, xm, mT, offs, out_0, out_1):
         banks = products("dw0", xm_q, g_q)
 
         x1 = load_rows("x1", xT[1], "w0")
+        for t in (2, 3):
+            m_in[t] = load_plane("m%d" % t, mT, t)
         y1 = load_rows("y1", y[1], "w1")
         xm1 = load_rows("xm1", xm[1], "w2")
-        for t, slot in ((1, "w3"), (2, "y0"), (0, "m0"), (3, "x0")):
+        for t, slot in enumerate(("w3", "y0", "m0", "x0")):
             m_out[t] = load_plane("m_out%d" % t, mT, t, slot)
         w_out[3] = load_plane("w_out3", wT, 3, "m3")
 
-        late = new("m_got_late", [P, 2, B, N], F32, "margin0")
-        for t in (2, 3):
-            for b in range(B):
-                gather_m(b, t, late[:, t - 2, b, :])
-
-        change = new("change00", [P, N], F32, "grad0")
-        nc.scalar.activation(change[:], banks[0][:], COPY, scale=-LR)
-        new_w[0, 0] = w_got[:, 0, 0:N]
-        nc.gpsimd.tensor_tensor(new_w[0, 0], early[:], change[:], ADD)
-        scatter_w(0, 0)
-        update_m(0, 1, banks[1])
-        update_m(0, 2, banks[2])
         x_rounded = new("x_rounded1", [P, PACK * R], BF16)
         round_on_scalar(stationary_views(x_rounded[:], x1[:]))
-        update_w(0, 1, change=new("change01", [P, N], F32, "w0")[:])
+        late = new("m_got_late", [P, 2, B, N], F32, "margin0")
+        for b in range(B):
+            gather_m(b, 2, late[:, 0, b, :])
         x_q = quantize("x1", x_rounded, E4M3)
-        scatter_w(0, 1)
-        staged = new("staged", [P, 2, N], F32, "x_rounded1")
-        update_w(0, 2, change=staged[:, 0, :])
-        scatter_w(0, 2)
-        nc.gpsimd.tensor_tensor(staged[:, 0, :], momentum[0, 0], change[:], ADD)
-        nc.scalar.activation(momentum[0, 0], staged[:, 0, :], COPY, scale=-1.0 / LR)
-        update_m(0, 3, banks[3], staged[:, 1, :])
+        grad = {0: leave("grad00", banks[0], -LR, "grad0")}
+        scatter(w_out[0], 0, early[:], grad[0])
+        for t in range(1, PACK):
+            grad[t] = leave("grad0%d" % t, banks[t], 1.0, "grad%d" % t)
+        for b in range(B):
+            gather_m(b, 3, late[:, 1, b, :])
+
+        step = {}
+
+        def sum_step(t):
+            step[t] = leave("step0%d" % t, turned("dw%d" % t if t else "score0", momentum[0, t], grad[t]), -LR if t else 1.0, "step%d" % t)
+
+        def put_w(t):
+            scatter(w_out[t], 0, leave("new_w0%d" % t, turned("dw%d" % t, step[t], w_turned[t]), 1.0, "grad%d" % t))
+
+        def put_m(t):
+            bank = turned("dw%d" % t, step[t])
+            nc.scalar.activation(momentum[0, t], bank[:], COPY, scale=-1.0 / LR)
+            scatter(m_out[t], 0, momentum[0, t])
+            return bank
+
+        sum_step(1)
+        sum_step(2)
+        put_w(1)
         banks = products("score1", x_q, w_q)
-        g_rounded, xm_rounded = gradient_on_gpsimd(banks, y1, "m1", "m2")
-        for t in (1, 2, 0, 3):
-            scatter_m(0, t)
+        g_rounded = new("g_rounded1", [P, PACK * N], BF16)
+        margin = new("margin1", [P, PACK, N], F32, "m1")
+        weight = new("weight1", [P, PACK, N], F32, "m2")
+        for j in range(PACK):
+            nc.scalar.activation(margin[:, j, :], banks[j][:], COPY)
+            nc.gpsimd.tensor_tensor(margin[:, j, :], margin[:, j, :], y1[:, j, :], MULT)
+        put_w(2)
+        sum_step(0)
+        put_m(0)
+        put_m(1)
+        for j in range(PACK):
+            nc.scalar.activation(weight[:, j, :], y1[:, j, :], COPY, scale=neg_wt[:, 1, j : j + 1])
+            nc.scalar.activation(margin[:, j, :], margin[:, j, :], SIGMOID, scale=-1.0)
+        sum_step(3)
+        xm_rounded = new("xm_rounded1", [P, PACK * D], BF16, "w1")
+        round_on_scalar(stationary_views(xm_rounded[:], xm1[:]))
+        put_m(2)
+        bank = put_m(3)
+        for j in range(PACK):
+            for cols in halves if j == PACK - 1 else [slice(0, N)]:
+                nc.gpsimd.tensor_tensor(margin[:, j, cols], margin[:, j, cols], weight[:, j, cols], MULT)
+        round_gradient(g_rounded, margin)
         xm_q = quantize("xm1", xm_rounded, E4M3, "m2")
         g_q = quantize("g1", g_rounded, E5M2)
+        scatter(w_out[3], 0, old_w(0, 3), leave("change03", bank, 1.0, "m1"))
         banks = products("dw1", xm_q, g_q)
-        update_w(0, 3, new("new_w03", [P, N], F32, "m1")[:])
-        scatter_w(0, 3)
-        for t in range(PACK + 1):
-            if t < PACK:
-                update_m(1, t, banks[t])
-                scatter_m(1, t)
-                nc.sync.dma_start(planes(out_1)[t], m_out[t][:])
-            if t > 0:
-                update_w(1, t - 1)
-                scatter_w(1, t - 1)
-                nc.sync.dma_start(planes(out_0)[t - 1], w_out[t - 1][:])
+        for t in range(PACK):
+            grad[t] = leave("grad1%d" % t, banks[t], 1.0, "grad%d" % t)
+            scatter(m_out[t], 1, momentum[1, t], grad[t])
+            nc.sync.dma_start(planes(out_1)[t], m_out[t][:])
+        for t in range(PACK):
+            step[t] = leave("step1%d" % t, turned("score%d" % t, momentum[1, t], grad[t]), -LR, "step%d" % t)
+        for t in range(PACK):
+            scatter(w_out[t], 1, old_w(1, t), leave("change1%d" % t, turned("score%d" % t, step[t]), 1.0, "change%d" % t))
+            nc.sync.dma_start(planes(out_0)[t], w_out[t][:])

@@ -106,9 +106,9 @@ def tile_attend_gsig_mom_kernel(tc, xT, wT, y, wt, xm, mT, offs, out_0, out_1):
         def gather_w(b, t):
             nc.vector.tensor_copy(w_got[:, t, b * N : (b + 1) * N], listed(w_in[t], b))
 
-        def gather_m(b, t, dest=None, factor=BETA):
+        def gather_m(b, t, dest=None):
             momentum[b, t] = new("m_got%d%d" % (b, t), [P, N], F32)[:] if dest is None else dest
-            nc.vector.tensor_scalar(momentum[b, t], listed(m_in[t], b), factor, 0.0, MULT, ADD)
+            nc.vector.tensor_copy(momentum[b, t], listed(m_in[t], b))
 
         def round_gradient(rounded, margin):
             for cols in halves:
@@ -176,14 +176,16 @@ def tile_attend_gsig_mom_kernel(tc, xT, wT, y, wt, xm, mT, offs, out_0, out_1):
         round_on_scalar(stationary_views(x_rounded[:], x0[:]))
         x_q = quantize("x0", x_rounded, E4M3)
         banks = products("score0", x_q, w_q)
-        gather_m(0, 0, new("drift", [P, N], F32)[:], -LR * BETA)
-        early = new("early", [P, N], F32)
-        nc.gpsimd.tensor_tensor(early[:], w_got[:, 0, 0:N], momentum[0, 0], ADD)
+        gather_m(0, 0)
+        drift = momentum[0, 0]
+        nc.gpsimd.tensor_scalar(drift, drift, -LR * BETA, 0.0, MULT, ADD)
         w_rounded = new("w_rounded1", [P, PACK * N], BF16, "x0")
         round_on_scalar(moving_views(w_rounded[:], w_got[:, :, N : 2 * N]))
         neg_wt = new("neg_wt", [P, B, PACK], F32)
         nc.scalar.activation(neg_wt[:], wt_in[:], COPY, scale=-1.0)
         g_rounded, xm_rounded = gradient_on_vector(banks, y0)
+        early = new("early", [P, N], F32, "y0")
+        nc.gpsimd.tensor_tensor(early[:], old_w(0, 0), drift, ADD)
         w_turned[2] = leave("w_turned2", turned("score3", old_w(0, 2)), 1.0)
         xm_q = quantize("xm0", xm_rounded, E4M3)
         for b in range(B):
@@ -197,9 +199,9 @@ def tile_attend_gsig_mom_kernel(tc, xT, wT, y, wt, xm, mT, offs, out_0, out_1):
         for t in (2, 3):
             m_in[t] = load_plane("m%d" % t, mT, t)
         y1 = load_rows("y1", y[1], "w1")
-        xm1 = load_rows("xm1", xm[1], "w2")
-        for t, slot in enumerate(("w3", "y0", "m0", "x0")):
+        for t, slot in enumerate(("w3", None, "m0", "x0")):
             m_out[t] = load_plane("m_out%d" % t, mT, t, slot)
+        xm1 = load_rows("xm1", xm[1], "w2")
         w_out[3] = load_plane("w_out3", wT, 3, "m3")
 
         x_rounded = new("x_rounded1", [P, PACK * R], BF16)
@@ -210,23 +212,23 @@ def tile_attend_gsig_mom_kernel(tc, xT, wT, y, wt, xm, mT, offs, out_0, out_1):
         x_q = quantize("x1", x_rounded, E4M3)
         grad = {0: leave("grad00", banks[0], -LR, "grad0")}
         scatter(w_out[0], 0, early[:], grad[0])
+        nc.gpsimd.tensor_tensor(early[:], drift, grad[0], ADD)
         for t in range(1, PACK):
-            grad[t] = leave("grad0%d" % t, banks[t], 1.0, "grad%d" % t)
+            grad[t] = leave("grad0%d" % t, banks[t], 1.0 / BETA, "grad%d" % t)
         for b in range(B):
             gather_m(b, 3, late[:, 1, b, :])
 
         step = {}
 
         def sum_step(t):
-            step[t] = leave("step0%d" % t, turned("dw%d" % t if t else "score0", momentum[0, t], grad[t]), -LR if t else 1.0, "step%d" % t)
+            step[t] = leave("step0%d" % t, turned("dw%d" % t, momentum[0, t], grad[t]), -LR * BETA, "step%d" % t)
 
         def put_w(t):
             scatter(w_out[t], 0, leave("new_w0%d" % t, turned("dw%d" % t, step[t], w_turned[t]), 1.0, "grad%d" % t))
 
         def put_m(t):
             bank = turned("dw%d" % t, step[t])
-            nc.scalar.activation(momentum[0, t], bank[:], COPY, scale=-1.0 / LR)
-            scatter(m_out[t], 0, momentum[0, t])
+            scatter(m_out[t], 0, leave("new_m0%d" % t, bank, -1.0 / LR))
             return bank
 
         sum_step(1)
@@ -240,31 +242,33 @@ def tile_attend_gsig_mom_kernel(tc, xT, wT, y, wt, xm, mT, offs, out_0, out_1):
             nc.scalar.activation(margin[:, j, :], banks[j][:], COPY)
             nc.gpsimd.tensor_tensor(margin[:, j, :], margin[:, j, :], y1[:, j, :], MULT)
         put_w(2)
-        sum_step(0)
-        put_m(0)
+        scatter(m_out[0], 0, leave("new_m00", early, -1.0 / LR, "w_turned2"))
         put_m(1)
         for j in range(PACK):
             nc.scalar.activation(weight[:, j, :], y1[:, j, :], COPY, scale=neg_wt[:, 1, j : j + 1])
             nc.scalar.activation(margin[:, j, :], margin[:, j, :], SIGMOID, scale=-1.0)
         sum_step(3)
-        xm_rounded = new("xm_rounded1", [P, PACK * D], BF16, "w1")
-        round_on_scalar(stationary_views(xm_rounded[:], xm1[:]))
         put_m(2)
         bank = put_m(3)
         for j in range(PACK):
             for cols in halves if j == PACK - 1 else [slice(0, N)]:
                 nc.gpsimd.tensor_tensor(margin[:, j, cols], margin[:, j, cols], weight[:, j, cols], MULT)
         round_gradient(g_rounded, margin)
-        xm_q = quantize("xm1", xm_rounded, E4M3, "m2")
-        g_q = quantize("g1", g_rounded, E5M2)
-        scatter(w_out[3], 0, old_w(0, 3), leave("change03", bank, 1.0, "m1"))
+        g_q = quantize("g1", g_rounded, E5M2, "new_m02")
+        xm_rounded = new("xm_rounded1", [P, PACK * D], BF16)
+        round_on_scalar(stationary_views(xm_rounded[:], xm1[:]))
+        xm_q = quantize("xm1", xm_rounded, E4M3)
+        scatter(w_out[3], 0, old_w(0, 3), leave("change03", bank, 1.0, "w2"))
+        kept = new("kept", [P, PACK, N], F32, "m1")
+        for t in range(PACK):
+            nc.scalar.activation(kept[:, t, :], momentum[1, t], COPY, scale=BETA)
         banks = products("dw1", xm_q, g_q)
         for t in range(PACK):
             grad[t] = leave("grad1%d" % t, banks[t], 1.0, "grad%d" % t)
-            scatter(m_out[t], 1, momentum[1, t], grad[t])
+            scatter(m_out[t], 1, kept[:, t, :], grad[t])
             nc.sync.dma_start(planes(out_1)[t], m_out[t][:])
         for t in range(PACK):
-            step[t] = leave("step1%d" % t, turned("score%d" % t, momentum[1, t], grad[t]), -LR, "step%d" % t)
+            step[t] = leave("step1%d" % t, turned("score%d" % t, kept[:, t, :], grad[t]), -LR, "step%d" % t)
         for t in range(PACK):
             scatter(w_out[t], 1, old_w(1, t), leave("change1%d" % t, turned("score%d" % t, step[t]), 1.0, "change%d" % t))
             nc.sync.dma_start(planes(out_0)[t], w_out[t][:])

@@ -1,7 +1,6 @@
 from contextlib import ExitStack
 
 import concourse.mybir as mybir
-from concourse.masks import make_identity
 
 B, N, T, D, R = 2, 512, 2048, 512, 512
 LR = 0.1
@@ -22,8 +21,10 @@ SIGMOID = mybir.ActivationFunctionType.Sigmoid
 
 P = 128
 PACK = 4
-HALF = N // 2
-LIST_COLS = N // 16
+STRIPE = 16
+ALL = slice(0, B * N)
+GROUP = [slice(b * N, (b + 1) * N) for b in range(B)]
+PIECES = [slice(0, 384), slice(384, 768), slice(768, 1024)]
 
 
 def tile_attend_gsig_mom_kernel(tc, xT, wT, y, wt, xm, mT, offs, out_0, out_1):
@@ -39,14 +40,14 @@ def tile_attend_gsig_mom_kernel(tc, xT, wT, y, wt, xm, mT, offs, out_0, out_1):
         sbuf = ctx.enter_context(tc.tile_pool(name="sbuf", bufs=1))
         psum = ctx.enter_context(tc.psum_pool(name="psum", bufs=1))
 
-        offsets = sbuf.tile([P, B * LIST_COLS], U16, name="offsets")
+        offsets = sbuf.tile([P, B * N // STRIPE], U16, name="offsets")
         nc.sync.dma_start(offsets[:], offs)
 
         def new(name, shape, dtype, slot=None):
             return sbuf.tile(shape, dtype, name=name, tag=slot or name, align_bytes=64)
 
-        def listed(window, b):
-            return window[:].indirect(offsets[:, b * LIST_COLS : (b + 1) * LIST_COLS])
+        def listed(window, entries):
+            return window[:].indirect(offsets[:, entries.start // STRIPE : entries.stop // STRIPE])
 
         def load(name, source, shape, slot=None):
             dest = new(name, shape, F32, slot)
@@ -59,8 +60,6 @@ def tile_attend_gsig_mom_kernel(tc, xT, wT, y, wt, xm, mT, offs, out_0, out_1):
         def load_rows(name, matrix, slot=None):
             return load(name, rows4(matrix), [P, PACK, 512], slot)
 
-        ident = new("ident", [P, P], F32)
-        make_identity(nc, ident[:])
         warm = new("warm", [P, 8], F32)
         nc.vector.memset(warm[:], 0.0)
         nc.scalar.activation(warm[:], warm[:], SIGMOID)
@@ -74,11 +73,16 @@ def tile_attend_gsig_mom_kernel(tc, xT, wT, y, wt, xm, mT, offs, out_0, out_1):
                 raw.rearrange("p j (m t) -> p m j t", t=PACK),
             )
 
-        def round_on_scalar(views):
+        def on_scalar(views):
             nc.scalar.activation(views[0], views[1], COPY)
 
-        def round_on_vector(views):
+        def on_vector(views):
             nc.vector.tensor_copy(views[0], views[1])
+
+        def rounded(name, engine, views, source, slot=None):
+            dest = new(name + "_rounded", [P, PACK * 512], BF16, slot)
+            engine(views(dest[:], source))
+            return dest
 
         def quantize(name, source, fmt, slot=None):
             codes = new(name + "_codes", [P, 512], U32, slot)
@@ -86,11 +90,11 @@ def tile_attend_gsig_mom_kernel(tc, xT, wT, y, wt, xm, mT, offs, out_0, out_1):
             nc.vector.quantize_mx(out=codes[:].bitcast(fmt), scales=scales[:], in_=source[:])
             return codes, scales, fmt
 
-        def products(name, stationary, moving):
+        def products(name, b, stationary, moving):
             banks = []
             for t in range(PACK):
                 rows = slice(t * P, (t + 1) * P)
-                bank = psum.tile([P, N], F32, name="%s%d" % (name, t), tag="%s%d" % (name[:-1], t))
+                bank = psum.tile([P, N], F32, name="%s%d%d" % (name, b, t), tag="bank%d%d" % (b, t))
                 nc.tensor.matmul_mx(
                     out=bank[:],
                     lhsT=stationary[0][:, rows].bitcast(stationary[2]),
@@ -103,172 +107,60 @@ def tile_attend_gsig_mom_kernel(tc, xT, wT, y, wt, xm, mT, offs, out_0, out_1):
                 banks.append(bank)
             return banks
 
-        def gather_w(b, t):
-            nc.vector.tensor_copy(w_got[:, t, b * N : (b + 1) * N], listed(w_in[t], b))
-
-        def gather_m(b, t, dest=None):
-            momentum[b, t] = new("m_got%d%d" % (b, t), [P, N], F32)[:] if dest is None else dest
-            nc.vector.tensor_copy(momentum[b, t], listed(m_in[t], b))
-
-        def round_gradient(rounded, margin):
-            for cols in halves:
-                round_on_scalar(moving_views(rounded[:, cols.start * PACK : cols.stop * PACK], margin[:, :, cols]))
-
-        def gradient_on_vector(banks, y_b):
-            rounded = new("g_rounded0", [P, PACK * N], BF16)
-            margin = new("margin0", [P, PACK, N], F32)
-            for j in range(PACK):
-                nc.vector.tensor_tensor(margin[:, j, :], banks[j][:], y_b[:, j, :], MULT)
-                nc.scalar.activation(margin[:, j, :], margin[:, j, :], SIGMOID, scale=-1.0)
-            for j in range(PACK):
-                nc.vector.scalar_tensor_tensor(margin[:, j, :], margin[:, j, :], neg_wt[:, 0, j : j + 1], y_b[:, j, :], MULT, MULT)
-            xm_rounded = new("xm_rounded0", [P, PACK * D], BF16)
-            round_on_scalar(stationary_views(xm_rounded[:], xm0[:]))
-            round_gradient(rounded, margin)
-            return rounded, xm_rounded
-
-        def turned(tag, *terms):
-            bank = psum.tile([P, N], F32, name="turned", tag=tag)
-            for s in range(N // P):
-                cols = slice(s * P, (s + 1) * P)
-                for k, term in enumerate(terms):
-                    nc.tensor.matmul(bank[:, cols], term[:, cols], ident[:], start=k == 0, stop=k == len(terms) - 1, is_transpose=True)
-            return bank
-
-        def leave(name, bank, scale, slot=None):
-            dest = new(name, [P, N], F32, slot)
-            nc.scalar.activation(dest[:], bank[:], COPY, scale=scale)
-            return dest[:]
-
-        def old_w(b, t):
-            return w_got[:, t, b * N : (b + 1) * N]
-
-        def scatter(window, b, values, more=None):
-            if more is None:
-                nc.vector.tensor_copy(listed(window, b), values)
-            else:
-                nc.vector.tensor_tensor(listed(window, b), values, more, ADD)
-
-        halves = [slice(0, HALF), slice(HALF, N)]
-        momentum, w_turned, w_out, m_out, m_in = {}, {}, {}, {}, {}
         w_got = new("w_got", [P, PACK, B * N], F32)
         w_in = [load_plane("w%d" % t, wT, t) for t in range(PACK)]
         x0 = load_rows("x0", xT[0])
         wt_in = new("wt_in", [P, B, PACK], F32)
         nc.sync.dma_start(wt_in[:], wt.rearrange("b (p j) c -> p b (j c)", j=PACK))
-        m_in[0] = load_plane("m0", mT, 0)
         y0 = load_rows("y0", y[0])
+        x1 = load_rows("x1", xT[1])
         xm0 = load_rows("xm0", xm[0])
-        m_in[1] = load_plane("m1", mT, 1)
+        y1 = load_rows("y1", y[1])
+        xm1 = load_rows("xm1", xm[1])
 
+        w_out = []
         for t in range(PACK):
-            for b in range(B):
-                gather_w(b, t)
-        for t in range(PACK - 1):
-            w_out[t] = new("w_out%d" % t, [P, T], F32)
+            nc.vector.tensor_copy(w_got[:, t, :], listed(w_in[t], ALL))
+            w_out.append(new("w_out%d" % t, [P, T], F32))
             nc.scalar.activation(w_out[t][:], w_in[t][:], COPY)
-        w_turned[1] = leave("w_turned1", turned("dw1", old_w(0, 1)), 1.0)
-
-        w_rounded = new("w_rounded0", [P, PACK * N], BF16)
-        round_on_vector(moving_views(w_rounded[:], w_got[:, :, 0:N]))
-        w_q = quantize("w0", w_rounded, E4M3)
-        x_rounded = new("x_rounded0", [P, PACK * R], BF16)
-        round_on_scalar(stationary_views(x_rounded[:], x0[:]))
-        x_q = quantize("x0", x_rounded, E4M3)
-        banks = products("score0", x_q, w_q)
-        gather_m(0, 0)
-        drift = momentum[0, 0]
-        nc.gpsimd.tensor_scalar(drift, drift, -LR * BETA, 0.0, MULT, ADD)
-        w_rounded = new("w_rounded1", [P, PACK * N], BF16, "x0")
-        round_on_scalar(moving_views(w_rounded[:], w_got[:, :, N : 2 * N]))
+        m_in, m_out = [], []
+        for t in range(PACK):
+            m_in.append(load_plane("m%d" % t, mT, t, "w%d" % t))
+            m_out.append(load_plane("m_out%d" % t, mT, t))
         neg_wt = new("neg_wt", [P, B, PACK], F32)
         nc.scalar.activation(neg_wt[:], wt_in[:], COPY, scale=-1.0)
-        g_rounded, xm_rounded = gradient_on_vector(banks, y0)
-        early = new("early", [P, N], F32, "y0")
-        nc.gpsimd.tensor_tensor(early[:], old_w(0, 0), drift, ADD)
-        w_turned[2] = leave("w_turned2", turned("score3", old_w(0, 2)), 1.0)
-        xm_q = quantize("xm0", xm_rounded, E4M3)
-        for b in range(B):
-            gather_m(b, 1)
-        gather_m(1, 0, new("m_got10", [P, N], F32, "xm0")[:])
-        w_q = quantize("w1", w_rounded, E4M3, "xm_rounded0")
-        g_q = quantize("g0", g_rounded, E5M2)
-        banks = products("dw0", xm_q, g_q)
 
-        x1 = load_rows("x1", xT[1], "w0")
-        for t in (2, 3):
-            m_in[t] = load_plane("m%d" % t, mT, t)
-        y1 = load_rows("y1", y[1], "w1")
-        for t, slot in enumerate(("w3", None, "m0", "x0")):
-            m_out[t] = load_plane("m_out%d" % t, mT, t, slot)
-        xm1 = load_rows("xm1", xm[1], "w2")
-        w_out[3] = load_plane("w_out3", wT, 3, "m3")
+        def scores(b, x_b):
+            w_rounded = rounded("w%d" % b, on_vector, moving_views, w_got[:, :, GROUP[b]])
+            x_rounded = rounded("x%d" % b, on_scalar, stationary_views, x_b[:])
+            w_q = quantize("w%d" % b, w_rounded, E4M3)
+            x_q = quantize("x%d" % b, x_rounded, E4M3)
+            return products("score", b, x_q, w_q)
 
-        x_rounded = new("x_rounded1", [P, PACK * R], BF16)
-        round_on_scalar(stationary_views(x_rounded[:], x1[:]))
-        late = new("m_got_late", [P, 2, B, N], F32, "margin0")
-        for b in range(B):
-            gather_m(b, 2, late[:, 0, b, :])
-        x_q = quantize("x1", x_rounded, E4M3)
-        grad = {0: leave("grad00", banks[0], -LR, "grad0")}
-        scatter(w_out[0], 0, early[:], grad[0])
-        nc.gpsimd.tensor_tensor(early[:], drift, grad[0], ADD)
-        for t in range(1, PACK):
-            grad[t] = leave("grad0%d" % t, banks[t], 1.0 / BETA, "grad%d" % t)
-        for b in range(B):
-            gather_m(b, 3, late[:, 1, b, :])
+        def gradient(b, banks, y_b, xm_b, slot):
+            margin = new("margin%d" % b, [P, PACK, N], F32, slot)
+            for j in range(PACK):
+                nc.vector.tensor_tensor(margin[:, j, :], banks[j][:], y_b[:, j, :], MULT)
+                nc.scalar.activation(margin[:, j, :], margin[:, j, :], SIGMOID, scale=-1.0)
+            xm_rounded = rounded("xm%d" % b, on_scalar, stationary_views, xm_b[:])
+            for j in range(PACK):
+                nc.vector.scalar_tensor_tensor(margin[:, j, :], margin[:, j, :], neg_wt[:, b, j : j + 1], y_b[:, j, :], MULT, MULT)
+            g_rounded = rounded("g%d" % b, on_vector, moving_views, margin[:], "x%d_rounded" % b)
+            xm_q = quantize("xm%d" % b, xm_rounded, E4M3)
+            g_q = quantize("g%d" % b, g_rounded, E5M2)
+            return products("dw", b, xm_q, g_q)
 
-        step = {}
+        score0 = scores(0, x0)
+        score1 = scores(1, x1)
+        dw = [gradient(0, score0, y0, xm0, None), gradient(1, score1, y1, xm1, "x0")]
 
-        def sum_step(t):
-            step[t] = leave("step0%d" % t, turned("dw%d" % t, momentum[0, t], grad[t]), -LR * BETA, "step%d" % t)
-
-        def put_w(t):
-            scatter(w_out[t], 0, leave("new_w0%d" % t, turned("dw%d" % t, step[t], w_turned[t]), 1.0, "grad%d" % t))
-
-        def put_m(t):
-            bank = turned("dw%d" % t, step[t])
-            scatter(m_out[t], 0, leave("new_m0%d" % t, bank, -1.0 / LR))
-            return bank
-
-        sum_step(1)
-        sum_step(2)
-        put_w(1)
-        banks = products("score1", x_q, w_q)
-        g_rounded = new("g_rounded1", [P, PACK * N], BF16)
-        margin = new("margin1", [P, PACK, N], F32, "m1")
-        weight = new("weight1", [P, PACK, N], F32, "m2")
-        for j in range(PACK):
-            nc.scalar.activation(margin[:, j, :], banks[j][:], COPY)
-            nc.gpsimd.tensor_tensor(margin[:, j, :], margin[:, j, :], y1[:, j, :], MULT)
-        put_w(2)
-        scatter(m_out[0], 0, leave("new_m00", early, -1.0 / LR, "w_turned2"))
-        put_m(1)
-        for j in range(PACK):
-            nc.scalar.activation(weight[:, j, :], y1[:, j, :], COPY, scale=neg_wt[:, 1, j : j + 1])
-            nc.scalar.activation(margin[:, j, :], margin[:, j, :], SIGMOID, scale=-1.0)
-        sum_step(3)
-        put_m(2)
-        bank = put_m(3)
-        for j in range(PACK):
-            for cols in halves if j == PACK - 1 else [slice(0, N)]:
-                nc.gpsimd.tensor_tensor(margin[:, j, cols], margin[:, j, cols], weight[:, j, cols], MULT)
-        round_gradient(g_rounded, margin)
-        g_q = quantize("g1", g_rounded, E5M2, "new_m02")
-        xm_rounded = new("xm_rounded1", [P, PACK * D], BF16)
-        round_on_scalar(stationary_views(xm_rounded[:], xm1[:]))
-        xm_q = quantize("xm1", xm_rounded, E4M3)
-        scatter(w_out[3], 0, old_w(0, 3), leave("change03", bank, 1.0, "w2"))
-        kept = new("kept", [P, PACK, N], F32, "m1")
         for t in range(PACK):
-            nc.scalar.activation(kept[:, t, :], momentum[1, t], COPY, scale=BETA)
-        banks = products("dw1", xm_q, g_q)
-        for t in range(PACK):
-            grad[t] = leave("grad1%d" % t, banks[t], 1.0, "grad%d" % t)
-            scatter(m_out[t], 1, kept[:, t, :], grad[t])
-            nc.sync.dma_start(planes(out_1)[t], m_out[t][:])
-        for t in range(PACK):
-            step[t] = leave("step1%d" % t, turned("score%d" % t, kept[:, t, :], grad[t]), -LR, "step%d" % t)
-        for t in range(PACK):
-            scatter(w_out[t], 1, old_w(1, t), leave("change1%d" % t, turned("score%d" % t, step[t]), 1.0, "change%d" % t))
+            step = new("step%d" % t, [P, B * N], F32)
+            nc.scalar.activation(step[:], listed(m_in[t], ALL), COPY, scale=-LR * BETA)
+            for b in range(B):
+                nc.vector.scalar_tensor_tensor(step[:, GROUP[b]], dw[b][t][:], -LR, step[:, GROUP[b]], MULT, ADD)
+            nc.vector.tensor_tensor(listed(w_out[t], ALL), w_got[:, t, :], step[:], ADD)
             nc.sync.dma_start(planes(out_0)[t], w_out[t][:])
+            for piece in PIECES:
+                nc.scalar.activation(listed(m_out[t], piece), step[:, piece], COPY, scale=-1.0 / LR)
+            nc.sync.dma_start(planes(out_1)[t], m_out[t][:])

@@ -25,6 +25,7 @@ STRIPE = 16
 ALL = slice(0, B * N)
 GROUP = [slice(b * N, (b + 1) * N) for b in range(B)]
 PIECES = [slice(0, 384), slice(384, 768), slice(768, 1024)]
+QUARTERS = [slice(k * 256, (k + 1) * 256) for k in range(4)]
 
 
 def tile_attend_gsig_mom_kernel(tc, xT, wT, y, wt, xm, mT, offs, out_0, out_1):
@@ -107,60 +108,102 @@ def tile_attend_gsig_mom_kernel(tc, xT, wT, y, wt, xm, mT, offs, out_0, out_1):
                 banks.append(bank)
             return banks
 
+        wt_in = new("wt_in", [P, B, PACK], F32)
+        nc.scalar.dma_start(wt_in[:], wt.rearrange("b (p j) c -> p b (j c)", j=PACK))
+        neg_wt = new("neg_wt", [P, B, PACK], F32)
+        nc.vector.tensor_scalar(neg_wt[:], wt_in[:], -1.0, None, MULT)
         w_got = new("w_got", [P, PACK, B * N], F32)
         w_in = [load_plane("w%d" % t, wT, t) for t in range(PACK)]
         x0 = load_rows("x0", xT[0])
-        wt_in = new("wt_in", [P, B, PACK], F32)
-        nc.sync.dma_start(wt_in[:], wt.rearrange("b (p j) c -> p b (j c)", j=PACK))
         y0 = load_rows("y0", y[0])
         x1 = load_rows("x1", xT[1])
         xm0 = load_rows("xm0", xm[0])
+
+        def copy_w(t, slot=None):
+            dest = new("w_out%d" % t, [P, T], F32, slot)
+            nc.scalar.activation(dest[:], w_in[t][:], COPY)
+            return dest
+
+        last = PACK - 1
+        w_out = []
+        for t in range(last):
+            nc.vector.tensor_copy(w_got[:, t, :], listed(w_in[t], ALL))
+            w_out.append(copy_w(t))
+        nc.vector.tensor_copy(w_got[:, last, GROUP[0]], listed(w_in[last], GROUP[0]))
+        nc.scalar.activation(w_got[:, last, GROUP[1]], listed(w_in[last], GROUP[1]), COPY)
+
+        w_rounded = [rounded("w%d" % b, engine, moving_views, w_got[:, :, GROUP[b]]) for b, engine in enumerate((on_vector, on_scalar))]
+        w_out.append(copy_w(last))
+        x_rounded = rounded("x0", on_vector, stationary_views, x0[:])
+        w_q = quantize("w0", w_rounded[0], E4M3, "x0")
+        score = [products("score", 0, quantize("x0", x_rounded, E4M3), w_q)]
+        w_q = quantize("w1", w_rounded[1], E4M3, "x0_rounded")
+
+        m_in, m_out = {}, {}
+        m_in[0] = load_plane("m0", mT, 0)
         y1 = load_rows("y1", y[1])
         xm1 = load_rows("xm1", xm[1])
+        m_in[1] = load_plane("m1", mT, 1)
+        m_in[2] = load_plane("m2", mT, 2, "w0")
+        m_out[0] = load_plane("m_out0", mT, 0)
+        m_in[3] = load_plane("m3", mT, 3, "w1")
+        m_out[1] = load_plane("m_out1", mT, 1)
+        m_out[2] = load_plane("m_out2", mT, 2, "w2")
+        m_out[3] = load_plane("m_out3", mT, 3, "w3")
 
-        w_out = []
-        for t in range(PACK):
-            nc.vector.tensor_copy(w_got[:, t, :], listed(w_in[t], ALL))
-            w_out.append(new("w_out%d" % t, [P, T], F32))
-            nc.scalar.activation(w_out[t][:], w_in[t][:], COPY)
-        m_in, m_out = [], []
-        for t in range(PACK):
-            m_in.append(load_plane("m%d" % t, mT, t, "w%d" % t))
-            m_out.append(load_plane("m_out%d" % t, mT, t))
-        neg_wt = new("neg_wt", [P, B, PACK], F32)
-        nc.scalar.activation(neg_wt[:], wt_in[:], COPY, scale=-1.0)
-
-        def scores(b, x_b):
-            w_rounded = rounded("w%d" % b, on_vector, moving_views, w_got[:, :, GROUP[b]])
-            x_rounded = rounded("x%d" % b, on_scalar, stationary_views, x_b[:])
-            w_q = quantize("w%d" % b, w_rounded, E4M3)
-            x_q = quantize("x%d" % b, x_rounded, E4M3)
-            return products("score", b, x_q, w_q)
-
-        def gradient(b, banks, y_b, xm_b, slot):
+        def margins(b, y_b, slot):
             margin = new("margin%d" % b, [P, PACK, N], F32, slot)
             for j in range(PACK):
-                nc.vector.tensor_tensor(margin[:, j, :], banks[j][:], y_b[:, j, :], MULT)
+                nc.vector.tensor_tensor(margin[:, j, :], score[b][j][:], y_b[:, j, :], MULT)
                 nc.scalar.activation(margin[:, j, :], margin[:, j, :], SIGMOID, scale=-1.0)
-            xm_rounded = rounded("xm%d" % b, on_scalar, stationary_views, xm_b[:])
+            return margin
+
+        def gradient(b, margin, y_b, slot):
             for j in range(PACK):
                 nc.vector.scalar_tensor_tensor(margin[:, j, :], margin[:, j, :], neg_wt[:, b, j : j + 1], y_b[:, j, :], MULT, MULT)
-            g_rounded = rounded("g%d" % b, on_vector, moving_views, margin[:], "x%d_rounded" % b)
-            xm_q = quantize("xm%d" % b, xm_rounded, E4M3)
-            g_q = quantize("g%d" % b, g_rounded, E5M2)
-            return products("dw", b, xm_q, g_q)
+            return rounded("g%d" % b, on_vector, moving_views, margin[:], slot)
 
-        score0 = scores(0, x0)
-        score1 = scores(1, x1)
-        dw = [gradient(0, score0, y0, xm0, None), gradient(1, score1, y1, xm1, "x0")]
+        def drift(t):
+            dest = new("step%d" % t, [P, B * N], F32)
+            nc.scalar.activation(dest[:], listed(m_in[t], ALL), COPY, scale=-LR * BETA)
+            return dest
 
-        for t in range(PACK):
-            step = new("step%d" % t, [P, B * N], F32)
-            nc.scalar.activation(step[:], listed(m_in[t], ALL), COPY, scale=-LR * BETA)
+        def finish(t, b):
+            nc.vector.scalar_tensor_tensor(step[t][:, GROUP[b]], dw[b][t][:], -LR, step[t][:, GROUP[b]], MULT, ADD)
+
+        def put_w(t, entries):
+            nc.vector.tensor_tensor(listed(w_out[t], entries), w_got[:, t, entries], step[t][:, entries], ADD)
+
+        def put_m(t, pieces):
+            for piece in pieces:
+                nc.scalar.activation(listed(m_out[t], piece), step[t][:, piece], COPY, scale=-1.0 / LR)
+
+        g_q = quantize("g0", gradient(0, margins(0, y0, None), y0, "w0_rounded"), E5M2)
+        x_q = quantize("x1", rounded("x1", on_scalar, stationary_views, x1[:]), E4M3)
+        score.append(products("score", 1, x_q, w_q))
+        xm_q = quantize("xm0", rounded("xm0", on_scalar, stationary_views, xm0[:]), E4M3)
+        step = [drift(0)]
+        margin = margins(1, y1, None)
+        dw = [products("dw0", 1, xm_q, g_q)]
+        finish(0, 0)
+        g_rounded = gradient(1, margin, y1, "w1_rounded")
+        xm_rounded = rounded("xm1", on_vector, stationary_views, xm1[:])
+        g_q = quantize("g1", g_rounded, E5M2)
+        dw.append(products("dw1", 0, quantize("xm1", xm_rounded, E4M3), g_q))
+        step.extend(drift(t) for t in range(1, last))
+        put_w(0, GROUP[0])
+        put_m(0, QUARTERS[:2])
+        finish(0, 1)
+        put_w(0, GROUP[1])
+        nc.sync.dma_start(planes(out_0)[0], w_out[0][:])
+        put_m(0, QUARTERS[2:])
+        nc.sync.dma_start(planes(out_1)[0], m_out[0][:])
+        step.append(drift(last))
+
+        for t in range(1, PACK):
             for b in range(B):
-                nc.vector.scalar_tensor_tensor(step[:, GROUP[b]], dw[b][t][:], -LR, step[:, GROUP[b]], MULT, ADD)
-            nc.vector.tensor_tensor(listed(w_out[t], ALL), w_got[:, t, :], step[:], ADD)
+                finish(t, b)
+            put_w(t, ALL)
             nc.sync.dma_start(planes(out_0)[t], w_out[t][:])
-            for piece in PIECES:
-                nc.scalar.activation(listed(m_out[t], piece), step[:, piece], COPY, scale=-1.0 / LR)
+            put_m(t, PIECES)
             nc.sync.dma_start(planes(out_1)[t], m_out[t][:])

@@ -115,8 +115,8 @@ def tile_attend_gsig_mom_kernel(tc, xT, wT, y, wt, xm, mT, offs, out_0, out_1):
         w_got = new("w_got", [P, PACK, B * N], F32)
         w_in = [load_plane("w%d" % t, wT, t) for t in range(PACK)]
         x0 = load_rows("x0", xT[0])
-        y0 = load_rows("y0", y[0])
         x1 = load_rows("x1", xT[1])
+        y0 = load_rows("y0", y[0])
         xm0 = load_rows("xm0", xm[0])
 
         def copy_w(t, slot=None):
@@ -142,68 +142,83 @@ def tile_attend_gsig_mom_kernel(tc, xT, wT, y, wt, xm, mT, offs, out_0, out_1):
         m_in, m_out = {}, {}
         m_in[0] = load_plane("m0", mT, 0)
         y1 = load_rows("y1", y[1])
-        xm1 = load_rows("xm1", xm[1])
         m_in[1] = load_plane("m1", mT, 1)
         m_in[2] = load_plane("m2", mT, 2, "w0")
-        m_out[0] = load_plane("m_out0", mT, 0)
+        xm1 = load_rows("xm1", xm[1])
         m_in[3] = load_plane("m3", mT, 3, "w1")
+        m_out[0] = load_plane("m_out0", mT, 0)
         m_out[1] = load_plane("m_out1", mT, 1)
         m_out[2] = load_plane("m_out2", mT, 2, "w2")
         m_out[3] = load_plane("m_out3", mT, 3, "w3")
 
-        def margins(b, y_b, slot):
-            margin = new("margin%d" % b, [P, PACK, N], F32, slot)
+        def weights(b, y_b, slot):
+            dest = new("weight%d" % b, [P, PACK, N], F32, slot)
             for j in range(PACK):
-                nc.vector.tensor_tensor(margin[:, j, :], score[b][j][:], y_b[:, j, :], MULT)
-                nc.scalar.activation(margin[:, j, :], margin[:, j, :], SIGMOID, scale=-1.0)
-            return margin
+                nc.gpsimd.tensor_scalar(dest[:, j, :], y_b[:, j, :], neg_wt[:, b, j : j + 1], 0.0, MULT, ADD)
+            return dest
 
-        def gradient(b, margin, y_b, slot):
-            for j in range(PACK):
-                nc.vector.scalar_tensor_tensor(margin[:, j, :], margin[:, j, :], neg_wt[:, b, j : j + 1], y_b[:, j, :], MULT, MULT)
-            return rounded("g%d" % b, on_vector, moving_views, margin[:], slot)
+        def gradient(b, prob, weight, slot):
+            dest = new("g%d_rounded" % b, [P, PACK * N], BF16, slot)
+            woven, planar = moving_views(dest[:], prob[:])
+            nc.vector.tensor_tensor(woven, planar, moving_views(dest[:], weight[:])[1], MULT)
+            return dest
 
         def drift(t):
-            dest = new("step%d" % t, [P, B * N], F32)
+            dest = new("drift%d" % t, [P, B * N], F32)
             nc.scalar.activation(dest[:], listed(m_in[t], ALL), COPY, scale=-LR * BETA)
             return dest
 
         def finish(t, b):
-            nc.vector.scalar_tensor_tensor(step[t][:, GROUP[b]], dw[b][t][:], -LR, step[t][:, GROUP[b]], MULT, ADD)
+            nc.vector.scalar_tensor_tensor(step[t][:, GROUP[b]], dw[b][t][:], -LR, drifts[t][:, GROUP[b]], MULT, ADD)
 
-        def put_w(t, entries):
-            nc.vector.tensor_tensor(listed(w_out[t], entries), w_got[:, t, entries], step[t][:, entries], ADD)
+        def put_w(t):
+            nc.vector.tensor_tensor(listed(w_out[t], ALL), w_got[:, t, :], step[t][:], ADD)
+            nc.sync.dma_start(planes(out_0)[t], w_out[t][:])
 
         def put_m(t, pieces):
             for piece in pieces:
                 nc.scalar.activation(listed(m_out[t], piece), step[t][:, piece], COPY, scale=-1.0 / LR)
 
-        g_q = quantize("g0", gradient(0, margins(0, y0, None), y0, "w0_rounded"), E5M2)
-        x_q = quantize("x1", rounded("x1", on_scalar, stationary_views, x1[:]), E4M3)
-        score.append(products("score", 1, x_q, w_q))
+        x_rounded = rounded("x1", on_scalar, stationary_views, x1[:])
+        weight = weights(0, y0, None)
+        prob = new("prob0", [P, PACK, N], F32)
+        margin = new("margin", [P, N], F32)
+        for j in range(PACK):
+            source = margin[:] if j == 0 else prob[:, j, :]
+            nc.vector.tensor_tensor(source, score[0][j][:], y0[:, j, :], MULT)
+            nc.scalar.activation(prob[:, j, :], source, SIGMOID, scale=-1.0)
+        score.append(products("score", 1, quantize("x1", x_rounded, E4M3, "margin"), w_q))
+        g_q = quantize("g0", gradient(0, prob, weight, "w0_rounded"), E5M2)
         xm_q = quantize("xm0", rounded("xm0", on_scalar, stationary_views, xm0[:]), E4M3)
-        step = [drift(0)]
-        margin = margins(1, y1, None)
+        drifts = [drift(0)]
+        weight = weights(1, y1, "xm0_rounded")
+        prob = new("prob1", [P, PACK, N], F32, "x1")
+        for j in range(PACK):
+            nc.vector.tensor_tensor(prob[:, j, :], score[1][j][:], y1[:, j, :], MULT)
+            nc.scalar.activation(prob[:, j, :], prob[:, j, :], SIGMOID, scale=-1.0)
         dw = [products("dw0", 1, xm_q, g_q)]
+        step = {0: drifts[0]}
         finish(0, 0)
-        g_rounded = gradient(1, margin, y1, "w1_rounded")
+        g_rounded = gradient(1, prob, weight, "w1_rounded")
+        drifts.extend(drift(t) for t in range(1, PACK))
+        step[1], step[3] = drifts[1], drifts[3]
+        finish(1, 0)
         xm_rounded = rounded("xm1", on_vector, stationary_views, xm1[:])
-        g_q = quantize("g1", g_rounded, E5M2)
+        g_q = quantize("g1", g_rounded, E5M2, "xm1")
         dw.append(products("dw1", 0, quantize("xm1", xm_rounded, E4M3), g_q))
-        step.extend(drift(t) for t in range(1, last))
-        put_w(0, GROUP[0])
+        step[2] = new("step2", [P, B * N], F32, "xm1_rounded")
+        finish(2, 0)
         put_m(0, QUARTERS[:2])
         finish(0, 1)
-        put_w(0, GROUP[1])
-        nc.sync.dma_start(planes(out_0)[0], w_out[0][:])
+        finish(1, 1)
+        put_w(0)
         put_m(0, QUARTERS[2:])
         nc.sync.dma_start(planes(out_1)[0], m_out[0][:])
-        step.append(drift(last))
-
+        finish(2, 1)
         for t in range(1, PACK):
-            for b in range(B):
-                finish(t, b)
-            put_w(t, ALL)
-            nc.sync.dma_start(planes(out_0)[t], w_out[t][:])
+            put_w(t)
             put_m(t, PIECES)
-            nc.sync.dma_start(planes(out_1)[t], m_out[t][:])
+            (nc.scalar if t == last else nc.sync).dma_start(planes(out_1)[t], m_out[t][:])
+            if t == 1:
+                for b in range(B):
+                    finish(last, b)

@@ -133,7 +133,6 @@ def tile_attend_gsig_mom_kernel(tc, xT, wT, y, wt, xm, mT, offs, out_0, out_1):
         nc.scalar.activation(w_got[:, last, GROUP[1]], listed(w_in[last], GROUP[1]), COPY)
 
         w_rounded = [rounded("w%d" % b, engine, moving_views, w_got[:, :, GROUP[b]]) for b, engine in enumerate((on_vector, on_scalar))]
-        w_out.append(copy_w(last))
         x_rounded = rounded("x0", on_vector, stationary_views, x0[:])
         w_q = quantize("w0", w_rounded[0], E4M3, "x0")
         score = [products("score", 0, quantize("x0", x_rounded, E4M3), w_q)]
@@ -142,14 +141,15 @@ def tile_attend_gsig_mom_kernel(tc, xT, wT, y, wt, xm, mT, offs, out_0, out_1):
         m_in, m_out = {}, {}
         m_in[0] = load_plane("m0", mT, 0)
         y1 = load_rows("y1", y[1])
+        m_out[0] = load_plane("m_out0", mT, 0)
         m_in[1] = load_plane("m1", mT, 1)
         m_in[2] = load_plane("m2", mT, 2, "w0")
-        xm1 = load_rows("xm1", xm[1])
-        m_in[3] = load_plane("m3", mT, 3, "w1")
-        m_out[0] = load_plane("m_out0", mT, 0)
         m_out[1] = load_plane("m_out1", mT, 1)
+        m_in[3] = load_plane("m3", mT, 3, "w1")
+        xm1 = load_rows("xm1", xm[1])
         m_out[2] = load_plane("m_out2", mT, 2, "w2")
         m_out[3] = load_plane("m_out3", mT, 3, "w3")
+        w_out.append(load_plane("w_out3", wT, 3))
 
         def weights(b, y_b, slot):
             dest = new("weight%d" % b, [P, PACK, N], F32, slot)
@@ -171,9 +171,8 @@ def tile_attend_gsig_mom_kernel(tc, xT, wT, y, wt, xm, mT, offs, out_0, out_1):
         def finish(t, b):
             nc.vector.scalar_tensor_tensor(step[t][:, GROUP[b]], dw[b][t][:], -LR, drifts[t][:, GROUP[b]], MULT, ADD)
 
-        def put_w(t):
-            nc.vector.tensor_tensor(listed(w_out[t], ALL), w_got[:, t, :], step[t][:], ADD)
-            nc.sync.dma_start(planes(out_0)[t], w_out[t][:])
+        def put_w(t, entries):
+            nc.vector.tensor_tensor(listed(w_out[t], entries), w_got[:, t, entries], step[t][:, entries], ADD)
 
         def put_m(t, pieces):
             for piece in pieces:
@@ -200,25 +199,29 @@ def tile_attend_gsig_mom_kernel(tc, xT, wT, y, wt, xm, mT, offs, out_0, out_1):
         step = {0: drifts[0]}
         finish(0, 0)
         g_rounded = gradient(1, prob, weight, "w1_rounded")
-        drifts.extend(drift(t) for t in range(1, PACK))
-        step[1], step[3] = drifts[1], drifts[3]
+        g_q = quantize("g1", g_rounded, E5M2)
+        put_w(0, GROUP[0])
+        put_m(0, QUARTERS[:2])
+        drifts.extend(drift(t) for t in (1, 2))
+        step[1] = drifts[1]
         finish(1, 0)
+        put_w(1, GROUP[0])
+        put_m(1, QUARTERS[:2])
+        drifts.append(drift(last))
         xm_rounded = rounded("xm1", on_vector, stationary_views, xm1[:])
-        g_q = quantize("g1", g_rounded, E5M2, "xm1")
         dw.append(products("dw1", 0, quantize("xm1", xm_rounded, E4M3), g_q))
         step[2] = new("step2", [P, B * N], F32, "xm1_rounded")
+        step[3] = new("step3", [P, B * N], F32, "g1_codes")
         finish(2, 0)
-        put_m(0, QUARTERS[:2])
         finish(0, 1)
         finish(1, 1)
-        put_w(0)
-        put_m(0, QUARTERS[2:])
-        nc.sync.dma_start(planes(out_1)[0], m_out[0][:])
-        finish(2, 1)
-        for t in range(1, PACK):
-            put_w(t)
-            put_m(t, PIECES)
+        for t in range(PACK):
+            put_w(t, GROUP[1] if t < 2 else ALL)
+            nc.sync.dma_start(planes(out_0)[t], w_out[t][:])
+            put_m(t, QUARTERS[2:] if t < 2 else PIECES)
             (nc.scalar if t == last else nc.sync).dma_start(planes(out_1)[t], m_out[t][:])
+            if t == 0:
+                finish(2, 1)
             if t == 1:
                 for b in range(B):
                     finish(last, b)

@@ -108,6 +108,12 @@ def tile_attend_gsig_mom_kernel(tc, xT, wT, y, wt, xm, mT, offs, out_0, out_1):
                 banks.append(bank)
             return banks
 
+        def load_halves(name, matrix):
+            dest = new(name, [P, PACK, 512], F32)
+            for j in range(0, PACK, 2):
+                nc.sync.dma_start(dest[:, j : j + 2, :], rows4(matrix)[:, j : j + 2, :])
+            return dest
+
         wt_in = new("wt_in", [P, B, PACK], F32)
         nc.scalar.dma_start(wt_in[:], wt.rearrange("b (p j) c -> p b (j c)", j=PACK))
         neg_wt = new("neg_wt", [P, B, PACK], F32)
@@ -116,7 +122,7 @@ def tile_attend_gsig_mom_kernel(tc, xT, wT, y, wt, xm, mT, offs, out_0, out_1):
         w_in = [load_plane("w%d" % t, wT, t) for t in range(PACK)]
         x0 = load_rows("x0", xT[0])
         x1 = load_rows("x1", xT[1])
-        y0 = load_rows("y0", y[0])
+        y0 = load_halves("y0", y[0])
         xm0 = load_rows("xm0", xm[0])
 
         def copy_w(t, slot=None):
@@ -129,10 +135,14 @@ def tile_attend_gsig_mom_kernel(tc, xT, wT, y, wt, xm, mT, offs, out_0, out_1):
         for t in range(last):
             nc.vector.tensor_copy(w_got[:, t, :], listed(w_in[t], ALL))
             w_out.append(copy_w(t))
-        nc.vector.tensor_copy(w_got[:, last, GROUP[0]], listed(w_in[last], GROUP[0]))
-        nc.scalar.activation(w_got[:, last, GROUP[1]], listed(w_in[last], GROUP[1]), COPY)
+        mine, rest = slice(0, 320), slice(320, B * N)
+        nc.vector.tensor_copy(w_got[:, last, mine], listed(w_in[last], mine))
+        nc.scalar.activation(w_got[:, last, rest], listed(w_in[last], rest), COPY)
 
-        w_rounded = [rounded("w%d" % b, engine, moving_views, w_got[:, :, GROUP[b]]) for b, engine in enumerate((on_vector, on_scalar))]
+        w_rounded = [new("w0_rounded", [P, PACK * N], BF16)]
+        on_vector(moving_views(w_rounded[0][:, 0 : PACK * 320], w_got[:, :, 0:320]))
+        on_scalar(moving_views(w_rounded[0][:, PACK * 320 : PACK * N], w_got[:, :, 320:N]))
+        w_rounded.append(rounded("w1", on_scalar, moving_views, w_got[:, :, GROUP[1]]))
         x_rounded = rounded("x0", on_vector, stationary_views, x0[:])
         w_q = quantize("w0", w_rounded[0], E4M3, "x0")
         score = [products("score", 0, quantize("x0", x_rounded, E4M3), w_q)]
@@ -141,12 +151,12 @@ def tile_attend_gsig_mom_kernel(tc, xT, wT, y, wt, xm, mT, offs, out_0, out_1):
         m_in, m_out = {}, {}
         m_in[0] = load_plane("m0", mT, 0)
         y1 = load_rows("y1", y[1])
-        m_out[0] = load_plane("m_out0", mT, 0)
         m_in[1] = load_plane("m1", mT, 1)
+        m_out[0] = load_plane("m_out0", mT, 0)
         m_in[2] = load_plane("m2", mT, 2, "w0")
         m_out[1] = load_plane("m_out1", mT, 1)
-        m_in[3] = load_plane("m3", mT, 3, "w1")
         xm1 = load_rows("xm1", xm[1])
+        m_in[3] = load_plane("m3", mT, 3, "w1")
         m_out[2] = load_plane("m_out2", mT, 2, "w2")
         m_out[3] = load_plane("m_out3", mT, 3, "w3")
         w_out.append(load_plane("w_out3", wT, 3))
@@ -179,7 +189,7 @@ def tile_attend_gsig_mom_kernel(tc, xT, wT, y, wt, xm, mT, offs, out_0, out_1):
                 nc.scalar.activation(listed(m_out[t], piece), step[t][:, piece], COPY, scale=-1.0 / LR)
 
         x_rounded = rounded("x1", on_scalar, stationary_views, x1[:])
-        weight = weights(0, y0, None)
+        weight = weights(0, y0, "w1_rounded")
         prob = new("prob0", [P, PACK, N], F32)
         margin = new("margin", [P, N], F32)
         for j in range(PACK):
@@ -198,20 +208,21 @@ def tile_attend_gsig_mom_kernel(tc, xT, wT, y, wt, xm, mT, offs, out_0, out_1):
         dw = [products("dw0", 1, xm_q, g_q)]
         step = {0: drifts[0]}
         finish(0, 0)
-        g_rounded = gradient(1, prob, weight, "w1_rounded")
-        g_q = quantize("g1", g_rounded, E5M2)
+        g_rounded = gradient(1, prob, weight, "x1_rounded")
+        drifts.append(drift(1))
         put_w(0, GROUP[0])
         put_m(0, QUARTERS[:2])
-        drifts.extend(drift(t) for t in (1, 2))
+        drifts.append(drift(2))
         step[1] = drifts[1]
         finish(1, 0)
         put_w(1, GROUP[0])
         put_m(1, QUARTERS[:2])
         drifts.append(drift(last))
         xm_rounded = rounded("xm1", on_vector, stationary_views, xm1[:])
+        g_q = quantize("g1", g_rounded, E5M2, "xm1")
         dw.append(products("dw1", 0, quantize("xm1", xm_rounded, E4M3), g_q))
         step[2] = new("step2", [P, B * N], F32, "xm1_rounded")
-        step[3] = new("step3", [P, B * N], F32, "g1_codes")
+        step[3] = new("step3", [P, B * N], F32, "xm1_codes")
         finish(2, 0)
         finish(0, 1)
         finish(1, 1)

@@ -108,12 +108,6 @@ def tile_attend_gsig_mom_kernel(tc, xT, wT, y, wt, xm, mT, offs, out_0, out_1):
                 banks.append(bank)
             return banks
 
-        def load_halves(name, matrix):
-            dest = new(name, [P, PACK, 512], F32)
-            for j in range(0, PACK, 2):
-                nc.sync.dma_start(dest[:, j : j + 2, :], rows4(matrix)[:, j : j + 2, :])
-            return dest
-
         wt_in = new("wt_in", [P, B, PACK], F32)
         nc.scalar.dma_start(wt_in[:], wt.rearrange("b (p j) c -> p b (j c)", j=PACK))
         neg_wt = new("neg_wt", [P, B, PACK], F32)
@@ -122,7 +116,7 @@ def tile_attend_gsig_mom_kernel(tc, xT, wT, y, wt, xm, mT, offs, out_0, out_1):
         w_in = [load_plane("w%d" % t, wT, t) for t in range(PACK)]
         x0 = load_rows("x0", xT[0])
         x1 = load_rows("x1", xT[1])
-        y0 = load_halves("y0", y[0])
+        y0 = load_rows("y0", y[0])
         xm0 = load_rows("xm0", xm[0])
 
         def copy_w(t, slot=None):
@@ -135,14 +129,10 @@ def tile_attend_gsig_mom_kernel(tc, xT, wT, y, wt, xm, mT, offs, out_0, out_1):
         for t in range(last):
             nc.vector.tensor_copy(w_got[:, t, :], listed(w_in[t], ALL))
             w_out.append(copy_w(t))
-        mine, rest = slice(0, 320), slice(320, B * N)
-        nc.vector.tensor_copy(w_got[:, last, mine], listed(w_in[last], mine))
-        nc.scalar.activation(w_got[:, last, rest], listed(w_in[last], rest), COPY)
+        nc.vector.tensor_copy(w_got[:, last, GROUP[0]], listed(w_in[last], GROUP[0]))
+        nc.scalar.activation(w_got[:, last, GROUP[1]], listed(w_in[last], GROUP[1]), COPY)
 
-        w_rounded = [new("w0_rounded", [P, PACK * N], BF16)]
-        on_vector(moving_views(w_rounded[0][:, 0 : PACK * 320], w_got[:, :, 0:320]))
-        on_scalar(moving_views(w_rounded[0][:, PACK * 320 : PACK * N], w_got[:, :, 320:N]))
-        w_rounded.append(rounded("w1", on_scalar, moving_views, w_got[:, :, GROUP[1]]))
+        w_rounded = [rounded("w%d" % b, engine, moving_views, w_got[:, :, GROUP[b]]) for b, engine in enumerate((on_vector, on_scalar))]
         x_rounded = rounded("x0", on_vector, stationary_views, x0[:])
         w_q = quantize("w0", w_rounded[0], E4M3, "x0")
         score = [products("score", 0, quantize("x0", x_rounded, E4M3), w_q)]
@@ -173,23 +163,27 @@ def tile_attend_gsig_mom_kernel(tc, xT, wT, y, wt, xm, mT, offs, out_0, out_1):
             nc.vector.tensor_tensor(woven, planar, moving_views(dest[:], weight[:])[1], MULT)
             return dest
 
-        def drift(t):
-            dest = new("drift%d" % t, [P, B * N], F32)
-            nc.scalar.activation(dest[:], listed(m_in[t], ALL), COPY, scale=-LR * BETA)
+        def drift(name, t, entries, slot=None):
+            dest = new(name, [P, entries.stop - entries.start], F32, slot)
+            nc.scalar.activation(dest[:], listed(m_in[t], entries), COPY, scale=-LR * BETA)
             return dest
 
-        def finish(t, b):
-            nc.vector.scalar_tensor_tensor(step[t][:, GROUP[b]], dw[b][t][:], -LR, drifts[t][:, GROUP[b]], MULT, ADD)
+        def finish(dest, bank, drifted):
+            nc.vector.scalar_tensor_tensor(dest, bank[:], -LR, drifted, MULT, ADD)
 
-        def put_w(t, entries):
-            nc.vector.tensor_tensor(listed(w_out[t], entries), w_got[:, t, entries], step[t][:, entries], ADD)
+        def put_w(t, entries, values):
+            nc.vector.tensor_tensor(listed(w_out[t], entries), w_got[:, t, entries], values, ADD)
 
-        def put_m(t, pieces):
+        def put_m(t, pieces, values, start=0):
             for piece in pieces:
-                nc.scalar.activation(listed(m_out[t], piece), step[t][:, piece], COPY, scale=-1.0 / LR)
+                nc.scalar.activation(listed(m_out[t], piece), values[:, piece.start - start : piece.stop - start], COPY, scale=-1.0 / LR)
+
+        def store(t):
+            nc.sync.dma_start(planes(out_0)[t], w_out[t][:])
+            (nc.scalar if t == last else nc.sync).dma_start(planes(out_1)[t], m_out[t][:])
 
         x_rounded = rounded("x1", on_scalar, stationary_views, x1[:])
-        weight = weights(0, y0, "w1_rounded")
+        weight = weights(0, y0, None)
         prob = new("prob0", [P, PACK, N], F32)
         margin = new("margin", [P, N], F32)
         for j in range(PACK):
@@ -197,42 +191,50 @@ def tile_attend_gsig_mom_kernel(tc, xT, wT, y, wt, xm, mT, offs, out_0, out_1):
             nc.vector.tensor_tensor(source, score[0][j][:], y0[:, j, :], MULT)
             nc.scalar.activation(prob[:, j, :], source, SIGMOID, scale=-1.0)
         score.append(products("score", 1, quantize("x1", x_rounded, E4M3, "margin"), w_q))
-        g_q = quantize("g0", gradient(0, prob, weight, "w0_rounded"), E5M2)
-        xm_q = quantize("xm0", rounded("xm0", on_scalar, stationary_views, xm0[:]), E4M3)
-        drifts = [drift(0)]
+        g_rounded = gradient(0, prob, weight, "w0_rounded")
+        xm_rounded = new("xm0_rounded", [P, PACK * D], BF16)
+        dealt, raw = stationary_views(xm_rounded[:], xm0[:])
+        on_vector((dealt[:, 0:32], raw[:, 0:32]))
+        on_scalar((dealt[:, 32:P], raw[:, 32:P]))
+        g_q = quantize("g0", g_rounded, E5M2)
+        xm_q = quantize("xm0", xm_rounded, E4M3)
+        step0 = drift("step0", 0, ALL)
         weight = weights(1, y1, "xm0_rounded")
         prob = new("prob1", [P, PACK, N], F32, "x1")
         for j in range(PACK):
             nc.vector.tensor_tensor(prob[:, j, :], score[1][j][:], y1[:, j, :], MULT)
             nc.scalar.activation(prob[:, j, :], prob[:, j, :], SIGMOID, scale=-1.0)
-        dw = [products("dw0", 1, xm_q, g_q)]
-        step = {0: drifts[0]}
-        finish(0, 0)
-        g_rounded = gradient(1, prob, weight, "x1_rounded")
-        drifts.append(drift(1))
-        put_w(0, GROUP[0])
-        put_m(0, QUARTERS[:2])
-        drifts.append(drift(2))
-        step[1] = drifts[1]
-        finish(1, 0)
-        put_w(1, GROUP[0])
-        put_m(1, QUARTERS[:2])
-        drifts.append(drift(last))
+        dw0 = products("dw0", 1, xm_q, g_q)
+        finish(step0[:, GROUP[0]], dw0[0], step0[:, GROUP[0]])
+        g_rounded = gradient(1, prob, weight, "w1_rounded")
+        step1 = drift("step1", 1, ALL)
+        put_w(0, GROUP[0], step0[:, GROUP[0]])
+        put_m(0, QUARTERS[:2], step0)
+        drift2 = drift("drift2", 2, ALL)
+        finish(step1[:, GROUP[0]], dw0[1], step1[:, GROUP[0]])
+        put_w(1, QUARTERS[0], step1[:, QUARTERS[0]])
+        put_m(1, QUARTERS[:2], step1)
+        drift30 = drift("drift30", 3, GROUP[0])
         xm_rounded = rounded("xm1", on_vector, stationary_views, xm1[:])
         g_q = quantize("g1", g_rounded, E5M2, "xm1")
-        dw.append(products("dw1", 0, quantize("xm1", xm_rounded, E4M3), g_q))
-        step[2] = new("step2", [P, B * N], F32, "xm1_rounded")
-        step[3] = new("step3", [P, B * N], F32, "xm1_codes")
-        finish(2, 0)
-        finish(0, 1)
-        finish(1, 1)
-        for t in range(PACK):
-            put_w(t, GROUP[1] if t < 2 else ALL)
-            nc.sync.dma_start(planes(out_0)[t], w_out[t][:])
-            put_m(t, QUARTERS[2:] if t < 2 else PIECES)
-            (nc.scalar if t == last else nc.sync).dma_start(planes(out_1)[t], m_out[t][:])
-            if t == 0:
-                finish(2, 1)
-            if t == 1:
-                for b in range(B):
-                    finish(last, b)
+        dw1 = products("dw1", 0, quantize("xm1", xm_rounded, E4M3), g_q)
+        step2 = new("step2", [P, B * N], F32, "xm1_rounded")
+        step3 = new("step3", [P, B * N], F32, "xm1_codes")
+        finish(step2[:, GROUP[0]], dw0[2], drift2[:, GROUP[0]])
+        finish(step0[:, GROUP[1]], dw1[0], step0[:, GROUP[1]])
+        finish(step1[:, GROUP[1]], dw1[1], step1[:, GROUP[1]])
+        put_w(0, GROUP[1], step0[:, GROUP[1]])
+        put_m(0, QUARTERS[2:], step0)
+        store(0)
+        finish(step2[:, GROUP[1]], dw1[2], drift2[:, GROUP[1]])
+        put_w(1, slice(256, B * N), step1[:, 256 : B * N])
+        put_m(1, QUARTERS[2:], step1)
+        store(1)
+        drift31 = new("drift31", [P, N], F32)
+        nc.vector.tensor_scalar(drift31[:], listed(m_in[3], GROUP[1]), -LR * BETA, 0.0, MULT, ADD)
+        finish(step3[:, GROUP[0]], dw0[3], drift30[:])
+        finish(step3[:, GROUP[1]], dw1[3], drift31[:])
+        for t, step in ((2, step2), (3, step3)):
+            put_w(t, ALL, step[:])
+            put_m(t, PIECES, step)
+            store(t)

@@ -1,3 +1,4 @@
+import math
 from contextlib import ExitStack
 
 import concourse.mybir as mybir
@@ -18,14 +19,14 @@ MULT = mybir.AluOpType.mult
 ADD = mybir.AluOpType.add
 COPY = mybir.ActivationFunctionType.Copy
 SIGMOID = mybir.ActivationFunctionType.Sigmoid
+ITEM_BYTES = {F32: 4, U32: 4, BF16: 2, U8: 1}
 
 P = 128
 PACK = 4
 STRIPE = 16
+ALIGN = 256
 ALL = slice(0, B * N)
 GROUP = [slice(b * N, (b + 1) * N) for b in range(B)]
-PIECES = [slice(0, 384), slice(384, 768), slice(768, 1024)]
-QUARTERS = [slice(k * 256, (k + 1) * 256) for k in range(4)]
 
 
 def tile_attend_gsig_mom_kernel(tc, xT, wT, y, wt, xm, mT, offs, out_0, out_1):
@@ -38,32 +39,37 @@ def tile_attend_gsig_mom_kernel(tc, xT, wT, y, wt, xm, mT, offs, out_0, out_1):
         return matrix.rearrange("(p j) c -> p j c", j=PACK)
 
     with ExitStack() as ctx:
+        lists = ctx.enter_context(tc.tile_pool(name="lists", bufs=1))
         sbuf = ctx.enter_context(tc.tile_pool(name="sbuf", bufs=1))
         psum = ctx.enter_context(tc.psum_pool(name="psum", bufs=1))
 
-        offsets = sbuf.tile([P, B * N // STRIPE], U16, name="offsets")
+        offsets = lists.tile([P, B * N // STRIPE], U16, name="offsets")
         nc.sync.dma_start(offsets[:], offs)
 
-        def new(name, shape, dtype, slot=None):
-            return sbuf.tile(shape, dtype, name=name, tag=slot or name, align_bytes=64)
+        place = {"end": 0}
+
+        def new(name, shape, dtype, over=None, at=0):
+            if over is None:
+                place[name] = place["end"]
+                size = math.prod(shape[1:]) * ITEM_BYTES[dtype]
+                place["end"] = place["end"] + -(-size // ALIGN) * ALIGN
+            else:
+                place[name] = place[over] + at
+            return sbuf.tile(shape, dtype, name=name, align_bytes=ALIGN, offset=place[name])
 
         def listed(window, entries):
             return window[:].indirect(offsets[:, entries.start // STRIPE : entries.stop // STRIPE])
 
-        def load(name, source, shape, slot=None):
-            dest = new(name, shape, F32, slot)
+        def load(name, source, shape, over=None):
+            dest = new(name, shape, F32, over)
             nc.sync.dma_start(dest[:], source)
             return dest
 
-        def load_plane(name, table, t, slot=None):
-            return load(name, planes(table)[t], [P, T], slot)
+        def load_plane(name, table, t, over=None):
+            return load(name, planes(table)[t], [P, T], over)
 
-        def load_rows(name, matrix, slot=None):
-            return load(name, rows4(matrix), [P, PACK, 512], slot)
-
-        warm = new("warm", [P, 8], F32)
-        nc.vector.memset(warm[:], 0.0)
-        nc.scalar.activation(warm[:], warm[:], SIGMOID)
+        def load_rows(name, matrix, over=None):
+            return load(name, rows4(matrix), [P, PACK, 512], over)
 
         def moving_views(dest, planar):
             return dest.rearrange("p (c i j) -> p c j i", i=4, j=PACK), planar.rearrange("p j (c i) -> p c j i", i=4)
@@ -74,167 +80,214 @@ def tile_attend_gsig_mom_kernel(tc, xT, wT, y, wt, xm, mT, offs, out_0, out_1):
                 raw.rearrange("p j (m t) -> p m j t", t=PACK),
             )
 
-        def on_scalar(views):
-            nc.scalar.activation(views[0], views[1], COPY)
-
-        def on_vector(views):
-            nc.vector.tensor_copy(views[0], views[1])
-
-        def rounded(name, engine, views, source, slot=None):
-            dest = new(name + "_rounded", [P, PACK * 512], BF16, slot)
-            engine(views(dest[:], source))
+        def round_shared(name, views, source, on_vector, over=None, at=0):
+            dest = new(name + "_rounded", [P, PACK * 512], BF16, over, at)
+            woven, planar = views(dest[:], source)
+            if on_vector > 0:
+                nc.vector.tensor_copy(woven[:, 0:on_vector], planar[:, 0:on_vector])
+            if on_vector < P:
+                nc.scalar.activation(woven[:, on_vector:P], planar[:, on_vector:P], COPY)
             return dest
 
-        def quantize(name, source, fmt, slot=None):
-            codes = new(name + "_codes", [P, 512], U32, slot)
-            scales = new(name + "_scales", [P, 512], U8)
-            nc.vector.quantize_mx(out=codes[:].bitcast(fmt), scales=scales[:], in_=source[:])
-            return codes, scales, fmt
+        def operand(name, fmt, over=None, at=0):
+            return new(name + "_codes", [P, 512], U32, over, at), new(name + "_scales", [P, 512], U8), fmt
 
-        def products(name, b, stationary, moving):
-            banks = []
-            for t in range(PACK):
+        def quantize_part(dest, source, columns):
+            codes, scales, fmt = dest
+            nc.vector.quantize_mx(
+                out=codes[:, columns].bitcast(fmt),
+                scales=scales[:, columns],
+                in_=source[:, PACK * columns.start : PACK * columns.stop],
+            )
+
+        def quantize(name, source, fmt, over=None, at=0):
+            dest = operand(name, fmt, over, at)
+            quantize_part(dest, source, slice(0, 512))
+            return dest
+
+        def new_banks(name, b):
+            return [psum.tile([P, N], F32, name="%s%d" % (name, t), tag="bank%d%d" % (b, t)) for t in range(PACK)]
+
+        def multiply(banks, stationary, moving, tiles, columns):
+            for t in tiles:
                 rows = slice(t * P, (t + 1) * P)
-                bank = psum.tile([P, N], F32, name="%s%d%d" % (name, b, t), tag="bank%d%d" % (b, t))
                 nc.tensor.matmul_mx(
-                    out=bank[:],
+                    out=banks[t][:, columns],
                     lhsT=stationary[0][:, rows].bitcast(stationary[2]),
                     lhsT_scale=stationary[1][:, rows],
-                    rhs=moving[0][:].bitcast(moving[2]),
-                    rhs_scale=moving[1][:],
+                    rhs=moving[0][:, columns].bitcast(moving[2]),
+                    rhs_scale=moving[1][:, columns],
                     start=True,
                     stop=True,
                 )
-                banks.append(bank)
+
+        def products(name, b, stationary, moving):
+            banks = new_banks(name, b)
+            multiply(banks, stationary, moving, range(PACK), slice(0, N))
             return banks
 
-        wt_in = new("wt_in", [P, B, PACK], F32)
-        nc.scalar.dma_start(wt_in[:], wt.rearrange("b (p j) c -> p b (j c)", j=PACK))
-        neg_wt = new("neg_wt", [P, B, PACK], F32)
-        nc.vector.tensor_scalar(neg_wt[:], wt_in[:], -1.0, None, MULT)
-        w_got = new("w_got", [P, PACK, B * N], F32)
-        w_in = [load_plane("w%d" % t, wT, t) for t in range(PACK)]
-        x0 = load_rows("x0", xT[0])
-        x1 = load_rows("x1", xT[1])
-        y0 = load_rows("y0", y[0])
-        xm0 = load_rows("xm0", xm[0])
-
-        def copy_w(t, slot=None):
-            dest = new("w_out%d" % t, [P, T], F32, slot)
-            nc.scalar.activation(dest[:], w_in[t][:], COPY)
-            return dest
-
-        last = PACK - 1
-        w_out = []
-        for t in range(last):
-            nc.vector.tensor_copy(w_got[:, t, :], listed(w_in[t], ALL))
-            w_out.append(copy_w(t))
-        nc.vector.tensor_copy(w_got[:, last, GROUP[0]], listed(w_in[last], GROUP[0]))
-        nc.scalar.activation(w_got[:, last, GROUP[1]], listed(w_in[last], GROUP[1]), COPY)
-
-        w_rounded = [rounded("w%d" % b, engine, moving_views, w_got[:, :, GROUP[b]]) for b, engine in enumerate((on_vector, on_scalar))]
-        x_rounded = rounded("x0", on_vector, stationary_views, x0[:])
-        w_q = quantize("w0", w_rounded[0], E4M3, "x0")
-        score = [products("score", 0, quantize("x0", x_rounded, E4M3), w_q)]
-        w_q = quantize("w1", w_rounded[1], E4M3, "x0_rounded")
-
-        m_in, m_out = {}, {}
-        m_in[0] = load_plane("m0", mT, 0)
-        y1 = load_rows("y1", y[1])
-        m_in[1] = load_plane("m1", mT, 1)
-        m_out[0] = load_plane("m_out0", mT, 0)
-        m_in[2] = load_plane("m2", mT, 2, "w0")
-        m_out[1] = load_plane("m_out1", mT, 1)
-        xm1 = load_rows("xm1", xm[1])
-        m_in[3] = load_plane("m3", mT, 3, "w1")
-        m_out[2] = load_plane("m_out2", mT, 2, "w2")
-        m_out[3] = load_plane("m_out3", mT, 3, "w3")
-        w_out.append(load_plane("w_out3", wT, 3))
-
-        def weights(b, y_b, slot):
-            dest = new("weight%d" % b, [P, PACK, N], F32, slot)
+        def probabilities(score, signs, margin, prob):
             for j in range(PACK):
-                nc.gpsimd.tensor_scalar(dest[:, j, :], y_b[:, j, :], neg_wt[:, b, j : j + 1], 0.0, MULT, ADD)
+                nc.vector.tensor_tensor(margin[:, j, :], score[j][:], signs[j], MULT)
+                nc.scalar.activation(prob[:, j, :], margin[:, j, :], SIGMOID, scale=-1.0)
+
+        def early_weights(b, signs, dest):
+            for j in range(PACK - 1):
+                nc.gpsimd.tensor_scalar(dest[:, j, :], signs[j], neg_wt[:, b, j : j + 1], 0.0, MULT, ADD)
             return dest
 
-        def gradient(b, prob, weight, slot):
-            dest = new("g%d_rounded" % b, [P, PACK * N], BF16, slot)
+        def last_weights(b, signs, dest):
+            nc.vector.tensor_scalar(dest[:, PACK - 1, :], signs[PACK - 1], neg_wt[:, b, PACK - 1 : PACK], None, MULT)
+
+        def gradient_part(dest, prob, weight, columns):
+            runs = slice(columns.start // 4, columns.stop // 4)
             woven, planar = moving_views(dest[:], prob[:])
-            nc.vector.tensor_tensor(woven, planar, moving_views(dest[:], weight[:])[1], MULT)
+            nc.vector.tensor_tensor(woven[:, runs], planar[:, runs], moving_views(dest[:], weight[:])[1][:, runs], MULT)
+
+        def gradient(b, prob, weight, over=None):
+            dest = new("g%d_rounded" % b, [P, PACK * N], BF16, over)
+            gradient_part(dest, prob, weight, slice(0, N))
             return dest
 
-        def drift(name, t, entries, slot=None):
-            dest = new(name, [P, entries.stop - entries.start], F32, slot)
-            nc.scalar.activation(dest[:], listed(m_in[t], entries), COPY, scale=-LR * BETA)
-            return dest
+        def fetch_w(on_vector, t, entries):
+            if on_vector:
+                nc.vector.tensor_copy(w_got[:, t, entries], listed(w_in[t], entries))
+            else:
+                nc.scalar.activation(w_got[:, t, entries], listed(w_in[t], entries), COPY)
+
+        def drift(dest, t, entries):
+            nc.scalar.activation(dest, listed(m_in[t], entries), COPY, scale=-LR * BETA)
 
         def finish(dest, bank, drifted):
-            nc.vector.scalar_tensor_tensor(dest, bank[:], -LR, drifted, MULT, ADD)
+            nc.vector.scalar_tensor_tensor(dest, bank, -LR, drifted, MULT, ADD)
 
         def put_w(t, entries, values):
             nc.vector.tensor_tensor(listed(w_out[t], entries), w_got[:, t, entries], values, ADD)
 
-        def put_m(t, pieces, values, start=0):
-            for piece in pieces:
-                nc.scalar.activation(listed(m_out[t], piece), values[:, piece.start - start : piece.stop - start], COPY, scale=-1.0 / LR)
+        def put_m(t, entries, values):
+            nc.scalar.activation(listed(m_out[t], entries), values, COPY, scale=undo_rate[:, 0:1])
 
-        def store(t):
-            nc.sync.dma_start(planes(out_0)[t], w_out[t][:])
-            (nc.scalar if t == last else nc.sync).dma_start(planes(out_1)[t], m_out[t][:])
+        warm = new("warm", [P, 8], F32)
+        nc.vector.memset(warm[:], 0.0)
+        nc.scalar.activation(warm[:], warm[:], SIGMOID)
 
-        x_rounded = rounded("x1", on_scalar, stationary_views, x1[:])
-        weight = weights(0, y0, None)
+        undo_rate = new("undo_rate", [P, 8], F32)
+        nc.vector.memset(undo_rate[:], -1.0 / LR)
+        wt_in = new("wt_in", [P, B, PACK], F32)
+        nc.scalar.dma_start(wt_in[:], wt.rearrange("b (p j) c -> p b (j c)", j=PACK))
+        neg_wt = new("neg_wt", [P, B, PACK], F32)
+        nc.vector.tensor_scalar(neg_wt[:], wt_in[:], -1.0, None, MULT)
+
+        last = PACK - 1
+        m_in, m_out, w_out = {}, {}, {}
+        w_in = [load_plane("w%d" % t, wT, t) for t in range(PACK)]
+        x0 = load_rows("x0", xT[0])
+        xm0 = load_rows("xm0", xm[0])
+        y0_low = load("y0_low", rows4(y[0])[:, 0:2, :], [P, 2, N])
+        y0_high = load("y0_high", rows4(y[0])[:, 2:4, :], [P, 2, N])
+        m_in[0] = load_plane("m0", mT, 0)
+        x1 = load_rows("x1", xT[1])
+        m_in[1] = load_plane("m1", mT, 1)
+        m_out[0] = load_plane("m_out0", mT, 0)
+        y1 = load_rows("y1", y[1])
+        xm1 = load_rows("xm1", xm[1])
+
+        first = slice(0, 256)
+        second = slice(256, N)
+        w_got = new("w_got", [P, PACK, B * N], F32)
+        for t in range(last):
+            split = 0 if t < 2 else 256
+            fetch_w(False, t, slice(split, B * N))
+            if split:
+                fetch_w(True, t, slice(0, split))
+            w_out[t] = new("w_out%d" % t, [P, T], F32)
+            nc.vector.tensor_copy(w_out[t][:], w_in[t][:])
+        fetch_w(True, last, first)
+        fetch_w(False, last, second)
+        fetch_w(False, last, GROUP[1])
+
+        m_in[3] = load_plane("m3", mT, 3, "w0")
+        m_out[1] = load_plane("m_out1", mT, 1)
+        m_in[2] = load_plane("m2", mT, 2, "w1")
+        m_out[3] = load_plane("m_out3", mT, 3, "w2")
+        m_out[2] = load_plane("m_out2", mT, 2, "w3")
+        w_out[3] = load_plane("w_out3", wT, 3)
+
+        w0_rounded = round_shared("w0", moving_views, w_got[:, :, GROUP[0]], P)
+        w_q = quantize("w0", w0_rounded, E4M3)
+        x_rounded = round_shared("x0", stationary_views, x0[:], 56)
+        x_q = operand("x0", E4M3)
+        score = new_banks("score0", 0)
+        quantize_part(x_q, x_rounded, slice(0, P))
+        multiply(score, x_q, w_q, range(1), slice(0, N))
+        quantize_part(x_q, x_rounded, slice(P, 512))
+        multiply(score, x_q, w_q, range(1, PACK), slice(0, N))
+        w1_rounded = round_shared("w1", moving_views, w_got[:, :, GROUP[1]], 0, "x0")
+
+        xm_rounded = round_shared("xm0", stationary_views, xm0[:], P)
+        signs = [y0_low[:, 0, :], y0_low[:, 1, :], y0_high[:, 0, :], y0_high[:, 1, :]]
+        weight = early_weights(0, signs, new("weight0", [P, PACK, N], F32))
+        margin = new("margin0", [P, PACK, N], F32)
         prob = new("prob0", [P, PACK, N], F32)
-        margin = new("margin", [P, N], F32)
-        for j in range(PACK):
-            source = margin[:] if j == 0 else prob[:, j, :]
-            nc.vector.tensor_tensor(source, score[0][j][:], y0[:, j, :], MULT)
-            nc.scalar.activation(prob[:, j, :], source, SIGMOID, scale=-1.0)
-        score.append(products("score", 1, quantize("x1", x_rounded, E4M3, "margin"), w_q))
+        probabilities(score, signs, margin, prob)
+        last_weights(0, signs, weight)
+        xm_q = quantize("xm0", xm_rounded, E4M3, "y0_high")
+        drift0 = new("drift0", [P, B * N], F32, "margin0")
+        drift(drift0[:], 0, ALL)
         g_rounded = gradient(0, prob, weight, "w0_rounded")
-        xm_rounded = new("xm0_rounded", [P, PACK * D], BF16)
-        dealt, raw = stationary_views(xm_rounded[:], xm0[:])
-        on_vector((dealt[:, 0:32], raw[:, 0:32]))
-        on_scalar((dealt[:, 32:P], raw[:, 32:P]))
-        g_q = quantize("g0", g_rounded, E5M2)
-        xm_q = quantize("xm0", xm_rounded, E4M3)
-        step0 = drift("step0", 0, ALL)
-        weight = weights(1, y1, "xm0_rounded")
-        prob = new("prob1", [P, PACK, N], F32, "x1")
-        for j in range(PACK):
-            nc.vector.tensor_tensor(prob[:, j, :], score[1][j][:], y1[:, j, :], MULT)
-            nc.scalar.activation(prob[:, j, :], prob[:, j, :], SIGMOID, scale=-1.0)
-        dw0 = products("dw0", 1, xm_q, g_q)
-        finish(step0[:, GROUP[0]], dw0[0], step0[:, GROUP[0]])
-        g_rounded = gradient(1, prob, weight, "w1_rounded")
-        step1 = drift("step1", 1, ALL)
-        put_w(0, GROUP[0], step0[:, GROUP[0]])
-        put_m(0, QUARTERS[:2], step0)
-        drift2 = drift("drift2", 2, ALL)
-        finish(step1[:, GROUP[0]], dw0[1], step1[:, GROUP[0]])
-        put_w(1, QUARTERS[0], step1[:, QUARTERS[0]])
-        put_m(1, QUARTERS[:2], step1)
-        drift30 = drift("drift30", 3, GROUP[0])
-        xm_rounded = rounded("xm1", on_vector, stationary_views, xm1[:])
-        g_q = quantize("g1", g_rounded, E5M2, "xm1")
-        dw1 = products("dw1", 0, quantize("xm1", xm_rounded, E4M3), g_q)
-        step2 = new("step2", [P, B * N], F32, "xm1_rounded")
-        step3 = new("step3", [P, B * N], F32, "xm1_codes")
-        finish(step2[:, GROUP[0]], dw0[2], drift2[:, GROUP[0]])
-        finish(step0[:, GROUP[1]], dw1[0], step0[:, GROUP[1]])
-        finish(step1[:, GROUP[1]], dw1[1], step1[:, GROUP[1]])
-        put_w(0, GROUP[1], step0[:, GROUP[1]])
-        put_m(0, QUARTERS[2:], step0)
-        store(0)
-        finish(step2[:, GROUP[1]], dw1[2], drift2[:, GROUP[1]])
+        dw0 = products("dw0", 0, xm_q, quantize("g0", g_rounded, E5M2))
+        w_q = quantize("w1", w1_rounded, E4M3, "prob0")
+        x_rounded = round_shared("x1", stationary_views, x1[:], 48, "x0_rounded")
+        finish(drift0[:, GROUP[0]], dw0[0][:], drift0[:, GROUP[0]])
+        score = products("score1", 1, quantize("x1", x_rounded, E4M3), w_q)
+        drift1 = new("drift1", [P, B * N], F32)
+        drift(drift1[:], 1, ALL)
+        early = slice(0, 448)
+        late = slice(448, B * N)
+        put_w(0, early, drift0[:, early])
+        put_m(0, early, drift0[:, early])
+
+        signs = [y1[:, j, :] for j in range(PACK)]
+        weight = early_weights(1, signs, new("weight1", [P, PACK, N], F32, "weight0"))
+        margin = new("margin1", [P, PACK, N], F32, "xm0")
+        prob = new("prob1", [P, PACK, N], F32, "prob0")
+        probabilities(score, signs, margin, prob)
+        last_weights(1, signs, weight)
+        step1 = new("step1", [P, B * N], F32, "y1")
+        finish(step1[:, second], dw0[1][:, second], drift1[:, second])
+        g_rounded = gradient(1, prob, weight, "g0_rounded")
+        xm_rounded = round_shared("xm1", stationary_views, xm1[:], 80, "margin1")
+        g_q = quantize("g1", g_rounded, E5M2)
+        dw1 = products("dw1", 1, quantize("xm1", xm_rounded, E4M3), g_q)
+        step1_first = new("step1_first", [P, first.stop], F32, "xm1_rounded")
+        finish(step1_first[:], dw0[1][:, first], drift1[:, first])
+        put_w(1, first, step1_first[:])
+
+        step3 = new("step3", [P, B * N], F32)
+        drift(step3[:], 3, ALL)
+        put_m(1, second, step1[:, second])
+        step2 = new("step2", [P, B * N], F32)
+        drift(step2[:], 2, ALL)
+        put_m(1, first, step1_first[:])
+        finish(drift0[:, GROUP[1]], dw1[0][:], drift0[:, GROUP[1]])
+        finish(step1[:, GROUP[1]], dw1[1][:], drift1[:, GROUP[1]])
+        put_w(0, late, drift0[:, late])
+        put_m(0, late, drift0[:, late])
+        nc.sync.dma_start(planes(out_0)[0], w_out[0][:])
+        nc.sync.dma_start(planes(out_1)[0], m_out[0][:])
+        for b, dw in enumerate((dw0, dw1)):
+            finish(step3[:, GROUP[b]], dw[3][:], step3[:, GROUP[b]])
+        put_m(1, GROUP[1], step1[:, GROUP[1]])
         put_w(1, slice(256, B * N), step1[:, 256 : B * N])
-        put_m(1, QUARTERS[2:], step1)
-        store(1)
-        drift31 = new("drift31", [P, N], F32)
-        nc.vector.tensor_scalar(drift31[:], listed(m_in[3], GROUP[1]), -LR * BETA, 0.0, MULT, ADD)
-        finish(step3[:, GROUP[0]], dw0[3], drift30[:])
-        finish(step3[:, GROUP[1]], dw1[3], drift31[:])
-        for t, step in ((2, step2), (3, step3)):
-            put_w(t, ALL, step[:])
-            put_m(t, PIECES, step)
-            store(t)
+        nc.sync.dma_start(planes(out_1)[1], m_out[1][:])
+        nc.sync.dma_start(planes(out_0)[1], w_out[1][:])
+        for b, dw in enumerate((dw0, dw1)):
+            finish(step2[:, GROUP[b]], dw[2][:], step2[:, GROUP[b]])
+        put_m(3, ALL, step3[:])
+        nc.sync.dma_start(planes(out_1)[3], m_out[3][:])
+        put_w(2, ALL, step2[:])
+        nc.sync.dma_start(planes(out_0)[2], w_out[2][:])
+        put_m(2, ALL, step2[:])
+        nc.scalar.dma_start(planes(out_1)[2], m_out[2][:])
+        put_w(3, ALL, step3[:])
+        nc.sync.dma_start(planes(out_0)[3], w_out[3][:])

@@ -254,21 +254,18 @@ def tile_attend_gsig_mom_kernel(tc, xT, wT, y, wt, xm, mT, offs, out_0, out_1):
         probabilities(score, signs, margin, prob)
         last_weights(1, signs, weight)
         step1 = new("step1", [P, B * N], F32, "y1")
-        finish(step1[:, second], dw0[1][:, second], drift1[:, second])
+        finish(step1[:, GROUP[0]], dw0[1][:], drift1[:, GROUP[0]])
         g_rounded = gradient(1, prob, weight, "g0_rounded")
         xm_rounded = round_shared("xm1", stationary_views, xm1[:], 80, "margin1")
         g_q = quantize("g1", g_rounded, E5M2)
         dw1 = products("dw1", 1, quantize("xm1", xm_rounded, E4M3), g_q)
-        step1_first = new("step1_first", [P, first.stop], F32, "xm1_rounded")
-        finish(step1_first[:], dw0[1][:, first], drift1[:, first])
-        put_w(1, first, step1_first[:])
+        put_w(1, slice(0, P), step1[:, 0:P])
 
         step3 = new("step3", [P, B * N], F32)
         drift(step3[:], 3, ALL)
-        put_m(1, second, step1[:, second])
+        put_m(1, GROUP[0], step1[:, GROUP[0]])
         step2 = new("step2", [P, B * N], F32)
         drift(step2[:], 2, ALL)
-        put_m(1, first, step1_first[:])
         finish(drift0[:, GROUP[1]], dw1[0][:], drift0[:, GROUP[1]])
         finish(step1[:, GROUP[1]], dw1[1][:], drift1[:, GROUP[1]])
         put_w(0, late, drift0[:, late])
@@ -278,7 +275,7 @@ def tile_attend_gsig_mom_kernel(tc, xT, wT, y, wt, xm, mT, offs, out_0, out_1):
         for b, dw in enumerate((dw0, dw1)):
             finish(step3[:, GROUP[b]], dw[3][:], step3[:, GROUP[b]])
         put_m(1, GROUP[1], step1[:, GROUP[1]])
-        put_w(1, slice(256, B * N), step1[:, 256 : B * N])
+        put_w(1, slice(P, B * N), step1[:, P : B * N])
         nc.sync.dma_start(planes(out_1)[1], m_out[1][:])
         nc.sync.dma_start(planes(out_0)[1], w_out[1][:])
         for b, dw in enumerate((dw0, dw1)):

@@ -165,13 +165,13 @@ def tile_attend_gsig_mom_kernel(tc, xT, wT, y, wt, xm, mT, offs, out_0, out_1):
             nc.vector.tensor_tensor(listed(w_out[t], entries), w_got[:, t, entries], values, ADD)
 
         def put_m(t, entries, values):
-            nc.scalar.activation(listed(m_out[t], entries), values, COPY, scale=undo_rate[:, 0:1])
+            nc.scalar.activation(listed(m_out[t], entries), values, COPY, scale=undo_rate[:])
 
         warm = new("warm", [P, 8], F32)
         nc.vector.memset(warm[:], 0.0)
         nc.scalar.activation(warm[:], warm[:], SIGMOID)
 
-        undo_rate = new("undo_rate", [P, 8], F32)
+        undo_rate = new("undo_rate", [P, 1], F32)
         nc.vector.memset(undo_rate[:], -1.0 / LR)
         wt_in = new("wt_in", [P, B, PACK], F32)
         nc.scalar.dma_start(wt_in[:], wt.rearrange("b (p j) c -> p b (j c)", j=PACK))
@@ -196,7 +196,7 @@ def tile_attend_gsig_mom_kernel(tc, xT, wT, y, wt, xm, mT, offs, out_0, out_1):
         second = slice(256, N)
         w_got = new("w_got", [P, PACK, B * N], F32)
         for t in range(last):
-            split = 0 if t < 2 else 256
+            split = 0 if t < 1 else 256
             fetch_w(False, t, slice(split, B * N))
             if split:
                 fetch_w(True, t, slice(0, split))

import math
from contextlib import ExitStack

import concourse.mybir as mybir

B, N, T, D, R = 2, 512, 2048, 512, 512
LR = 0.1
BETA = 0.9
FLOPS = 2 * 2 * B * N * D * R

F32 = mybir.dt.float32
BF16 = mybir.dt.bfloat16
U32 = mybir.dt.uint32
U16 = mybir.dt.uint16
U8 = mybir.dt.uint8
E4M3 = mybir.dt.float8_e4m3fn_x4
E5M2 = mybir.dt.float8_e5m2_x4
MULT = mybir.AluOpType.mult
ADD = mybir.AluOpType.add
COPY = mybir.ActivationFunctionType.Copy
SIGMOID = mybir.ActivationFunctionType.Sigmoid
ITEM_BYTES = {F32: 4, U32: 4, BF16: 2, U8: 1}

P = 128
PACK = 4
STRIPE = 16
ALIGN = 256
ALL = slice(0, B * N)
GROUP = [slice(b * N, (b + 1) * N) for b in range(B)]


def tile_attend_gsig_mom_kernel(tc, xT, wT, y, wt, xm, mT, offs, out_0, out_1):
    nc = tc.nc

    def planes(table):
        return table.rearrange("(p t) c -> t p c", t=PACK)

    def rows4(matrix):
        return matrix.rearrange("(p j) c -> p j c", j=PACK)

    with ExitStack() as ctx:
        lists = ctx.enter_context(tc.tile_pool(name="lists", bufs=1))
        sbuf = ctx.enter_context(tc.tile_pool(name="sbuf", bufs=1))
        psum = ctx.enter_context(tc.psum_pool(name="psum", bufs=1))

        offsets = lists.tile([P, B * N // STRIPE], U16, name="offsets")
        nc.sync.dma_start(offsets[:], offs)

        place = {"end": 0}

        def new(name, shape, dtype, over=None, at=0):
            if over is None:
                place[name] = place["end"]
                size = math.prod(shape[1:]) * ITEM_BYTES[dtype]
                place["end"] = place["end"] + -(-size // ALIGN) * ALIGN
            else:
                place[name] = place[over] + at
            return sbuf.tile(shape, dtype, name=name, align_bytes=ALIGN, offset=place[name])

        def listed(window, entries):
            return window[:].indirect(offsets[:, entries.start // STRIPE : entries.stop // STRIPE])

        def load(name, source, shape, over=None):
            dest = new(name, shape, F32, over)
            nc.sync.dma_start(dest[:], source)
            return dest

        def load_plane(name, table, t, over=None):
            return load(name, planes(table)[t], [P, T], over)

        def load_rows(name, matrix, over=None):
            return load(name, rows4(matrix), [P, PACK, 512], over)

        def moving_views(dest, planar):
            return dest.rearrange("p (c i j) -> p c j i", i=4, j=PACK), planar.rearrange("p j (c i) -> p c j i", i=4)

        def stationary_views(dest, raw):
            return (
                dest.rearrange("p (t m j) -> p m j t", t=PACK, j=PACK),
                raw.rearrange("p j (m t) -> p m j t", t=PACK),
            )

        def round_shared(name, views, source, on_vector, over=None, at=0):
            dest = new(name + "_rounded", [P, PACK * 512], BF16, over, at)
            woven, planar = views(dest[:], source)
            if on_vector > 0:
                nc.vector.tensor_copy(woven[:, 0:on_vector], planar[:, 0:on_vector])
            if on_vector < P:
                nc.scalar.activation(woven[:, on_vector:P], planar[:, on_vector:P], COPY)
            return dest

        def operand(name, fmt, over=None, at=0):
            return new(name + "_codes", [P, 512], U32, over, at), new(name + "_scales", [P, 512], U8), fmt

        def quantize_part(dest, source, columns):
            codes, scales, fmt = dest
            nc.vector.quantize_mx(
                out=codes[:, columns].bitcast(fmt),
                scales=scales[:, columns],
                in_=source[:, PACK * columns.start : PACK * columns.stop],
            )

        def quantize(name, source, fmt, over=None, at=0):
            dest = operand(name, fmt, over, at)
            quantize_part(dest, source, slice(0, 512))
            return dest

        def new_banks(name, b):
            return [psum.tile([P, N], F32, name="%s%d" % (name, t), tag="bank%d%d" % (b, t)) for t in range(PACK)]

        def multiply(banks, stationary, moving, tiles, columns):
            for t in tiles:
                rows = slice(t * P, (t + 1) * P)
                nc.tensor.matmul_mx(
                    out=banks[t][:, columns],
                    lhsT=stationary[0][:, rows].bitcast(stationary[2]),
                    lhsT_scale=stationary[1][:, rows],
                    rhs=moving[0][:, columns].bitcast(moving[2]),
                    rhs_scale=moving[1][:, columns],
                    start=True,
                    stop=True,
                )

        def products(name, b, stationary, moving):
            banks = new_banks(name, b)
            multiply(banks, stationary, moving, range(PACK), slice(0, N))
            return banks

        def probabilities(score, signs, margin, prob):
            for j in range(PACK):
                nc.vector.tensor_tensor(margin[:, j, :], score[j][:], signs[j], MULT)
                nc.scalar.activation(prob[:, j, :], margin[:, j, :], SIGMOID, scale=-1.0)

        def early_weights(b, signs, dest):
            for j in range(PACK - 1):
                nc.gpsimd.tensor_scalar(dest[:, j, :], signs[j], neg_wt[:, b, j : j + 1], 0.0, MULT, ADD)
            return dest

        def last_weights(b, signs, dest):
            nc.vector.tensor_scalar(dest[:, PACK - 1, :], signs[PACK - 1], neg_wt[:, b, PACK - 1 : PACK], None, MULT)

        def gradient_part(dest, prob, weight, columns):
            runs = slice(columns.start // 4, columns.stop // 4)
            woven, planar = moving_views(dest[:], prob[:])
            nc.vector.tensor_tensor(woven[:, runs], planar[:, runs], moving_views(dest[:], weight[:])[1][:, runs], MULT)

        def gradient(b, prob, weight, over=None):
            dest = new("g%d_rounded" % b, [P, PACK * N], BF16, over)
            gradient_part(dest, prob, weight, slice(0, N))
            return dest

        def fetch_w(on_vector, t, entries):
            if on_vector:
                nc.vector.tensor_copy(w_got[:, t, entries], listed(w_in[t], entries))
            else:
                nc.scalar.activation(w_got[:, t, entries], listed(w_in[t], entries), COPY)

        def drift(dest, t, entries):
            nc.scalar.activation(dest, listed(m_in[t], entries), COPY, scale=-LR * BETA)

        def finish(dest, bank, drifted):
            nc.vector.scalar_tensor_tensor(dest, bank, -LR, drifted, MULT, ADD)

        def put_w(t, entries, values):
            nc.vector.tensor_tensor(listed(w_out[t], entries), w_got[:, t, entries], values, ADD)

        def put_m(t, entries, values):
            nc.scalar.activation(listed(m_out[t], entries), values, COPY, scale=undo_rate[:])

        warm = new("warm", [P, 8], F32)
        nc.vector.memset(warm[:], 0.0)
        nc.scalar.activation(warm[:], warm[:], SIGMOID)

        undo_rate = new("undo_rate", [P, 1], F32)
        nc.vector.memset(undo_rate[:], -1.0 / LR)
        wt_in = new("wt_in", [P, B, PACK], F32)
        nc.scalar.dma_start(wt_in[:], wt.rearrange("b (p j) c -> p b (j c)", j=PACK))
        neg_wt = new("neg_wt", [P, B, PACK], F32)
        nc.vector.tensor_scalar(neg_wt[:], wt_in[:], -1.0, None, MULT)

        last = PACK - 1
        m_in, m_out, w_out = {}, {}, {}
        w_in = [load_plane("w%d" % t, wT, t) for t in range(PACK)]
        x0 = load_rows("x0", xT[0])
        xm0 = load_rows("xm0", xm[0])
        y0_low = load("y0_low", rows4(y[0])[:, 0:2, :], [P, 2, N])
        y0_high = load("y0_high", rows4(y[0])[:, 2:4, :], [P, 2, N])
        m_in[0] = load_plane("m0", mT, 0)
        x1 = load_rows("x1", xT[1])
        m_in[1] = load_plane("m1", mT, 1)
        m_out[0] = load_plane("m_out0", mT, 0)
        y1 = load_rows("y1", y[1])
        xm1 = load_rows("xm1", xm[1])

        first = slice(0, 256)
        second = slice(256, N)
        w_got = new("w_got", [P, PACK, B * N], F32)
        for t in range(last):
            split = 0 if t < 1 else 256
            fetch_w(False, t, slice(split, B * N))
            if split:
                fetch_w(True, t, slice(0, split))
            w_out[t] = new("w_out%d" % t, [P, T], F32)
            nc.vector.tensor_copy(w_out[t][:], w_in[t][:])
        fetch_w(True, last, first)
        fetch_w(False, last, second)
        fetch_w(False, last, GROUP[1])

        m_in[3] = load_plane("m3", mT, 3, "w0")
        m_out[1] = load_plane("m_out1", mT, 1)
        m_in[2] = load_plane("m2", mT, 2, "w1")
        m_out[3] = load_plane("m_out3", mT, 3, "w2")
        m_out[2] = load_plane("m_out2", mT, 2, "w3")
        w_out[3] = load_plane("w_out3", wT, 3)

        w0_rounded = round_shared("w0", moving_views, w_got[:, :, GROUP[0]], P)
        w_q = quantize("w0", w0_rounded, E4M3)
        x_rounded = round_shared("x0", stationary_views, x0[:], 56)
        x_q = operand("x0", E4M3)
        score = new_banks("score0", 0)
        quantize_part(x_q, x_rounded, slice(0, P))
        multiply(score, x_q, w_q, range(1), slice(0, N))
        quantize_part(x_q, x_rounded, slice(P, 512))
        multiply(score, x_q, w_q, range(1, PACK), slice(0, N))
        w1_rounded = round_shared("w1", moving_views, w_got[:, :, GROUP[1]], 0, "x0")

        xm_rounded = round_shared("xm0", stationary_views, xm0[:], P)
        signs = [y0_low[:, 0, :], y0_low[:, 1, :], y0_high[:, 0, :], y0_high[:, 1, :]]
        weight = early_weights(0, signs, new("weight0", [P, PACK, N], F32))
        margin = new("margin0", [P, PACK, N], F32)
        prob = new("prob0", [P, PACK, N], F32)
        probabilities(score, signs, margin, prob)
        last_weights(0, signs, weight)
        xm_q = quantize("xm0", xm_rounded, E4M3, "y0_high")
        drift0 = new("drift0", [P, B * N], F32, "margin0")
        drift(drift0[:], 0, ALL)
        g_rounded = gradient(0, prob, weight, "w0_rounded")
        dw0 = products("dw0", 0, xm_q, quantize("g0", g_rounded, E5M2))
        w_q = quantize("w1", w1_rounded, E4M3, "prob0")
        x_rounded = round_shared("x1", stationary_views, x1[:], 48, "x0_rounded")
        finish(drift0[:, GROUP[0]], dw0[0][:], drift0[:, GROUP[0]])
        score = products("score1", 1, quantize("x1", x_rounded, E4M3), w_q)
        drift1 = new("drift1", [P, B * N], F32)
        drift(drift1[:], 1, ALL)
        early = slice(0, 448)
        late = slice(448, B * N)
        put_w(0, early, drift0[:, early])
        put_m(0, early, drift0[:, early])

        signs = [y1[:, j, :] for j in range(PACK)]
        weight = early_weights(1, signs, new("weight1", [P, PACK, N], F32, "weight0"))
        margin = new("margin1", [P, PACK, N], F32, "xm0")
        prob = new("prob1", [P, PACK, N], F32, "prob0")
        probabilities(score, signs, margin, prob)
        last_weights(1, signs, weight)
        step1 = new("step1", [P, B * N], F32, "y1")
        finish(step1[:, GROUP[0]], dw0[1][:], drift1[:, GROUP[0]])
        g_rounded = gradient(1, prob, weight, "g0_rounded")
        xm_rounded = round_shared("xm1", stationary_views, xm1[:], 80, "margin1")
        g_q = quantize("g1", g_rounded, E5M2)
        dw1 = products("dw1", 1, quantize("xm1", xm_rounded, E4M3), g_q)
        put_w(1, slice(0, P), step1[:, 0:P])

        step3 = new("step3", [P, B * N], F32)
        drift(step3[:], 3, ALL)
        put_m(1, GROUP[0], step1[:, GROUP[0]])
        step2 = new("step2", [P, B * N], F32)
        drift(step2[:], 2, ALL)
        finish(drift0[:, GROUP[1]], dw1[0][:], drift0[:, GROUP[1]])
        finish(step1[:, GROUP[1]], dw1[1][:], drift1[:, GROUP[1]])
        put_w(0, late, drift0[:, late])
        put_m(0, late, drift0[:, late])
        nc.sync.dma_start(planes(out_0)[0], w_out[0][:])
        nc.sync.dma_start(planes(out_1)[0], m_out[0][:])
        for b, dw in enumerate((dw0, dw1)):
            finish(step3[:, GROUP[b]], dw[3][:], step3[:, GROUP[b]])
        put_m(1, GROUP[1], step1[:, GROUP[1]])
        put_w(1, slice(P, B * N), step1[:, P : B * N])
        nc.sync.dma_start(planes(out_1)[1], m_out[1][:])
        nc.sync.dma_start(planes(out_0)[1], w_out[1][:])
        for b, dw in enumerate((dw0, dw1)):
            finish(step2[:, GROUP[b]], dw[2][:], step2[:, GROUP[b]])
        put_m(3, ALL, step3[:])
        nc.sync.dma_start(planes(out_1)[3], m_out[3][:])
        put_w(2, ALL, step2[:])
        nc.sync.dma_start(planes(out_0)[2], w_out[2][:])
        put_m(2, ALL, step2[:])
        nc.scalar.dma_start(planes(out_1)[2], m_out[2][:])
        put_w(3, ALL, step3[:])
        nc.sync.dma_start(planes(out_0)[3], w_out[3][:])
